import numpy as np, ml_dtypes
CORES = [242,247,114,119]
N = 4
BF = ml_dtypes.bfloat16
def gentries(a):
    return np.ascontiguousarray(a.reshape(8, 16, -1).transpose(0, 2, 1)).reshape(8, -1)
def gtable(e):
    e = np.asarray(e); return np.ascontiguousarray(e.reshape(8, -1, 16).transpose(0, 2, 1)).reshape(128, -1).astype(np.int32)
L, V, W, RO, MP = 128, 1024, 2048, 4, 10
HN, HZ = [1, 2, 3, 1], [3, 1, 2, 2]
def parts(rng):
    return (rng.integers(0, 256, (N, 8, 16, W)), rng.integers(0, W, (N, 8, 16, V)), rng.integers(0, 256, (N, 8, 16, L)),
            rng.integers(0, V, (N, 8, L)), rng.integers(1, 4096, (N, 8, 16, 1)), rng.integers(0, 256, (N, 8, RO)))
def pack(x, b, z, v, w, t):
    return {"xt": np.ascontiguousarray(x.reshape(N, 128, W)).astype(np.float32).astype(BF), "bag": np.ascontiguousarray(b.reshape(N, 128, V)).astype(np.int32),
            "z0": np.ascontiguousarray(z.reshape(N, 128, L)).astype(np.float32).astype(BF), "v0": np.stack([gtable(a) for a in v]),
            "uw": np.ascontiguousarray(w.reshape(N, 128, 1)).astype(np.int32), "bt": np.ascontiguousarray(t).astype(np.int32)}
def setup_inputs(rng):
    return pack(*parts(rng))
def setup_inputs_spread(rng):
    x, b, z, v, w, t = parts(rng)
    x = np.minimum((np.exp2(8 * rng.random((N, 8, 1, W))) * rng.random(x.shape) * 1.2).astype(np.int64), 255)
    z = np.minimum((np.exp2(8 * rng.random((N, 8, 1, L))) * rng.random(z.shape) * 1.2).astype(np.int64), 255)
    p = rng.choice(np.array([1, 2, 3, 5]), (N, 8, 1, 1))
    b = np.minimum((W * rng.random(b.shape) ** p).astype(np.int64), W - 1); v = np.minimum((V * rng.random(v.shape) ** p[..., 0]).astype(np.int64), V - 1)
    w = np.minimum(np.maximum(np.exp2(12 * rng.random(w.shape)).astype(np.int64), 1), 4095); t = np.minimum(np.exp2(8 * rng.random(t.shape)).astype(np.int64) - 1, 255)
    return pack(x, b, z, v, w, t)
def twos(rng, n):
    a = rng.integers(0, 2, (N, 8, 16, n))
    return 255 * np.where(rng.random((N, 8, 1, n)) < 0.5, a[:, :, :1], a)
def setup_inputs_ends(rng):
    x, b, z, v, w, t = parts(rng)
    x = twos(rng, W); z = twos(rng, L); x[:, 1::2, :, 0] = 0; x[:, 1::2, :, W - 1] = 255
    eb = (W - 1) * rng.integers(0, 2, b.shape); ev = (V - 1) * rng.integers(0, 2, v.shape)
    kb = rng.random(b.shape) < 0.7; kv = rng.random(v.shape) < 0.7; kb[:, 3::4] = True; kv[:, 3::4] = True
    b = np.where(kb, eb, b); v = np.where(kv, ev, v)
    b[:, 7, :, V - 1] = W - 1; b[:, 7, 0, V - 1] = 0
    b[:, 7, :, 0] = W - 1; b[:, 7, 1::2, 0] = 0
    v[:, :, 0] = 0; v[:, :, L - 1] = V - 1; v[:, 7, 4] = V - 1; v[:, 7, 7] = 0
    z[:, 7, :, L - 1] = 255; z[:, 7, :, 4] = 255; z[:, 7, :, 7] = 0; z[:, 6, :, L - 1] = 255; z[:, 6, :, 2] = 0
    w = np.where(rng.random(w.shape) < 0.5, 1, 4095); w[:, 7] = 4095; w[:, 6] = 1
    t = 255 * rng.integers(0, 2, t.shape); t[:, 7, 0] = 255; t[:, 6, 0] = 0
    return pack(x, b, z, v, w, t)
def setup_inputs_corners(rng):
    x, b, z, v, w, t = parts(rng); lane = np.arange(L)
    for g in range(3):
        h = 5 * g + 1; x[:, g] = 0; x[:, g, h] = np.arange(W) & 255; z[:, g] = 0
        be = rng.integers(0, 61, N); be[0] = (0, 1, 60)[g]; be[N - 1] = (60, 0, 1)[g]; t[:, g, 0] = be
        v[:, g] = np.argsort(rng.random((N, V)), axis=1)[:, :L]
        for r in range(N):
            e = int(be[r]); m = rng.integers(100, 180, (L, 1)); c = np.array([0, max(e - 1, 0), e, e + 1])
            q = np.concatenate([m - rng.choice(c, (L, MP - 1)), m, m + rng.choice(c, (L, 15 - MP))], axis=1)
            q = np.concatenate([np.zeros((L, 1), np.int64), rng.permuted(q, axis=1)], axis=1)
            b[r, g, :, v[r, g]] = q + 256 * rng.integers(0, W // 256, (L, 16))
            z[r, g, h] = m[:, 0] + rng.choice(np.array([-e - 1, -e, -1, 0, e, e + 1]), L)
    v[:, 3] = lane; t[:, 3] = 255
    v[:, 4] = np.where(rng.random((N, L)) < 0.5, rng.choice(np.array([0, V - 1, V // 2 - 1, V // 2]), (N, L)), lane); t[:, 4] = 0
    v[:, 5] = (lane >> 1) + V // 2 * (lane & 1); b[:, 5, :, V // 2:] = b[:, 5, :, :V // 2]
    b[:, 6] = np.where(rng.random((N, 1, V)) < 0.5, b[:, 6, :1], b[:, 6])
    p0 = np.take_along_axis(b[:, 6, 0], v[:, 6], 1); z[:, 6, :, ::2] = np.take_along_axis(x[:, 6], p0[:, None, :], 2)[:, :, ::2]
    own = 16 * ((V - 1 - np.arange(V)) & (L - 1)) + rng.integers(0, 16, (N, 16, V))
    b[:, 7] = np.where(rng.random((N, 16, V)) < 0.7, own, rng.choice(np.array([0, W - 1]), (N, 16, V))); v[:, 7] = V - 1 - lane
    z[:, 7] = 255 * rng.integers(0, 2, (N, 1, L)); w[:, 7] = rng.choice(np.array([1, 4095]), (N, 16, 1))
    return pack(x, b, z, v, w, t)
def setup_inputs_crowd(rng):
    x, b, z, v, w, t = parts(rng); lane = np.arange(L)
    for g in range(8):
        p = int(rng.integers(1, V // 2 - 2)) if g != 7 else V - 1; c = int(rng.integers(0, W)); q = int(rng.integers(0, L - 1))
        x[:, g, :, c] = 0; b[:, g, 0, p] = c; v[:, g] = p
        small = rng.integers(0, 21, (N, 16, L))
        if g in (0, 1, 2, 7): z[:, g] = small
        if g in (3, 4): z[:, g] = 255 - small
        if g == 1: v[:, g, q] = p + 1
        if g == 2: v[:, g] = p + V // 2 * (lane & 1); b[:, g, :, p + V // 2] = b[:, g, :, p]
        if g == 4: z[:, g, :, q] = small[:, :, q]
        if g == 5: v[:, g] = rng.choice(np.array([p, 0, V - 1]), (N, L)); b[:, g] = rng.choice(np.array([0, c, W // 2, W // 2 + 5, W - 1]), (N, 16, V))
        if g == 7: v[:, g, L - 1] = 0
    return pack(x, b, z, v, w, t)
def check_inputs(d):
    bad = []
    for k, lo, hi in (("xt", 0, 255), ("bag", 0, W - 1), ("z0", 0, 255), ("v0", 0, V - 1), ("uw", 1, 4095), ("bt", 0, 255)):
        a = np.asarray(d[k]).astype(np.float64)
        if not np.all((a >= lo) & (a <= hi)): bad.append("range of " + k)
        elif not np.all(a == np.floor(a)): bad.append("whole numbers of " + k)
    return bad
def reference(xt, bag, z0, v0, uw, bt):
    X = xt.astype(np.float32).astype(np.int64).reshape(N, 8, 16, W); B = bag.astype(np.int64).reshape(N, 8, 16, V)
    z = z0.astype(np.float32).astype(np.int64).reshape(N, 8, 16, L); v = np.stack([gentries(a) for a in v0]).astype(np.int64)
    wt = uw.astype(np.int64).reshape(N, 8, 16, 1); bands = bt.astype(np.int64); A = np.zeros((N, 8, L), np.int64)
    lane = np.arange(L); k = np.arange(16).reshape(1, 1, 16, 1); ri = np.arange(N).reshape(N, 1, 1); gi = np.arange(8).reshape(1, 8, 1)
    u = np.add.reduce(wt * z, axis=2) & (W - 1)
    for t in range(RO):
        P = np.take_along_axis(B, v[:, :, None, :], 3)
        flat = np.ascontiguousarray(P.transpose(0, 1, 3, 2)).reshape(N, 8, 1, 16 * L)
        x = np.take_along_axis(X, flat, 3).reshape(N, 8, 16, L, 16)
        D = np.add.reduce(np.abs(x - x[..., :1]), axis=2)
        o = np.argsort(D, axis=3, kind="stable")
        m = np.take_along_axis(D, o[..., MP:MP + 1], 3)[..., 0]; e = o[..., 15][:, :, None, :]
        beta = bands[:, :, t][:, :, None] + 32 * A; q = np.add.reduce(np.abs(z - x[..., 0]), axis=2)
        far = q >= m; amb = np.abs(q - m) <= beta
        D = D.transpose(0, 1, 3, 2); m = m[:, :, None]; be = beta[:, :, None]
        M = np.where(np.abs(D - m) <= be, P, -1)
        sn = [(r - HN[t]) % N for r in range(N)]; sz = [(r - HZ[t]) % N for r in range(N)]
        M2 = M[sn]; z2 = z[sz]; a2 = amb[sz]
        side = np.where(far[:, :, None], D > m + be, D < m - be)
        F = np.where(side, P, np.where(M2 >= 0, M2, (P + (2 * k + 1) * u[:, :, None]) & (W - 1)))
        fe = np.take_along_axis(F, e, 2); F = np.where(k == e, F[:, :, :1], np.where(k == 0, fe, F))
        w = (2 * v + 1 + far) & (V - 1)
        top = np.full((N, 8, V), -1, np.int64); np.maximum.at(top, (ri, gi, w), np.broadcast_to(lane, w.shape))
        r_, g_, i_ = np.nonzero(np.take_along_axis(top, w, 2) == lane)
        B[r_, g_, :, w[r_, g_, i_]] = F[r_, g_, :, i_]
        c = np.broadcast_to((16 * lane + (u & 15))[:, :, None, :], z.shape)
        np.put_along_axis(X, c, (np.take_along_axis(X, c, 3) + z) & 255, 3)
        z = np.where(a2[:, :, None], (z + z2) >> 1, z); u = np.add.reduce(wt * z, axis=2) & (W - 1)
        v = np.where(a2, u & (V - 1), w); A = amb.astype(np.int64)
    return {"yx": X.reshape(N, 128, W).astype(np.float32).astype(BF), "yb": (B[..., :V // 2] + W * B[..., V // 2:]).reshape(N, 128, V // 2).astype(np.float32),
            "yz": z.reshape(N, 128, L).astype(np.float32).astype(BF), "yv": np.stack([gtable(a) for a in v]).astype(np.float32)}

@@ -1,0 +1,506 @@
+from concourse.bass import DstId, RemoteDMATransfer
+from concourse.mybir import AluOpType as A, ActivationFunctionType as F, AxisListType
+
+X1 = AxisListType.X
+NE = 3
+CV = 4
+
+RO, HN, HZ = 4, [1, 2, 3, 1], [3, 1, 2, 2]
+NV = 8
+NS = 15 - NV
+GVS = (32, 32)
+MAGIC = 12582912.0
+f32, bf, f16, i32, u16 = "float32", "bfloat16", "float16", "int32", "uint16"
+
+
+def _sb(n, d):
+    return ("sbuf", [128] + (n if isinstance(n, list) else [n]), d)
+
+
+SCRATCH = {
+    "X": _sb(2048, bf), "Bi": _sb(1024, i32), "B": _sb(1152, f32), "xg": _sb(2048, bf),
+    "Z": _sb([5, 16], i32), "VX": _sb([5, 16], u16), "vf": _sb(8, f32),
+    "uwi": _sb(4, i32), "bti": _sb(4, i32), "zb": _sb([5, 128], bf),
+    "Pu": _sb([4, 128], u16), "lP": _sb([4, 128], u16), "lZ": _sb([4, 128], bf), "lM": _sb([4, 128], bf),
+    "lA": _sb([4, 160], bf), "sM": _sb([4, 128], bf), "sA": _sb([4, 160], bf), "jr": _sb(24 * NV, bf), "one": _sb(128, bf),
+    "v2": _sb(8, i32), "h2": _sb(16, i32),
+    "mn": _sb([NV, 128], bf), "ad": _sb([NS, 128], bf), "aq": _sb(128, bf), "SB": _sb(960, f32),
+    "FL": _sb([2, 128], bf), "FQ": _sb([3, 128], bf), "PP": _sb(256, f16), "hy": _sb(128, f32), "nn": _sb(128, f32),
+    "w1": _sb(16, f32), "wM": _sb(128, f16), "bc": _sb(16, f32), "cnt": _sb(16, f32), "junk": _sb([16, 128], bf),
+    "wi": _sb(8, i32), "dw": _sb(16, f32), "ds": _sb(16, f32), "wu": _sb(8, u16),
+    "nc": _sb(144, bf), "nMa": _sb(128, bf), "xa": _sb(128, bf), "ns": _sb(128, f32),
+    "sg": _sb(128, f32), "av1": _sb(128, f32), "av": _sb(128, bf), "uM": _sb(128, f32), "ui": _sb(8, i32),
+    "u15": _sb(8, i32), "un": _sb(16, i32), "dv": _sb(32, f32), "vs": _sb(32, f32),
+    "xo": _sb(128, bf), "xs": _sb(128, bf), "xn": _sb(128, bf), "sbf": _sb(128, f16),
+    "tp": _sb(128, f16), "y1": _sb(128, f32), "y2": _sb(128, f32), "rr": _sb(128, f32), "zr": _sb(256, bf),
+    "yo": _sb(512, f32), "kd": _sb([8 - CV, 128], f32),
+    "pi": _sb(4, i32), "pc": _sb(4, i32), "pf": _sb(4, f32), "jb": _sb(128, bf), "gb": _sb(128, bf), "j24": _sb(24, bf),
+    "ci": _sb(8, f32), "tA": _sb(128, i32), "tB": _sb(128, i32), "tC": _sb(128, i32), "ok": _sb(128, bf),
+    "I": _sb(128, bf), "nI": _sb(128, bf), "I16": _sb(128, f16), "nI16": _sb(128, f16), "I32": _sb(128, f32),
+    "IX": _sb(128, bf), "Bo": _sb(128, bf), "RB": _sb(256, bf), "Bo8": _sb(128, bf), "nBo8": _sb(128, bf),
+    "BoK": _sb(128, f16), "nBo16": _sb(128, f16), "Bo16": _sb(128, f16), "Dg": _sb(128, bf), "M0": _sb(128, bf),
+    "M1": _sb(128, bf), "M2": _sb(128, bf), "CS": _sb(384, bf), "CQ": _sb(384, bf), "R0": _sb(24 * NV, bf),
+    "R16": _sb(24, bf), "R32": _sb(24, bf), "R1": _sb(160, bf), "nR1": _sb(160, bf), "sel32": _sb(8, f32),
+    "big": _sb(128, f32), "m256": _sb(128, bf), "mh": _sb(128, bf), "btf": _sb(4, f32), "btB": _sb([4, 128], bf),
+    "W2": _sb(128, f16), "Wu": _sb(128, f16), "uwx": _sb(4, i32), "uwf": _sb(4, f32),
+    "oc": _sb(8, u16), "l16": _sb(8, f32), "cl": _sb(16, bf), "cap": _sb(16, f32),
+    "p0": ("psum", [128, 512], f32), "p1": ("psum", [128, 512], f32), "p2": ("psum", [128, 512], f32),
+    "PK": ("psum", [128, 8, 128], f32), "p5": ("psum", [128, 512], f32), "p6": ("psum", [128, 512], f32),
+    "p7": ("psum", [128, 512], f32),
+}
+SEMAPHORES = (["cV", "cS", "cP", "cG", "sent", "dv", "du", "db", "dz", "dB", "dX", "o1", "o2", "o3", "o4", "o5"]
+              + ["a%s%d" % (k, t) for k in "PZMA" for t in range(RO)])
+
+
+def rank_program(g, core, T, topo):
+    rank = T.rank_of(core)
+    if rank is None:
+        return
+    N = len(T.cores)
+    Q = {"V": g.vector, "S": g.scalar, "P": g.tensor, "G": g, "Y": g.sync}
+    count = {}
+    know = {e: {} for e in Q}
+    after = {}
+    lastw, readers, bank = {}, {}, {}
+
+    def wait(e, tok):
+        s, v = tok
+        if know[e].get(s, 0) >= v:
+            return
+        Q[e].wait_ge(T.sem[s], v)
+        for s2, v2 in after[tok].items():
+            if know[e].get(s2, 0) < v2:
+                know[e][s2] = v2
+
+    def op(e, fn, r="", w="", b="", sem=None, inc=1):
+        r, w = r.split(), w.split()
+        deps = [lastw[k] for k in r + w if k in lastw]
+        for k in w:
+            deps += readers.get(k, [])
+        deps += [bank[k][1] for k in b if k in bank and bank[k][0] != e]
+        if e == "P":
+            deps = [d for d in deps if d[0] != "cP"]
+        best = {}
+        for s, v in deps:
+            best[s] = max(best.get(s, 0), v)
+        for s, v in sorted(best.items(), key=lambda x: -len(after[x])):
+            wait(e, (s, v))
+        ins = fn(Q[e])
+        if sem is False:
+            return
+        s = sem or "c" + e
+        count[s] = count.get(s, 0) + inc
+        tok = (s, count[s])
+        ins.then_inc(T.sem[s], inc)
+        after[tok] = dict(know[e])
+        after[tok][s] = count[s]
+        for k in r:
+            readers.setdefault(k, []).append(tok)
+        for k in w:
+            lastw[k] = tok
+            readers[k] = []
+        for k in b:
+            bank[k] = (e, tok)
+
+    def lands(key, s, n):
+        count[s] = n
+        after[(s, n)] = {s: n}
+        lastw[key] = (s, n)
+
+    def ts(out, in0, s1, s2, o0, o1=None, r="", w="", b=""):
+        if o1 is None:
+            op("V", lambda q: q.tensor_scalar(out, in0, s1, None, o0), r, w, b)
+        else:
+            op("V", lambda q: q.tensor_scalar(out, in0, s1, s2, o0, o1), r, w, b)
+
+    def tt(out, x, y, o, r="", w="", b=""):
+        op("V", lambda q: q.tensor_tensor(out, x, y, o), r, w, b)
+
+    def cp(out, x, r="", w="", b=""):
+        op("V", lambda q: q.tensor_copy(out, x), r, w, b)
+
+    def act(out, x, fn, r="", w="", b="", **kw):
+        op("S", lambda q: q.activation(out, x, fn, **kw), r, w, b)
+
+    def mm(out, l, rh, st, sp, r="", w="", b=""):
+        op("P", lambda q: q.matmul(out, l, rh, st, sp), r, w, b)
+
+    def ms(ap, val, w):
+        op("V", lambda q: q.memset(ap, val), "", w)
+
+    def dma(e, out, x, r, w, sem):
+        op(e, lambda q: q.dma_start(out, x), r, w, "", sem, 16)
+
+    def iota(out, pat, cm, w, whole=False):
+        if whole:
+            op("G", lambda q: q.iota(out, pat, 0, cm), "", w)
+        else:
+            op("G", lambda q: q.iota(out, pat, 0, cm, allow_small_or_imprecise_dtypes=True), "", w)
+
+    def bits(es):
+        return sum(1 << e for e in es)
+
+    def masks(src, da, dc):
+        ea, ec = topo.engines(src, da), topo.engines(src, dc)
+        if len(ea) > len(ec):
+            return [e for e in ea if e not in ec], ec, True
+        if len(ec) > len(ea):
+            return ea, [e for e in ec if e not in ea], True
+        return ea, ec, False
+
+    def early(src, da, dc):
+        ea, ec, apart = masks(src, da, dc)
+        return (ea, ec) if apart else (ea[:len(ea) // 2], ec[len(ec) // 2:])
+
+    def peers(r, t):
+        return T.cores[r % N], T.cores[(r + HN[t]) % N], T.cores[(r + HZ[t]) % N]
+
+    ms(T.bti[:], 0, "bti")
+    dma("Y", T.Z[:, 0, 0:8], T.v0[:], "", "v0", "dv")
+    dma("Y", T.uwi[:, 0:1], T.uw[:], "", "uwi", "du")
+    dma("S", T.zb[:, 0, :], T.z0[:], "", "z0", "dz")
+    dma("S", T.bti[0:128:16, :], T.bt[:], "", "bti", "db")
+    dma("Y", T.Bi[:], T.bag[:], "", "Bi", "dB")
+    dma("Y", T.X[:], T.xt[:], "", "X", "dX")
+
+    kb = T.CS[:, 0:128]
+    iota(T.pi[:, 0:1], [[0, 1]], 1, "pi", True)
+    iota(T.gb[:], [[1, 8], [0, 16]], 0, "gb")
+    iota(T.jb[:], [[1, 128]], 0, "jb")
+    iota(kb, [[0, 8], [1, 16]], 0, "kb")
+    iota(T.j24[:], [[0, 3], [1, 8]], 0, "j24")
+    iota(T.ci[:], [[16, 8]], 0, "ci")
+    iota(T.jr[:], [[0, 3], [1, 8], [0, NV]], 0, "jr")
+    ms(T.m256[:], -256.0, "m256")
+    ms(T.mh[:], -0.5, "mh")
+    ms(T.CS[:, 128:256], 16.0, "CS1")
+    ms(T.CS[:, 256:384], 0.0, "CS2")
+    ts(T.pc[:, 0:1], T.pi[:, 0:1], 4, None, A.arith_shift_right, r="pi", w="pc0")
+    ts(T.pc[:, 1:2], T.pi[:, 0:1], 15, None, A.bitwise_and, r="pi", w="pc1")
+    cp(T.pf[:, 2:3], T.pi[:, 0:1], "pi", "pf2")
+    for s, c in enumerate((-31.0, 1.0, -31.0)):
+        act(T.CQ[:, 128 * s:128 * s + 128], T.mh[:], F.Identity, "mh", "CQ%d" % s, scale=c)
+    cp(T.pf[:, 0:2], T.pc[:, 0:2], "pc0 pc1", "pf0")
+    pg, pk, pp = T.pf[:, 0:1], T.pf[:, 1:2], T.pf[:, 2:3]
+    ms(T.SB[:, 15:960:80], 0.0, " ".join("s%d%d" % (j, h) for j in range(6) for h in range(2)))
+    ms(T.nc[:, 0:16], 0.0, "nc")
+    ms(T.cap[:], -1.0, "cap")
+    ms(T.cl[:], 0.0, "cl")
+    ms(T.R1[:, 128:160], 0.0, "R1b")
+    ms(T.nR1[:, 128:160], 0.0, "nR1b")
+    ts(T.Bo[:], T.gb[:], pg, None, A.is_equal, r="gb pf0", w="Bo")
+    for name, c in (("BoK", 128.0), ("nBo16", -1.0), ("Bo16", 1.0)):
+        ts(T[name][:], T.gb[:], pg, c, A.is_equal, A.mult, "gb pf0", name)
+    ts(T.I[:], T.jb[:], pp, None, A.is_equal, r="jb pf2", w="I")
+    for name, c in (("I16", 1.0), ("nI16", -1.0)):
+        ts(T[name][:], T.jb[:], pp, c, A.is_equal, A.mult, "jb pf2", name)
+    ts(T.Dg[:], kb, pk, None, A.is_equal, r="kb pf0", w="Dg")
+    ts(T.ok[:], kb, 2.0, 1.0, A.mult, A.add, "kb", "ok")
+    ts(T.R16[:], T.j24[:], pg, 16.0, A.is_equal, A.mult, "j24 pf0", "R16")
+    ts(T.R32[:], T.j24[:], pg, -32.0, A.is_equal, A.mult, "j24 pf0", "R32")
+    ts(T.sel32[:], T.j24[:, 0:8], pg, None, A.is_equal, r="j24 pf0", w="sel32")
+    ts(T.R1[:, 129:160:2], T.j24[:, 0:16], pg, 0.5, A.is_equal, A.mult, "j24 pf0", "R1b")
+    ts(T.nR1[:, 129:160:2], T.j24[:, 0:16], pg, -0.5, A.is_equal, A.mult, "j24 pf0", "nR1b")
+    ts(T.oc[:], T.ci[:], 0.0625, None, A.mult, r="ci", w="oc")
+    ts(T.l16[:], T.ci[:], pk, 16.0, A.add, A.mult, "ci pf0", "l16")
+    act(T.M0[:], T.gb[:], F.Identity, "gb", "M0", scale=65536.0)
+    act(T.RB[:, 0:128], T.Bo[:], F.Identity, "Bo", "RB0", scale=16.0)
+    act(T.RB[:, 128:256], T.Bo[:], F.Identity, "Bo", "RB1", scale=-16.0)
+    act(T.nI[:], T.I[:], F.Identity, "I", "nI", scale=-1.0)
+    act(T.M1[:], T.Dg[:], F.Identity, "Dg", "M1", scale=-1048576.0, bias=1048576.0)
+    act(T.M2[:], T.Dg[:], F.Identity, "Dg", "M2", scale=16777216.0, bias=-16777216.0)
+    for name, src, c in (("Bo8", "Bo", 8.0), ("nBo8", "Bo", -8.0), ("I32", "I", 1.0), ("IX", "I", -128.0)):
+        act(T[name][:], T[src][:], F.Identity, src, name, scale=c)
+    act(T.R1[:, 0:128], T.I[:], F.Identity, "I", "R1a", scale=16.0)
+    act(T.nR1[:, 0:128], T.I[:], F.Identity, "I", "nR1a", scale=-16.0)
+    ts(T.cl[:, 8:16], T.l16[:], -1.0 / 2048, 127.0 / 128, A.mult, A.add, "l16", "cl")
+    ts(T.cl[:, 8 + CV:16], T.l16[:, CV:8], -1.0 / 4096, 127.0 / 256, A.mult, A.add, "l16", "cl")
+    ts(T.cnt[:, CV:8], T.l16[:, CV:8], -0.125, 254.0, A.mult, A.add, "l16", "cntc")
+    ts(T.cap[:, 1:16:2], T.l16[:], 1.0 / 16384, 1.0, A.mult, A.add, "l16", "cap")
+    cp(T.VX[:, 0, 0:8], T.Z[:, 0, 0:8], "v0", "vu0")
+    ts(T.uwx[:, 0:1], T.uwi[:, 0:1], 2047, None, A.bitwise_and, r="uwi", w="uwx0")
+    ts(T.R0[:], T.jr[:], pg, 16.0, A.is_equal, A.mult, "jr pf0", "R0")
+    cp(T.uwf[:, 0:1], T.uwx[:, 0:1], "uwx0", "uwf0")
+    ts(T.Wu[:], T.Bo[:], T.uwf[:, 0:1], None, A.mult, r="Bo uwf0", w="Wu")
+    ts(T.tC[:], T.ok[:], T.uwf[:, 0:1], None, A.mult, r="ok uwf0", w="tC")
+    act(T.one[:], T.mh[:], F.Identity, "mh", "one", scale=-2.0)
+
+    sent = [0]
+    PK = T.PK
+
+    def blk(a, b):
+        return PK[:, a, :] if b == a + 1 else PK[:, a:b, :]
+
+    def u_list(zz, kk):
+        o = T.p1[:, 256:384]
+        mm(o, T.I[:], T.M2[:], True, False, "I M2", "ub", "1")
+        mm(o, zz, T.Wu[:], False, True, kk + " Wu", "ub", "1")
+        act(T.uM[:], o, F.Relu, "ub", "uM", "1")
+        mm(T.p7[:, 144:152], T.uM[:], T.sel32[:], True, True, "uM sel32", "uL", "7")
+
+    def key_start(t):
+        mm(blk(1, 4), T.I[:], T.CS[:], True, False, "I kb CS1 CS2", "K", "3")
+        for s in range(1, 4):
+            mm(blk(s, s + 1), T.I[:], T.M0[:], False, False, "M0", "K", "3")
+        mm(blk(2, 4), T.btB[:, t, :], T.RB[:], False, False, "btB%d RB0 RB1" % t, "K", "3")
+        if t:
+            mm(blk(2, 4), T.sA[:, t - 1, 0:128], T.RB[:], False, False, "sA%d" % (t - 1), "K", "3")
+
+    def query_start(t):
+        mm(blk(4, 7), T.I[:], T.CQ[:], True, False, "CQ0 CQ1 CQ2", "KQ", "4")
+        for s in range(4, 7):
+            mm(blk(s, s + 1), T.I[:], T.M1[:], False, False, "M1", "KQ", "4")
+        mm(blk(4, 6), T.btB[:, t, :], T.RB[:], False, False, "btB%d RB0 RB1" % t, "KQ", "4")
+        if t:
+            mm(blk(4, 6), T.sA[:, t - 1, 0:128], T.RB[:], False, False, "sA%d" % (t - 1), "KQ", "4")
+
+    tt(T.M1[:], T.M1[:], T.M0[:], A.add, "M1 M0", "M1")
+    u_list(T.zb[:, 0, :], "z0")
+    ts(T.tA[:], T.tC[:], 2047, None, A.bitwise_and, r="tC", w="tA")
+    tt(T.W2[:], T.tA[:], T.Bo[:], A.mult, "tA Bo", "W2")
+    cp(T.ui[:], T.p7[:, 144:152], "uL", "ui", "7")
+    ts(T.u15[:], T.ui[:], 15, None, A.bitwise_and, r="ui", w="u15")
+    tt(T.Z[:, 0, 8:16], T.u15[:], T.l16[:], A.add, "u15 l16", "x0i")
+    cp(T.Pu[:, 0, :], T.Bi[:].indirect(T.VX[:, 0, 0:8]), "Bi vu0", "P0")
+    cp(T.VX[:, 0, 8:16], T.Z[:, 0, 8:16], "x0i", "xu0")
+    cp(T.btf[:], T.bti[:], "bti", "btf")
+    cp(T.B[:, 0:1024], T.Bi[:], "Bi", "B")
+    for t in range(RO):
+        act(T.btB[:, t, :], T.one[:], F.Identity, "one btf", "btB%d" % t, scale=T.btf[:, t:t + 1])
+    query_start(0)
+
+    for t in range(RO):
+        last = t == RO - 1
+        z, zk, Pk = T.zb[:, t, :], "z%d" % t, "P%d" % t
+        xu, xuk = T.VX[:, t, 8:16], "xu%d" % t
+        _, da, dc = peers(rank, t)
+        ida, idc = topo.addr(da, core), topo.addr(dc, core)
+        sa, sc = peers(rank - HN[t], t), peers(rank - HZ[t], t)
+        lands("lP%d" % t, "aP%d" % t, len(early(*sa)[0]))
+        lands("lZ%d" % t, "aZ%d" % t, len(early(*sc)[1]))
+        lands("lM%d" % t, "aM%d" % t, len(masks(*sa)[0]))
+        lands("lA%d" % t, "aA%d" % t, len(masks(*sc)[1]))
+        ea, ec = early(core, da, dc)
+        trs = [RemoteDMATransfer(dst_ids=[DstId(rid=ida[0], pnc=ida[1])], dma_engine_mask=bits(ea), remote_sem=T.sem["aP%d" % t],
+                                 src=T.Pu[:, t, :], dst=T.lP[:, t, :]),
+               RemoteDMATransfer(dst_ids=[DstId(rid=idc[0], pnc=idc[1])], dma_engine_mask=bits(ec), remote_sem=T.sem["aZ%d" % t],
+                                 src=z, dst=T.lZ[:, t, :])]
+        op("G", lambda q: q.remote_dma_fused(trs, local_sem=T.sem.sent), Pk + " " + zk, sem=False)
+        sent[0] += len(ea) + len(ec)
+
+
+        for h, GV in enumerate(GVS):
+            c = 64 * h
+            cp(T.xg[:, 16 * c:16 * (c + GV)], T.X[:].indirect(T.Pu[:, t, c:c + GV]), "X " + Pk, "xg%da" % h)
+            act(T.xg[:, 16 * (c + GV):16 * c + 1024], T.X[:].indirect(T.Pu[:, t, c + GV:c + 64]), F.Copy, "X " + Pk, "xg%db" % h)
+            xk = "xg%da xg%db" % (h, h)
+            pd, bd = (T.p1, "1") if h == 0 else (T.p2, "2")
+            if h == 0:
+                key_start(t)
+                o = T.p6[:, 256:384]
+                mm(T.p7[:, 0:128], T.I[:], z, True, False, zk, "dq", "7")
+                mm(o, T.nI[:], T.mh[:], True, False, "nI mh", "Hr", "6")
+                mm(o, T.nBo8[:], T.m256[:], False, False, "nBo8 m256", "Hr", "6")
+                mm(o, T.W2[:], z, False, False, "W2 " + zk, "Hr", "6")
+            mm(T.p0[:, c:c + 64], T.I[:], T.xg[:, 16 * c:16 * c + 1024:16], True, True, xk, "x0", "0")
+            for j in range(NS):
+                k = 2 * j + 2
+                mm(pd[:, 64 * j:64 * j + 64], T.I[:], T.xg[:, 16 * c + k:16 * c + 1024:16], True, False, xk, "pd%d" % h, bd)
+                mm(pd[:, 64 * j:64 * j + 64], T.nI[:], T.xg[:, 16 * c:16 * c + 1024:16], False, True, "nI", "pd%d" % h, bd)
+            if h == 0:
+                mm(T.p7[:, 0:64], T.nI[:], T.xg[:, 0:1024:16], False, False, xk, "dq", "7")
+        xk = "xg0a xg0b xg1a xg1b"
+        cp(T.PP[:, 0:128], T.Pu[:, t, :], Pk, "PP0")
+        if t:
+            cp(T.Z[:, t, :], T.vs[:, 1:32:2], "vs", "v%d x%di" % (t, t))
+        act(T.ad[:, :, 0:64], T.p1[:, 0:64 * NS], F.Abs, "pd0", "ad0", "1")
+        act(T.ad[:, :, 64:128], T.p2[:, 0:64 * NS], F.Abs, "pd1", "ad1", "2")
+        for k in range(1, NV + 1):
+            tt(T.mn[:, k - 1, :], T.xg[:, 2 * k - 1:2048:16], T.p0[:, 0:128], A.min, xk + " x0", "mn%d" % k, "0")
+        mm(PK[:, 1:4, 1:128:2], T.xg[:, 0:2048:16], T.R0[:], False, False, xk + " R0", "K", "3")
+        for k in range(1, NV + 1):
+            mm(PK[:, 1:4, 2 * k - 1:128:16], T.xg[:, 2 * k - 1:2048:16], T.R16[:], False, False, "R16", "K", "3")
+        for k in range(1, NV):
+            mm(PK[:, 1:4, 2 * k - 1:128:16], T.mn[:, k - 1, :], T.R32[:], False, False, "mn%d R32" % k, "K", "3")
+        for j in range(NS):
+            mm(PK[:, 1:4, 2 * j + 2:128:16], T.ad[:, j, :], T.R16[:], False, False, "ad0 ad1", "K", "3")
+        mm(PK[:, 1:4, 15:128:16], T.mn[:, NV - 1, :], T.R32[:], False, True, "mn%d" % NV, "K", "3")
+        ts(T.v2[:], T.Z[:, t, 0:8], 2.0, None, A.mult, r="v%d" % t, w="v2")
+        ts(T.h2[:, 0:8], T.v2[:], 1023, None, A.bitwise_and, r="v2", w="h2a")
+        ts(T.h2[:, 8:16], T.v2[:], 1023, None, A.bitwise_and, r="v2", w="h2b")
+
+        def item_sum():
+            act(T.xo[:], T.X[:].indirect(xu), F.Copy, "X " + xuk, "xo")
+            mm(T.p1[:, 0:128], T.I[:], z, True, False, zk, "xq", "1")
+            mm(T.p1[:, 0:128], T.I[:], T.xo[:], False, True, "xo", "xq", "1")
+
+        def item_wrap():
+            act(T.xs[:], T.p1[:, 0:128], F.Sign, "xq", "xs", "1", bias=-255.5)
+            mm(T.p1[:, 0:128], T.I[:], z, True, False, zk, "xq", "1")
+            mm(T.p1[:, 0:128], T.I[:], T.xo[:], False, False, "xo", "xq", "1")
+            mm(T.p1[:, 0:128], T.IX[:], T.xs[:], False, True, "IX xs", "xq", "1")
+
+        mm(T.p7[:, 64:128], T.nI[:], T.xg[:, 1024:2048:16], False, True, xk, "dq", "7")
+        mm(T.p6[:, 256:384], T.I16[:], T.PP[:, 0:128], False, True, "I16 PP0", "Hr", "6")
+        item_sum()
+        act(T.aq[:], T.p7[:, 0:128], F.Abs, "dq", "aq", "7")
+        for s in range(4, 7):
+            mm(blk(s, s + 1), T.aq[:], T.RB[:, 0:128], False, s == 6, "aq", "KQ", "4")
+        item_wrap()
+        act(T.hy[:], T.p6[:, 256:384], F.Identity, "Hr", "hy", "6", bias=8388607.5, scale=1.0 / 2048)
+        E1, E2 = T.p2[:, 128:256], T.p2[:, 256:384]
+        mm(E1, T.W2[:], z, True, False, "", "E1", "2")
+        mm(E2, T.W2[:], z, False, False, "", "E2", "2")
+        mm(E2, T.I16[:], T.PP[:, 0:128], False, False, "", "E2", "2")
+
+        for j in range(6):
+            for h in range(2):
+                c = 160 * j + 80 * h + 16
+                d1 = T.m256[:, 0:64] if j == 0 else T.SB[:, c - 161:c - 97]
+                op("V", lambda q: q.tensor_tensor_scan(T.SB[:, c:c + 64], PK[:, 1, 64 * h:64 * h + 64], d1, 0.0, A.max,
+                                                       A.min if j else A.max),
+                   "K " + ("m256" if j == 0 else "s%d%d" % (j - 1, h)), "s%d%d" % (j, h), "3")
+
+        def before_e(gs):
+            for gi in gs:
+                c = 16 + 16 * gi + 16 * (gi // 4)
+                act(T.nc[:, 16 + 16 * gi:32 + 16 * gi], T.SB[:, c:c + 16], F.Sign, "s0%d nc" % (gi // 4), "nc%d" % gi,
+                    scale=-1.0, bias=T.SB[:, c + 15:c + 16])
+
+        act(T.nn[:], T.hy[:], F.Identity, "hy", "nn", bias=2048.0 * 8388624, scale=-2048.0)
+        act(T.xn[:], T.p1[:, 0:128], F.Identity, "xq", "xn", "1", bias=-128.0)
+        mm(E1, T.I32[:], T.nn[:], False, False, "I32 nn", "E1", "2")
+        for gi in range(8):
+            c = 816 + 16 * gi + 16 * (gi // 4) + 15
+            ts(T.FL[:, :, 16 * gi:16 * gi + 16], PK[:, 2:4, 16 * gi:16 * gi + 16], T.SB[:, c:c + 1], None, A.is_le,
+               r="K s5%d" % (gi // 4), w="F%d" % gi, b="3")
+            act(T.FQ[:, :, 16 * gi:16 * gi + 16], PK[:, 4:7, 16 * gi:16 * gi + 16], F.Sign, "KQ s5%d" % (gi // 4), "G%d" % gi, "4",
+                scale=-1.0, bias=T.SB[:, c:c + 1])
+        fl = " ".join("F%d" % gi for gi in range(8))
+        fq = " ".join("G%d" % gi for gi in range(8))
+        nk = " ".join("nc%d" % gi for gi in range(8))
+        mm(T.p5[:, 0:128], T.FL[:, 1, :], T.I[:], True, False, fl, "mid", "5")
+        mm(T.p5[:, 0:128], T.FL[:, 0, :], T.nI[:], False, True, "", "mid", "5")
+        mm(T.p7[:, 128:144], T.I[:], T.cl[:], True, False, "cl", "nL", "7")
+        mm(T.p7[:, 128:144], T.FQ[:, 2, :], T.R1[:, 129:160:2], False, True, fq + " R1b", "nL", "7")
+        mm(T.p6[:, 0:160], T.FQ[:, 1, :], T.R1[:], True, False, "R1a R1b", "amb", "6")
+        mm(T.p6[:, 0:160], T.FQ[:, 0, :], T.nR1[:], False, True, "nR1a nR1b", "amb", "6")
+        mm(T.p0[:, 128:256], T.FQ[:, 2, :], T.I[:], True, True, "", "nT", "0")
+        before_e(range(NE))
+        mm(T.p1[:, 128:256], T.I[:], z, True, False, zk, "zs", "1")
+        mm(T.p1[:, 128:256], T.I[:], T.mh[:], False, False, "mh", "zs", "1")
+        mm(T.p1[:, 128:256], T.I[:], T.lZ[:, t, :], False, True, "lZ%d" % t, "zs", "1")
+        mm(E2, T.I32[:], T.nn[:], False, False, "", "E2", "2")
+        cp(T.X[:].indirect(xu), T.xn[:], xuk + " xn", "X")
+        act(T.sM[:, t, :], T.p5[:, 0:128], F.Copy, "mid", "sM%d" % t, "5")
+        act(T.sA[:, t, :], T.p6[:, 0:160], F.Copy, "amb", "sA%d" % t, "6")
+        ea, ec, _ = masks(core, da, dc)
+        op("G", lambda q: q.remote_dma(T.lM[:, t, :], T.sM[:, t, :], T.sem["aM%d" % t], T.sem.sent, ida[1], ida[0], bits(ea)),
+           "sM%d" % t, sem=False)
+        op("G", lambda q: q.remote_dma(T.lA[:, t, :], T.sA[:, t, :], T.sem["aA%d" % t], T.sem.sent, idc[1], idc[0], bits(ec)),
+           "sA%d" % t, sem=False)
+        sent[0] += len(ea) + len(ec)
+
+        tt(T.w1[:], T.h2[:], T.p7[:, 128:144], A.subtract, "h2a h2b nL", "w1", "7")
+        act(T.nMa[:], T.p0[:, 128:256], F.Copy, "nT", "nMa", "0")
+        cp(T.PP[:, 128:256], T.lP[:, t, :], "lP%d" % t, "PP1")
+        tt(T.wM[:], T.w1[:, 0:8].indirect(T.oc[:]), T.Dg[:], A.mult, "w1 oc Dg", "wM")
+        ts(T.bc[:], T.w1[:], -128.0, -127.5, A.mult, A.add, "w1", "bc")
+        ts(T.wi[:], T.w1[:, 0:8], -6.0, None, A.add, r="w1", w="wi")
+        mm(blk(7, 8), T.I[:], T.jb[:], True, False, "jb", "Kv", "4")
+        mm(blk(7, 8), T.BoK[:], T.wM[:], False, True, "BoK wM", "Kv", "4")
+        mm(T.p5[:, 128:256], T.FL[:, 0, :], T.I[:], True, False, fl, "Xs", "5")
+        mm(T.p5[:, 128:256], T.FL[:, 1, :], T.I[:], False, False, fl, "Xs", "5")
+        mm(T.p5[:, 128:256], T.Bo[:], T.nMa[:], False, True, "Bo nMa", "Xs", "5")
+        mm(E2, T.nI16[:], T.PP[:, 128:256], False, True, "nI16 PP1", "E2", "2")
+        mm(T.p6[:, 384:512], T.I[:], T.jb[:], True, False, "jb", "Kb", "6")
+        mm(T.p6[:, 384:512], T.BoK[:], T.wM[:], False, True, "BoK wM", "Kb", "6")
+        before_e(range(NE, 8))
+        act(T.av1[:], T.p1[:, 128:256], F.Identity, "zs", "av1", "1", bias=MAGIC, scale=0.5)
+        act(T.xa[:], T.p5[:, 128:256], F.Abs, "Xs", "xa", "5", bias=14.0)
+        act(T.av[:], T.av1[:], F.Identity, "av1", "av", bias=-MAGIC)
+        mm(T.p0[:, 0:128], T.nc[:, 16:144], T.I[:], True, False, nk, "sT", "0")
+        mm(T.p0[:, 0:128], T.nc[:, 15:143], T.nI[:], False, True, "", "sT", "0")
+        act(T.ns[:], T.xa[:], F.Sign, "xa", "ns", scale=-1.0, bias=2.0)
+        act(T.sg[:], T.p0[:, 0:128], F.Copy, "sT", "sg", "0")
+        u_list(T.av[:], "av")
+        ts(T.Z[:, t, 0:8], T.wi[:], 1023, None, A.bitwise_and, r="wi", w="v%d" % t)
+        for c in range(CV, 8):
+            ts(T.kd[:, c - CV, 16 * c:128], PK[:, 7, 16 * c:128], T.bc[:, 8 + c:9 + c], 4.0, A.add, A.mult,
+               "Kv bc", "kd%d" % c, "4")
+        ts(T.dw[:, 1:16:2], T.Z[:, t, 0:8], 1.0 / 1024, None, A.mult, r="v%d" % t, w="dw1")
+        for c in range(CV, 8):
+            op("V", lambda q: q.tensor_reduce(T.cnt[:, 8 + c:9 + c], T.kd[:, c - CV, 16 * c:128], X1, A.min,
+                                              apply_absolute_value=True), "kd%d" % c, "cnt%d" % (8 + c))
+        tt(E1, E1, T.ns[:], A.mult, "E1 E2 ns", "E1", "2")
+        tt(E2, E2, T.ns[:], A.mult, "E2 ns", "E2", "2")
+        tt(E1, E1, T.PP[:, 0:128], A.add, "E1 PP0", "E1", "2")
+        tt(T.p0[:, 256:384], E2, T.sg[:], A.mult, "E2 sg", "sd", "20")
+        tt(T.sbf[:], E1, T.sg[:], A.mult, "E1 sg", "sbf", "2")
+        for c in range(CV):
+            for j in range(2):
+                n = 8 * j + c
+                act(T.junk[:, n, 16 * c:128], T.p6[:, 384 + 16 * c:512], F.Sign, "Kb bc", "cnt%d" % n, "6",
+                    bias=T.bc[:, n:n + 1], accum_out=T.cnt[:, n:n + 1])
+        cp(T.ui[:], T.p7[:, 144:152], "uL", "ui", "7")
+        tt(T.dw[:, 2 * CV:16:2], T.cnt[:, CV:8], T.cnt[:, 8 + CV:16], A.subtract,
+           "cntc " + " ".join("cnt%d" % n for n in range(8 + CV, 16)), "dw2")
+        ts(T.u15[:], T.ui[:], 15, None, A.bitwise_and, r="ui", w="u15")
+        ts(T.un[:, 0:8], T.ui[:], 1023, None, A.bitwise_and, r="ui", w="un0")
+        tt(T.un[:, 8:16], T.u15[:], T.l16[:], A.add, "u15 l16", "un1")
+        cp(T.dv[:, 1:32:2], T.Z[:, t, :], "v%d x%di" % (t, t), "dv1")
+        ck = " ".join("cnt%d" % n for n in range(16))
+        tt(T.dw[:, 0:2 * CV:2], T.cnt[:, 8:8 + CV], T.cnt[:, 0:CV], A.subtract, ck, "dw0")
+        tt(T.dv[:, 0:32:2], T.un[:], T.Z[:, t, :], A.subtract, "un0 un1 v%d x%di" % (t, t), "dv")
+        op("V", lambda q: q.tensor_tensor_scan(T.ds[:], T.cap[:], T.dw[:], 0.0, A.min, A.max), "cap dw0 dw1 dw2", "ds")
+        if last:
+            lands("allsent", "sent", sent[0])
+            dma("Y", T.yx[:], T.X[:], "X allsent", "", "o1")
+        else:
+            query_start(t + 1)
+        mm(T.p5[:, 0:128], T.nBo16[:], T.sbf[:], True, False, "nBo16 sbf", "S", "5")
+        mm(T.p7[:, 256:384], T.I[:], z, True, False, zk, "zq", "7")
+        mm(T.p7[:, 384:512], T.I[:], T.av[:], False, False, "av", "zq", "7")
+        mm(T.p7[:, 384:512], T.I[:], T.m256[:], False, False, "m256", "zq", "7")
+
+        lm, la = "lM%d" % t, "lA%d" % t
+        tt(T.tp[:], T.lM[:, t, :], T.p0[:, 256:384], A.mult, lm + " sd", "tp", "0")
+        mm(T.p5[:, 0:128], T.Bo16[:], T.tp[:], False, True, "Bo16 tp", "S", "5")
+        tt(T.y1[:], T.lM[:, t, :], E2, A.mult, lm + " E2", "y1", "2")
+        ts(T.wu[:], T.ds[:, 1:16:2], 1024.0, None, A.mult, r="ds", w="wu")
+        tt(T.y2[:], E1, T.y1[:], A.subtract, "y1 E1", "y2", "2")
+        tt(T.rr[:], T.p5[:, 0:128], T.sg[:], A.mult, "S sg", "rr", "5")
+        mm(T.p7[:, 256:384], T.nBo8[:], T.lA[:, t, 0:128], False, False, "nBo8 " + la, "zq", "7")
+        mm(T.p7[:, 384:512], T.Bo8[:], T.lA[:, t, 0:128], False, True, "Bo8", "zq", "7")
+        act(T.zr[:], T.p7[:, 256:512], F.Relu, "zq", "zr", "7")
+        mm(T.p6[:, 0:128], T.I[:], T.zr[:, 0:128], True, False, "zr", "zn", "6")
+        mm(T.p6[:, 0:128], T.I[:], T.zr[:, 128:256], False, True, "zr", "zn", "6")
+        if not last:
+            act(T.zb[:, t + 1, :], T.p6[:, 0:128], F.Copy, "zn", "z%d" % (t + 1), "6")
+
+        def pick():
+            op("V", lambda q: q.tensor_tensor_scan(T.vs[:], T.lA[:, t, 128:160], T.dv[:], 0.0, A.mult, A.add),
+               la + " dv dv1", "vs")
+
+        late = not masks(*sc)[2]
+        if not last and not late:
+            pick()
+        tt(T.B[:].indirect(T.wu[:]), T.y2[:], T.rr[:], A.add, "wu y2 rr", "B")
+        if not last:
+            if late:
+                pick()
+            cp(T.VX[:, t + 1, :], T.vs[:, 1:32:2], "vs", "vu%d xu%d" % (t + 1, t + 1))
+            cp(T.Pu[:, t + 1, :], T.B[:, 0:1024].indirect(T.VX[:, t + 1, 0:8]), "B vu%d" % (t + 1), "P%d" % (t + 1))
+    pick()
+    cp(T.vf[:], T.vs[:, 1:16:2], "vs", "vf")
+    dma("Y", T.yv[:], T.vf[:], "vf", "", "o5")
+    for h, (pb, bk) in enumerate(((T.p1, "1"), (T.p2, "2"), (T.p5, "5"), (T.p0, "0"))):
+        c = 128 * h
+        act(pb[:, 0:128], T.B[:, 512 + c:640 + c], F.Identity, "B", "hi%d" % h, bk, scale=2048.0)
+        tt(T.yo[:, c:c + 128], T.B[:, c:c + 128], pb[:, 0:128], A.add, "B hi%d" % h, "yo%d" % h, bk)
+    dma("Y", T.yb[:, 0:256], T.yo[:, 0:256], "yo0 yo1", "", "o3")
+    act(T.zb[:, RO, :], T.p6[:, 0:128], F.Copy, "zn", "z%d" % RO, "6")
+    dma("S", T.yz[:], T.zb[:, RO, :], "z%d" % RO, "", "o2")
+    dma("Y", T.yb[:, 256:512], T.yo[:, 256:512], "yo2 yo3", "", "o4")
+    for s, v in count.items():
+        wait("G", (s, v))

@@ -2,7 +2,8 @@ from concourse.bass import DstId, RemoteDMATransfer
 from concourse.mybir import AluOpType as A, ActivationFunctionType as F, AxisListType
 
 X1 = AxisListType.X
-NE = 3
+NA, NB = 4, 4
+NE = 4
 CV = 4
 
 RO, HN, HZ = 4, [1, 2, 3, 1], [3, 1, 2, 2]
@@ -25,7 +26,7 @@ SCRATCH = {
     "lA": _sb([4, 160], bf), "sM": _sb([4, 128], bf), "sA": _sb([4, 160], bf), "jr": _sb(24 * NV, bf), "one": _sb(128, bf),
     "v2": _sb(8, i32), "h2": _sb(16, i32),
     "mn": _sb([NV, 128], bf), "ad": _sb([NS, 128], bf), "aq": _sb(128, bf), "SB": _sb(960, f32),
-    "FL": _sb([2, 128], bf), "FQ": _sb([3, 128], bf), "PP": _sb(256, f16), "hy": _sb(128, f32), "nn": _sb(128, f32),
+    "FL": _sb([2, 128], bf), "FQ": _sb([4, 128], bf), "PP": _sb(256, f16), "hy": _sb(128, f32), "nn": _sb(128, f32),
     "w1": _sb(16, f32), "wM": _sb(128, f16), "bc": _sb(16, f32), "cnt": _sb(16, f32), "junk": _sb([16, 128], bf),
     "wi": _sb(8, i32), "dw": _sb(16, f32), "ds": _sb(16, f32), "wu": _sb(8, u16),
     "nc": _sb(144, bf), "nMa": _sb(128, bf), "xa": _sb(128, bf), "ns": _sb(128, f32),
@@ -149,8 +150,7 @@ def rank_program(g, core, T, topo):
         return ea, ec, False
 
     def early(src, da, dc):
-        ea, ec, apart = masks(src, da, dc)
-        return (ea, ec) if apart else (ea[:len(ea) // 2], ec[len(ec) // 2:])
+        return masks(src, da, dc)[:2]
 
     def peers(r, t):
         return T.cores[r % N], T.cores[(r + HN[t]) % N], T.cores[(r + HZ[t]) % N]
@@ -159,8 +159,8 @@ def rank_program(g, core, T, topo):
     dma("Y", T.Z[:, 0, 0:8], T.v0[:], "", "v0", "dv")
     dma("Y", T.uwi[:, 0:1], T.uw[:], "", "uwi", "du")
     dma("S", T.zb[:, 0, :], T.z0[:], "", "z0", "dz")
-    dma("S", T.bti[0:128:16, :], T.bt[:], "", "bti", "db")
     dma("Y", T.Bi[:], T.bag[:], "", "Bi", "dB")
+    dma("Y", T.bti[0:128:16, :], T.bt[:], "", "bti", "db")
     dma("Y", T.X[:], T.xt[:], "", "X", "dX")
 
     kb = T.CS[:, 0:128]
@@ -250,6 +250,8 @@ def rank_program(g, core, T, topo):
         mm(blk(4, 7), T.I[:], T.CQ[:], True, False, "CQ0 CQ1 CQ2", "KQ", "4")
         for s in range(4, 7):
             mm(blk(s, s + 1), T.I[:], T.M1[:], False, False, "M1", "KQ", "4")
+        mm(blk(7, 8), T.I[:], T.CQ[:, 0:128], False, False, "", "KQ Kv", "4")
+        mm(blk(7, 8), T.I[:], T.M0[:], False, False, "M0", "KQ", "4")
         mm(blk(4, 6), T.btB[:, t, :], T.RB[:], False, False, "btB%d RB0 RB1" % t, "KQ", "4")
         if t:
             mm(blk(4, 6), T.sA[:, t - 1, 0:128], T.RB[:], False, False, "sA%d" % (t - 1), "KQ", "4")
@@ -261,7 +263,7 @@ def rank_program(g, core, T, topo):
     cp(T.ui[:], T.p7[:, 144:152], "uL", "ui", "7")
     ts(T.u15[:], T.ui[:], 15, None, A.bitwise_and, r="ui", w="u15")
     tt(T.Z[:, 0, 8:16], T.u15[:], T.l16[:], A.add, "u15 l16", "x0i")
-    cp(T.Pu[:, 0, :], T.Bi[:].indirect(T.VX[:, 0, 0:8]), "Bi vu0", "P0")
+    cp(T.Pu[:, 0, :], T.Bi[:].indirect(T.VX[:, 0, 0:8]), "Bi vu0", "P0a P0b")
     cp(T.VX[:, 0, 8:16], T.Z[:, 0, 8:16], "x0i", "xu0")
     cp(T.btf[:], T.bti[:], "bti", "btf")
     cp(T.B[:, 0:1024], T.Bi[:], "Bi", "B")
@@ -271,7 +273,7 @@ def rank_program(g, core, T, topo):
 
     for t in range(RO):
         last = t == RO - 1
-        z, zk, Pk = T.zb[:, t, :], "z%d" % t, "P%d" % t
+        z, zk, Pk = T.zb[:, t, :], "z%d" % t, "P%da P%db" % (t, t)
         xu, xuk = T.VX[:, t, 8:16], "xu%d" % t
         _, da, dc = peers(rank, t)
         ida, idc = topo.addr(da, core), topo.addr(dc, core)
@@ -285,14 +287,19 @@ def rank_program(g, core, T, topo):
                                  src=T.Pu[:, t, :], dst=T.lP[:, t, :]),
                RemoteDMATransfer(dst_ids=[DstId(rid=idc[0], pnc=idc[1])], dma_engine_mask=bits(ec), remote_sem=T.sem["aZ%d" % t],
                                  src=z, dst=T.lZ[:, t, :])]
-        op("G", lambda q: q.remote_dma_fused(trs, local_sem=T.sem.sent), Pk + " " + zk, sem=False)
+        if masks(core, da, dc)[2]:
+            op("G", lambda q: q.remote_dma_fused(trs, local_sem=T.sem.sent), Pk + " " + zk, sem=False)
+        else:
+            op("G", lambda q: q.remote_dma_fused(trs[1:], local_sem=T.sem.sent), zk, sem=False)
+            op("G", lambda q: q.remote_dma_fused(trs[:1], local_sem=T.sem.sent), Pk, sem=False)
         sent[0] += len(ea) + len(ec)
 
 
         for h, GV in enumerate(GVS):
             c = 64 * h
-            cp(T.xg[:, 16 * c:16 * (c + GV)], T.X[:].indirect(T.Pu[:, t, c:c + GV]), "X " + Pk, "xg%da" % h)
-            act(T.xg[:, 16 * (c + GV):16 * c + 1024], T.X[:].indirect(T.Pu[:, t, c + GV:c + 64]), F.Copy, "X " + Pk, "xg%db" % h)
+            cp(T.xg[:, 16 * c:16 * (c + GV)], T.X[:].indirect(T.Pu[:, t, c:c + GV]), "X " + Pk.split()[h], "xg%da" % h)
+            act(T.xg[:, 16 * (c + GV):16 * c + 1024], T.X[:].indirect(T.Pu[:, t, c + GV:c + 64]), F.Copy, "X " + Pk.split()[h],
+                "xg%db" % h)
             xk = "xg%da xg%db" % (h, h)
             pd, bd = (T.p1, "1") if h == 0 else (T.p2, "2")
             if h == 0:
@@ -304,30 +311,40 @@ def rank_program(g, core, T, topo):
                 mm(o, T.W2[:], z, False, False, "W2 " + zk, "Hr", "6")
             mm(T.p0[:, c:c + 64], T.I[:], T.xg[:, 16 * c:16 * c + 1024:16], True, True, xk, "x0", "0")
             for j in range(NS):
-                k = 2 * j + 2
-                mm(pd[:, 64 * j:64 * j + 64], T.I[:], T.xg[:, 16 * c + k:16 * c + 1024:16], True, False, xk, "pd%d" % h, bd)
-                mm(pd[:, 64 * j:64 * j + 64], T.nI[:], T.xg[:, 16 * c:16 * c + 1024:16], False, True, "nI", "pd%d" % h, bd)
+                k, pk_ = 2 * j + 2, "pd%d" % h
+                if h == 1 and j == NB:
+                    for kk in range(1, NA + 1):
+                        tt(T.mn[:, kk - 1, 0:64], T.xg[:, 2 * kk - 1:1024:16], T.p5[:, 0:64], A.min, "xg0a xg0b xa0",
+                           "ma%d" % kk, "5")
+                if h == 1 and j >= NB:
+                    pd, bd, pk_ = T.p5, "5", "pd2"
+                mm(pd[:, 64 * j:64 * j + 64], T.I[:], T.xg[:, 16 * c + k:16 * c + 1024:16], True, False, xk, pk_, bd)
+                mm(pd[:, 64 * j:64 * j + 64], T.nI[:], T.xg[:, 16 * c:16 * c + 1024:16], False, True, "nI", pk_, bd)
             if h == 0:
+                mm(T.p5[:, 0:64], T.I[:], T.xg[:, 0:1024:16], True, True, xk, "xa0", "5")
                 mm(T.p7[:, 0:64], T.nI[:], T.xg[:, 0:1024:16], False, False, xk, "dq", "7")
         xk = "xg0a xg0b xg1a xg1b"
         cp(T.PP[:, 0:128], T.Pu[:, t, :], Pk, "PP0")
+        act(T.ad[:, :, 0:64], T.p1[:, 0:64 * NS], F.Abs, "pd0", "ad0", "1")
+        act(T.ad[:, 0:NB, 64:128], T.p2[:, 0:64 * NB], F.Abs, "pd1", "ad1", "2")
+        act(T.ad[:, NB:NS, 64:128], T.p5[:, 64 * NB:64 * NS], F.Abs, "pd2", "ad2", "5")
+        for k in range(1, NV + 1):
+            c = 64 if k <= NA else 0
+            tt(T.mn[:, k - 1, c:128], T.xg[:, 16 * c + 2 * k - 1:2048:16], T.p0[:, c:128], A.min, xk + " x0", "mn%d" % k, "0")
         if t:
             cp(T.Z[:, t, :], T.vs[:, 1:32:2], "vs", "v%d x%di" % (t, t))
-        act(T.ad[:, :, 0:64], T.p1[:, 0:64 * NS], F.Abs, "pd0", "ad0", "1")
-        act(T.ad[:, :, 64:128], T.p2[:, 0:64 * NS], F.Abs, "pd1", "ad1", "2")
-        for k in range(1, NV + 1):
-            tt(T.mn[:, k - 1, :], T.xg[:, 2 * k - 1:2048:16], T.p0[:, 0:128], A.min, xk + " x0", "mn%d" % k, "0")
         mm(PK[:, 1:4, 1:128:2], T.xg[:, 0:2048:16], T.R0[:], False, False, xk + " R0", "K", "3")
         for k in range(1, NV + 1):
             mm(PK[:, 1:4, 2 * k - 1:128:16], T.xg[:, 2 * k - 1:2048:16], T.R16[:], False, False, "R16", "K", "3")
-        for k in range(1, NV):
-            mm(PK[:, 1:4, 2 * k - 1:128:16], T.mn[:, k - 1, :], T.R32[:], False, False, "mn%d R32" % k, "K", "3")
-        for j in range(NS):
-            mm(PK[:, 1:4, 2 * j + 2:128:16], T.ad[:, j, :], T.R16[:], False, False, "ad0 ad1", "K", "3")
-        mm(PK[:, 1:4, 15:128:16], T.mn[:, NV - 1, :], T.R32[:], False, True, "mn%d" % NV, "K", "3")
+        for k in range(1, NV + 1):
+            mm(PK[:, 1:4, 2 * k - 1:128:16], T.mn[:, k - 1, :], T.R32[:], False, False, "mn%d ma%d R32" % (k, k), "K", "3")
+            if k == NV - 2:
+                for j in range(NB):
+                    mm(PK[:, 1:4, 2 * j + 2:128:16], T.ad[:, j, :], T.R16[:], False, False, "ad0 ad1", "K", "3")
+        for j in range(NB, NS):
+            mm(PK[:, 1:4, 2 * j + 2:128:16], T.ad[:, j, :], T.R16[:], False, j == NS - 1, "ad0 ad2", "K", "3")
         ts(T.v2[:], T.Z[:, t, 0:8], 2.0, None, A.mult, r="v%d" % t, w="v2")
-        ts(T.h2[:, 0:8], T.v2[:], 1023, None, A.bitwise_and, r="v2", w="h2a")
-        ts(T.h2[:, 8:16], T.v2[:], 1023, None, A.bitwise_and, r="v2", w="h2b")
+        cp(T.dv[:, 17:32:2], T.Z[:, t, 8:16], "x%di" % t, "dv2")
 
         def item_sum():
             act(T.xo[:], T.X[:].indirect(xu), F.Copy, "X " + xuk, "xo")
@@ -344,10 +361,13 @@ def rank_program(g, core, T, topo):
         mm(T.p6[:, 256:384], T.I16[:], T.PP[:, 0:128], False, True, "I16 PP0", "Hr", "6")
         item_sum()
         act(T.aq[:], T.p7[:, 0:128], F.Abs, "dq", "aq", "7")
-        for s in range(4, 7):
-            mm(blk(s, s + 1), T.aq[:], T.RB[:, 0:128], False, s == 6, "aq", "KQ", "4")
-        item_wrap()
+        for s in range(4, 8):
+            mm(blk(s, s + 1), T.aq[:], T.RB[:, 0:128], False, s == 7, "aq", "KQ", "4")
         act(T.hy[:], T.p6[:, 256:384], F.Identity, "Hr", "hy", "6", bias=8388607.5, scale=1.0 / 2048)
+        item_wrap()
+        mm(T.p0[:, 384:512], T.I[:], z, True, False, zk, "zs", "0")
+        mm(T.p0[:, 384:512], T.I[:], T.mh[:], False, False, "mh", "zs", "0")
+        mm(T.p0[:, 384:512], T.I[:], T.lZ[:, t, :], False, True, "lZ%d" % t, "zs", "0")
         E1, E2 = T.p2[:, 128:256], T.p2[:, 256:384]
         mm(E1, T.W2[:], z, True, False, "", "E1", "2")
         mm(E2, T.W2[:], z, False, False, "", "E2", "2")
@@ -360,6 +380,8 @@ def rank_program(g, core, T, topo):
                 op("V", lambda q: q.tensor_tensor_scan(T.SB[:, c:c + 64], PK[:, 1, 64 * h:64 * h + 64], d1, 0.0, A.max,
                                                        A.min if j else A.max),
                    "K " + ("m256" if j == 0 else "s%d%d" % (j - 1, h)), "s%d%d" % (j, h), "3")
+            if j < 2:
+                ts(T.h2[:, 8 * j:8 * j + 8], T.v2[:], 1023, None, A.bitwise_and, r="v2", w="h2" + "ab"[j])
 
         def before_e(gs):
             for gi in gs:
@@ -368,13 +390,17 @@ def rank_program(g, core, T, topo):
                     scale=-1.0, bias=T.SB[:, c + 15:c + 16])
 
         act(T.nn[:], T.hy[:], F.Identity, "hy", "nn", bias=2048.0 * 8388624, scale=-2048.0)
+        before_e(range(3))
         act(T.xn[:], T.p1[:, 0:128], F.Identity, "xq", "xn", "1", bias=-128.0)
+        act(T.av1[:], T.p0[:, 384:512], F.Identity, "zs", "av1", "0", bias=MAGIC, scale=0.5)
+        before_e(range(3, 8 - NE))
         mm(E1, T.I32[:], T.nn[:], False, False, "I32 nn", "E1", "2")
+        mm(E2, T.I32[:], T.nn[:], False, False, "", "E2", "2")
         for gi in range(8):
             c = 816 + 16 * gi + 16 * (gi // 4) + 15
             ts(T.FL[:, :, 16 * gi:16 * gi + 16], PK[:, 2:4, 16 * gi:16 * gi + 16], T.SB[:, c:c + 1], None, A.is_le,
                r="K s5%d" % (gi // 4), w="F%d" % gi, b="3")
-            act(T.FQ[:, :, 16 * gi:16 * gi + 16], PK[:, 4:7, 16 * gi:16 * gi + 16], F.Sign, "KQ s5%d" % (gi // 4), "G%d" % gi, "4",
+            act(T.FQ[:, :, 16 * gi:16 * gi + 16], PK[:, 4:8, 16 * gi:16 * gi + 16], F.Sign, "KQ s5%d" % (gi // 4), "G%d" % gi, "4",
                 scale=-1.0, bias=T.SB[:, c:c + 1])
         fl = " ".join("F%d" % gi for gi in range(8))
         fq = " ".join("G%d" % gi for gi in range(8))
@@ -385,12 +411,15 @@ def rank_program(g, core, T, topo):
         mm(T.p7[:, 128:144], T.FQ[:, 2, :], T.R1[:, 129:160:2], False, True, fq + " R1b", "nL", "7")
         mm(T.p6[:, 0:160], T.FQ[:, 1, :], T.R1[:], True, False, "R1a R1b", "amb", "6")
         mm(T.p6[:, 0:160], T.FQ[:, 0, :], T.nR1[:], False, True, "nR1a nR1b", "amb", "6")
-        mm(T.p0[:, 128:256], T.FQ[:, 2, :], T.I[:], True, True, "", "nT", "0")
-        before_e(range(NE))
-        mm(T.p1[:, 128:256], T.I[:], z, True, False, zk, "zs", "1")
-        mm(T.p1[:, 128:256], T.I[:], T.mh[:], False, False, "mh", "zs", "1")
-        mm(T.p1[:, 128:256], T.I[:], T.lZ[:, t, :], False, True, "lZ%d" % t, "zs", "1")
-        mm(E2, T.I32[:], T.nn[:], False, False, "", "E2", "2")
+        act(T.av[:], T.av1[:], F.Identity, "av1", "av", bias=-MAGIC)
+        before_e(range(8 - NE, 8))
+        mm(T.p0[:, 128:256], T.FL[:, 0, :], T.I[:], True, False, "", "Xs", "0")
+        mm(T.p0[:, 128:256], T.FL[:, 1, :], T.I[:], False, False, "", "Xs", "0")
+        mm(T.p0[:, 128:256], T.FQ[:, 3, :], T.I[:], False, True, "", "Xs", "0")
+        mm(T.p1[:, 256:384], T.I[:], T.M2[:], True, False, "", "ub", "1")
+        mm(T.p1[:, 256:384], T.av[:], T.Wu[:], False, True, "av", "ub", "1")
+        mm(T.p1[:, 384:512], T.nc[:, 16:144], T.I[:], True, False, nk, "sT", "1")
+        mm(T.p1[:, 384:512], T.nc[:, 15:143], T.nI[:], False, True, "", "sT", "1")
         cp(T.X[:].indirect(xu), T.xn[:], xuk + " xn", "X")
         act(T.sM[:, t, :], T.p5[:, 0:128], F.Copy, "mid", "sM%d" % t, "5")
         act(T.sA[:, t, :], T.p6[:, 0:160], F.Copy, "amb", "sA%d" % t, "6")
@@ -402,56 +431,51 @@ def rank_program(g, core, T, topo):
         sent[0] += len(ea) + len(ec)
 
         tt(T.w1[:], T.h2[:], T.p7[:, 128:144], A.subtract, "h2a h2b nL", "w1", "7")
-        act(T.nMa[:], T.p0[:, 128:256], F.Copy, "nT", "nMa", "0")
         cp(T.PP[:, 128:256], T.lP[:, t, :], "lP%d" % t, "PP1")
         tt(T.wM[:], T.w1[:, 0:8].indirect(T.oc[:]), T.Dg[:], A.mult, "w1 oc Dg", "wM")
-        ts(T.bc[:], T.w1[:], -128.0, -127.5, A.mult, A.add, "w1", "bc")
         ts(T.wi[:], T.w1[:, 0:8], -6.0, None, A.add, r="w1", w="wi")
-        mm(blk(7, 8), T.I[:], T.jb[:], True, False, "jb", "Kv", "4")
-        mm(blk(7, 8), T.BoK[:], T.wM[:], False, True, "BoK wM", "Kv", "4")
-        mm(T.p5[:, 128:256], T.FL[:, 0, :], T.I[:], True, False, fl, "Xs", "5")
-        mm(T.p5[:, 128:256], T.FL[:, 1, :], T.I[:], False, False, fl, "Xs", "5")
-        mm(T.p5[:, 128:256], T.Bo[:], T.nMa[:], False, True, "Bo nMa", "Xs", "5")
-        mm(E2, T.nI16[:], T.PP[:, 128:256], False, True, "nI16 PP1", "E2", "2")
+        ts(T.bc[:], T.w1[:], -128.0, -127.5, A.mult, A.add, "w1", "bc")
+        mm(E2, T.nI16[:], T.PP[:, 128:256], False, True, "nI16 PP1", "E2 E2c", "2")
+        mm(blk(7, 8), T.I[:], T.jb[:], True, False, "jb", "Kv KQ", "4")
         mm(T.p6[:, 384:512], T.I[:], T.jb[:], True, False, "jb", "Kb", "6")
         mm(T.p6[:, 384:512], T.BoK[:], T.wM[:], False, True, "BoK wM", "Kb", "6")
-        before_e(range(NE, 8))
-        act(T.av1[:], T.p1[:, 128:256], F.Identity, "zs", "av1", "1", bias=MAGIC, scale=0.5)
-        act(T.xa[:], T.p5[:, 128:256], F.Abs, "Xs", "xa", "5", bias=14.0)
-        act(T.av[:], T.av1[:], F.Identity, "av1", "av", bias=-MAGIC)
-        mm(T.p0[:, 0:128], T.nc[:, 16:144], T.I[:], True, False, nk, "sT", "0")
-        mm(T.p0[:, 0:128], T.nc[:, 15:143], T.nI[:], False, True, "", "sT", "0")
+        mm(blk(7, 8), T.BoK[:], T.wM[:], False, True, "BoK wM", "Kv", "4")
+        act(T.xa[:], T.p0[:, 128:256], F.Abs, "Xs", "xa", "0", bias=-1.0)
         act(T.ns[:], T.xa[:], F.Sign, "xa", "ns", scale=-1.0, bias=2.0)
-        act(T.sg[:], T.p0[:, 0:128], F.Copy, "sT", "sg", "0")
-        u_list(T.av[:], "av")
+        act(T.uM[:], T.p1[:, 256:384], F.Relu, "ub", "uM", "1")
+        act(T.sg[:], T.p1[:, 384:512], F.Copy, "sT", "sg", "1")
+        mm(T.p7[:, 144:152], T.uM[:], T.sel32[:], True, True, "uM sel32", "uL", "7")
+
+        def counts(cs):
+            for c in cs:
+                for j in range(2):
+                    n = 8 * j + c
+                    act(T.junk[:, n, 16 * c:128], T.p6[:, 384 + 16 * c:512], F.Sign, "Kb bc", "cnt%d" % n, "6",
+                        bias=T.bc[:, n:n + 1], accum_out=T.cnt[:, n:n + 1])
+
+        counts(range(CV))
         ts(T.Z[:, t, 0:8], T.wi[:], 1023, None, A.bitwise_and, r="wi", w="v%d" % t)
+        tt(E1, E1, T.ns[:], A.mult, "E1 E2c ns", "E1", "2")
+        tt(E2, E2, T.ns[:], A.mult, "E2 ns", "E2", "2")
+        ts(T.dw[:, 1:16:2], T.Z[:, t, 0:8], 1.0 / 1024, None, A.mult, r="v%d" % t, w="dw1")
+        cp(T.dv[:, 1:16:2], T.Z[:, t, 0:8], "v%d" % t, "dv1")
         for c in range(CV, 8):
             ts(T.kd[:, c - CV, 16 * c:128], PK[:, 7, 16 * c:128], T.bc[:, 8 + c:9 + c], 4.0, A.add, A.mult,
                "Kv bc", "kd%d" % c, "4")
-        ts(T.dw[:, 1:16:2], T.Z[:, t, 0:8], 1.0 / 1024, None, A.mult, r="v%d" % t, w="dw1")
+        tt(E1, E1, T.PP[:, 0:128], A.add, "E1 PP0", "E1", "2")
+        cp(T.ui[:], T.p7[:, 144:152], "uL", "ui", "7")
         for c in range(CV, 8):
             op("V", lambda q: q.tensor_reduce(T.cnt[:, 8 + c:9 + c], T.kd[:, c - CV, 16 * c:128], X1, A.min,
                                               apply_absolute_value=True), "kd%d" % c, "cnt%d" % (8 + c))
-        tt(E1, E1, T.ns[:], A.mult, "E1 E2 ns", "E1", "2")
-        tt(E2, E2, T.ns[:], A.mult, "E2 ns", "E2", "2")
-        tt(E1, E1, T.PP[:, 0:128], A.add, "E1 PP0", "E1", "2")
-        tt(T.p0[:, 256:384], E2, T.sg[:], A.mult, "E2 sg", "sd", "20")
         tt(T.sbf[:], E1, T.sg[:], A.mult, "E1 sg", "sbf", "2")
-        for c in range(CV):
-            for j in range(2):
-                n = 8 * j + c
-                act(T.junk[:, n, 16 * c:128], T.p6[:, 384 + 16 * c:512], F.Sign, "Kb bc", "cnt%d" % n, "6",
-                    bias=T.bc[:, n:n + 1], accum_out=T.cnt[:, n:n + 1])
-        cp(T.ui[:], T.p7[:, 144:152], "uL", "ui", "7")
+        ts(T.u15[:], T.ui[:], 15, None, A.bitwise_and, r="ui", w="u15")
         tt(T.dw[:, 2 * CV:16:2], T.cnt[:, CV:8], T.cnt[:, 8 + CV:16], A.subtract,
            "cntc " + " ".join("cnt%d" % n for n in range(8 + CV, 16)), "dw2")
-        ts(T.u15[:], T.ui[:], 15, None, A.bitwise_and, r="ui", w="u15")
+        ck = " ".join("cnt%d" % n for n in range(CV)) + " " + " ".join("cnt%d" % n for n in range(8, 8 + CV))
+        tt(T.dw[:, 0:2 * CV:2], T.cnt[:, 8:8 + CV], T.cnt[:, 0:CV], A.subtract, ck, "dw0")
         ts(T.un[:, 0:8], T.ui[:], 1023, None, A.bitwise_and, r="ui", w="un0")
         tt(T.un[:, 8:16], T.u15[:], T.l16[:], A.add, "u15 l16", "un1")
-        cp(T.dv[:, 1:32:2], T.Z[:, t, :], "v%d x%di" % (t, t), "dv1")
-        ck = " ".join("cnt%d" % n for n in range(16))
-        tt(T.dw[:, 0:2 * CV:2], T.cnt[:, 8:8 + CV], T.cnt[:, 0:CV], A.subtract, ck, "dw0")
-        tt(T.dv[:, 0:32:2], T.un[:], T.Z[:, t, :], A.subtract, "un0 un1 v%d x%di" % (t, t), "dv")
+        tt(T.p0[:, 256:384], E2, T.sg[:], A.mult, "E2 sg", "sd", "20")
         op("V", lambda q: q.tensor_tensor_scan(T.ds[:], T.cap[:], T.dw[:], 0.0, A.min, A.max), "cap dw0 dw1 dw2", "ds")
         if last:
             lands("allsent", "sent", sent[0])
@@ -467,6 +491,7 @@ def rank_program(g, core, T, topo):
         tt(T.tp[:], T.lM[:, t, :], T.p0[:, 256:384], A.mult, lm + " sd", "tp", "0")
         mm(T.p5[:, 0:128], T.Bo16[:], T.tp[:], False, True, "Bo16 tp", "S", "5")
         tt(T.y1[:], T.lM[:, t, :], E2, A.mult, lm + " E2", "y1", "2")
+        tt(T.dv[:, 0:32:2], T.un[:], T.Z[:, t, :], A.subtract, "un0 un1 v%d x%di" % (t, t), "dv")
         ts(T.wu[:], T.ds[:, 1:16:2], 1024.0, None, A.mult, r="ds", w="wu")
         tt(T.y2[:], E1, T.y1[:], A.subtract, "y1 E1", "y2", "2")
         tt(T.rr[:], T.p5[:, 0:128], T.sg[:], A.mult, "S sg", "rr", "5")
@@ -480,17 +505,16 @@ def rank_program(g, core, T, topo):
 
         def pick():
             op("V", lambda q: q.tensor_tensor_scan(T.vs[:], T.lA[:, t, 128:160], T.dv[:], 0.0, A.mult, A.add),
-               la + " dv dv1", "vs")
+               la + " dv dv1 dv2", "vs")
 
-        late = not masks(*sc)[2]
-        if not last and not late:
+        if not last:
             pick()
         tt(T.B[:].indirect(T.wu[:]), T.y2[:], T.rr[:], A.add, "wu y2 rr", "B")
         if not last:
-            if late:
-                pick()
             cp(T.VX[:, t + 1, :], T.vs[:, 1:32:2], "vs", "vu%d xu%d" % (t + 1, t + 1))
-            cp(T.Pu[:, t + 1, :], T.B[:, 0:1024].indirect(T.VX[:, t + 1, 0:8]), "B vu%d" % (t + 1), "P%d" % (t + 1))
+            for h in range(2):
+                cp(T.Pu[:, t + 1, 64 * h:64 * h + 64], T.B[:, 0:1024].indirect(T.VX[:, t + 1, 4 * h:4 * h + 4]),
+                   "B vu%d" % (t + 1), "P%d%s" % (t + 1, "ab"[h]))
     pick()
     cp(T.vf[:], T.vs[:, 1:16:2], "vs", "vf")
     dma("Y", T.yv[:], T.vf[:], "vf", "", "o5")

@@ -1,16 +1,16 @@
 from concourse.bass import DstId, RemoteDMATransfer
-from concourse.mybir import AluOpType as A, ActivationFunctionType as F, AxisListType
-
-X1 = AxisListType.X
-NA, NB = 4, 4
-NE = 4
-CV = 4
+from concourse.mybir import AluOpType as A, ActivationFunctionType as F
 
 RO, HN, HZ = 4, [1, 2, 3, 1], [3, 1, 2, 2]
 NV = 8
 NS = 15 - NV
+NB = 4
+NE = 4
 GVS = (32, 32)
+BP = (0, 448, 864, 1024)
 MAGIC = 12582912.0
+B0 = 7
+KD = [128 * c - 8 * c * (c - 1) for c in range(9)]
 f32, bf, f16, i32, u16 = "float32", "bfloat16", "float16", "int32", "uint16"
 
 
@@ -19,32 +19,31 @@ def _sb(n, d):
 
 
 SCRATCH = {
-    "X": _sb(2048, bf), "Bi": _sb(1024, i32), "B": _sb(1152, f32), "xg": _sb(2048, bf),
-    "Z": _sb([5, 16], i32), "VX": _sb([5, 16], u16), "vf": _sb(8, f32),
+    "X": _sb(2048, bf), "Bi": _sb(1024, i32), "B": _sb(1168, f32), "xg": _sb(2048, bf),
+    "Z": _sb(8, i32), "VX": _sb([4, 16], u16), "vf": _sb(8, f32), "O": _sb([5, 48], f32),
     "uwi": _sb(4, i32), "bti": _sb(4, i32), "zb": _sb([5, 128], bf),
-    "Pu": _sb([4, 128], u16), "lP": _sb([4, 128], u16), "lZ": _sb([4, 128], bf), "lM": _sb([4, 128], bf),
-    "lA": _sb([4, 160], bf), "sM": _sb([4, 128], bf), "sA": _sb([4, 160], bf), "jr": _sb(24 * NV, bf), "one": _sb(128, bf),
-    "v2": _sb(8, i32), "h2": _sb(16, i32),
-    "mn": _sb([NV, 128], bf), "ad": _sb([NS, 128], bf), "aq": _sb(128, bf), "SB": _sb(960, f32),
-    "FL": _sb([2, 128], bf), "FQ": _sb([4, 128], bf), "PP": _sb(256, f16), "hy": _sb(128, f32), "nn": _sb(128, f32),
-    "w1": _sb(16, f32), "wM": _sb(128, f16), "bc": _sb(16, f32), "cnt": _sb(16, f32), "junk": _sb([16, 128], bf),
-    "wi": _sb(8, i32), "dw": _sb(16, f32), "ds": _sb(16, f32), "wu": _sb(8, u16),
-    "nc": _sb(144, bf), "nMa": _sb(128, bf), "xa": _sb(128, bf), "ns": _sb(128, f32),
-    "sg": _sb(128, f32), "av1": _sb(128, f32), "av": _sb(128, bf), "uM": _sb(128, f32), "ui": _sb(8, i32),
-    "u15": _sb(8, i32), "un": _sb(16, i32), "dv": _sb(32, f32), "vs": _sb(32, f32),
+    "Pu": _sb(128, u16), "PP": _sb([4, 128], f16), "lP": _sb([4, 128], f16), "lZ": _sb([4, 128], bf), "lM": _sb([4, 128], bf),
+    "lA": _sb([4, 160], bf), "sM": _sb([4, 128], bf), "sA": _sb([4, 160], bf), "one": _sb(128, bf),
+    "v2": _sb(8, i32), "h2": _sb(16, i32), "hM": _sb(128, f16),
+    "mn": _sb([NV, 128], bf), "ad": _sb([NS, 128], bf), "dd": _sb([NS - NB, 64], bf), "aq": _sb(128, bf), "SB": _sb(960, f32),
+    "FL": _sb([2, 128], bf), "FQ": _sb([4, 128], bf), "hy": _sb(128, f32), "nn": _sb(128, f16),
+    "kd": _sb(576, bf), "km": _sb(576, bf), "rs": _sb(576, bf), "ds": _sb(16, f32), "wu": _sb(8, u16), "wl": _sb(8, f32),
+    "nc": _sb(144, bf), "xa": _sb(128, bf), "ns": _sb(128, f32), "be": _sb(128, f16),
+    "sg": _sb(128, f32), "av1": _sb(128, f32), "av": _sb(128, bf), "uM": _sb(128, f32), "ui": _sb(16, i32),
+    "u15": _sb(8, i32), "un": _sb(16, i32),
     "xo": _sb(128, bf), "xs": _sb(128, bf), "xn": _sb(128, bf), "sbf": _sb(128, f16),
     "tp": _sb(128, f16), "y1": _sb(128, f32), "y2": _sb(128, f32), "rr": _sb(128, f32), "zr": _sb(256, bf),
-    "yo": _sb(512, f32), "kd": _sb([8 - CV, 128], f32),
-    "pi": _sb(4, i32), "pc": _sb(4, i32), "pf": _sb(4, f32), "jb": _sb(128, bf), "gb": _sb(128, bf), "j24": _sb(24, bf),
-    "ci": _sb(8, f32), "tA": _sb(128, i32), "tB": _sb(128, i32), "tC": _sb(128, i32), "ok": _sb(128, bf),
-    "I": _sb(128, bf), "nI": _sb(128, bf), "I16": _sb(128, f16), "nI16": _sb(128, f16), "I32": _sb(128, f32),
+    "yo": _sb(512, f32),
+    "pi": _sb(4, i32), "pc": _sb(4, i32), "pf": _sb(8, f32), "jb": _sb(128, bf), "gb": _sb(128, bf), "j24": _sb(24, bf),
+    "ci": _sb(8, f32), "tA": _sb(128, i32), "tC": _sb(128, i32), "ok": _sb(128, bf),
+    "I": _sb(128, bf), "nI": _sb(128, bf), "IQ": _sb(128, bf),
     "IX": _sb(128, bf), "Bo": _sb(128, bf), "RB": _sb(256, bf), "Bo8": _sb(128, bf), "nBo8": _sb(128, bf),
-    "BoK": _sb(128, f16), "nBo16": _sb(128, f16), "Bo16": _sb(128, f16), "Dg": _sb(128, bf), "M0": _sb(128, bf),
-    "M1": _sb(128, bf), "M2": _sb(128, bf), "CS": _sb(384, bf), "CQ": _sb(384, bf), "R0": _sb(24 * NV, bf),
-    "R16": _sb(24, bf), "R32": _sb(24, bf), "R1": _sb(160, bf), "nR1": _sb(160, bf), "sel32": _sb(8, f32),
-    "big": _sb(128, f32), "m256": _sb(128, bf), "mh": _sb(128, bf), "btf": _sb(4, f32), "btB": _sb([4, 128], bf),
-    "W2": _sb(128, f16), "Wu": _sb(128, f16), "uwx": _sb(4, i32), "uwf": _sb(4, f32),
-    "oc": _sb(8, u16), "l16": _sb(8, f32), "cl": _sb(16, bf), "cap": _sb(16, f32),
+    "BoK": _sb(128, bf), "nBo": _sb(128, bf), "Dg": _sb(128, bf), "top": _sb(64, f32),
+    "hc": _sb(128, bf), "M2": _sb(128, bf), "CS": _sb(256, bf), "CQ": _sb(512, bf), "sel": _sb(24, bf),
+    "R16": _sb(24, bf), "R32": _sb(24, bf), "R1": _sb(160, bf), "nR1": _sb(160, bf), "sel32": _sb(16, f32),
+    "m256": _sb(128, bf), "mh": _sb(128, bf), "btf": _sb(4, f32), "btB": _sb([4, 128], bf),
+    "W2": _sb(128, f16), "Wu": _sb(128, f16), "uwf": _sb(4, f32),
+    "oc": _sb(8, u16), "ke": _sb(2, u16), "l16": _sb(8, f32), "cl": _sb([2, 16], f16), "cu": _sb(16, f16), "cap": _sb(16, f32),
     "p0": ("psum", [128, 512], f32), "p1": ("psum", [128, 512], f32), "p2": ("psum", [128, 512], f32),
     "PK": ("psum", [128, 8, 128], f32), "p5": ("psum", [128, 512], f32), "p6": ("psum", [128, 512], f32),
     "p7": ("psum", [128, 512], f32),
@@ -120,6 +119,9 @@ def rank_program(g, core, T, topo):
     def cp(out, x, r="", w="", b=""):
         op("V", lambda q: q.tensor_copy(out, x), r, w, b)
 
+    def scan(out, x, y, init, o0, o1, r="", w="", b=""):
+        op("V", lambda q: q.tensor_tensor_scan(out, x, y, init, o0, o1), r, w, b)
+
     def act(out, x, fn, r="", w="", b="", **kw):
         op("S", lambda q: q.activation(out, x, fn, **kw), r, w, b)
 
@@ -138,250 +140,271 @@ def rank_program(g, core, T, topo):
         else:
             op("G", lambda q: q.iota(out, pat, 0, cm, allow_small_or_imprecise_dtypes=True), "", w)
 
-    def bits(es):
-        return sum(1 << e for e in es)
-
-    def masks(src, da, dc):
+    def masks(r, t):
+        src, da, dc = T.cores[r % N], T.cores[(r + HN[t]) % N], T.cores[(r + HZ[t]) % N]
         ea, ec = topo.engines(src, da), topo.engines(src, dc)
         if len(ea) > len(ec):
-            return [e for e in ea if e not in ec], ec, True
+            return [e for e in ea if e not in ec], ec
         if len(ec) > len(ea):
-            return ea, [e for e in ec if e not in ea], True
-        return ea, ec, False
-
-    def early(src, da, dc):
-        return masks(src, da, dc)[:2]
-
-    def peers(r, t):
-        return T.cores[r % N], T.cores[(r + HN[t]) % N], T.cores[(r + HZ[t]) % N]
-
-    ms(T.bti[:], 0, "bti")
-    dma("Y", T.Z[:, 0, 0:8], T.v0[:], "", "v0", "dv")
-    dma("Y", T.uwi[:, 0:1], T.uw[:], "", "uwi", "du")
-    dma("S", T.zb[:, 0, :], T.z0[:], "", "z0", "dz")
-    dma("Y", T.Bi[:], T.bag[:], "", "Bi", "dB")
-    dma("Y", T.bti[0:128:16, :], T.bt[:], "", "bti", "db")
-    dma("Y", T.X[:], T.xt[:], "", "X", "dX")
-
-    kb = T.CS[:, 0:128]
-    iota(T.pi[:, 0:1], [[0, 1]], 1, "pi", True)
-    iota(T.gb[:], [[1, 8], [0, 16]], 0, "gb")
-    iota(T.jb[:], [[1, 128]], 0, "jb")
-    iota(kb, [[0, 8], [1, 16]], 0, "kb")
-    iota(T.j24[:], [[0, 3], [1, 8]], 0, "j24")
-    iota(T.ci[:], [[16, 8]], 0, "ci")
-    iota(T.jr[:], [[0, 3], [1, 8], [0, NV]], 0, "jr")
-    ms(T.m256[:], -256.0, "m256")
-    ms(T.mh[:], -0.5, "mh")
-    ms(T.CS[:, 128:256], 16.0, "CS1")
-    ms(T.CS[:, 256:384], 0.0, "CS2")
-    ts(T.pc[:, 0:1], T.pi[:, 0:1], 4, None, A.arith_shift_right, r="pi", w="pc0")
-    ts(T.pc[:, 1:2], T.pi[:, 0:1], 15, None, A.bitwise_and, r="pi", w="pc1")
-    cp(T.pf[:, 2:3], T.pi[:, 0:1], "pi", "pf2")
-    for s, c in enumerate((-31.0, 1.0, -31.0)):
-        act(T.CQ[:, 128 * s:128 * s + 128], T.mh[:], F.Identity, "mh", "CQ%d" % s, scale=c)
-    cp(T.pf[:, 0:2], T.pc[:, 0:2], "pc0 pc1", "pf0")
-    pg, pk, pp = T.pf[:, 0:1], T.pf[:, 1:2], T.pf[:, 2:3]
-    ms(T.SB[:, 15:960:80], 0.0, " ".join("s%d%d" % (j, h) for j in range(6) for h in range(2)))
-    ms(T.nc[:, 0:16], 0.0, "nc")
-    ms(T.cap[:], -1.0, "cap")
-    ms(T.cl[:], 0.0, "cl")
-    ms(T.R1[:, 128:160], 0.0, "R1b")
-    ms(T.nR1[:, 128:160], 0.0, "nR1b")
-    ts(T.Bo[:], T.gb[:], pg, None, A.is_equal, r="gb pf0", w="Bo")
-    for name, c in (("BoK", 128.0), ("nBo16", -1.0), ("Bo16", 1.0)):
-        ts(T[name][:], T.gb[:], pg, c, A.is_equal, A.mult, "gb pf0", name)
-    ts(T.I[:], T.jb[:], pp, None, A.is_equal, r="jb pf2", w="I")
-    for name, c in (("I16", 1.0), ("nI16", -1.0)):
-        ts(T[name][:], T.jb[:], pp, c, A.is_equal, A.mult, "jb pf2", name)
-    ts(T.Dg[:], kb, pk, None, A.is_equal, r="kb pf0", w="Dg")
-    ts(T.ok[:], kb, 2.0, 1.0, A.mult, A.add, "kb", "ok")
-    ts(T.R16[:], T.j24[:], pg, 16.0, A.is_equal, A.mult, "j24 pf0", "R16")
-    ts(T.R32[:], T.j24[:], pg, -32.0, A.is_equal, A.mult, "j24 pf0", "R32")
-    ts(T.sel32[:], T.j24[:, 0:8], pg, None, A.is_equal, r="j24 pf0", w="sel32")
-    ts(T.R1[:, 129:160:2], T.j24[:, 0:16], pg, 0.5, A.is_equal, A.mult, "j24 pf0", "R1b")
-    ts(T.nR1[:, 129:160:2], T.j24[:, 0:16], pg, -0.5, A.is_equal, A.mult, "j24 pf0", "nR1b")
-    ts(T.oc[:], T.ci[:], 0.0625, None, A.mult, r="ci", w="oc")
-    ts(T.l16[:], T.ci[:], pk, 16.0, A.add, A.mult, "ci pf0", "l16")
-    act(T.M0[:], T.gb[:], F.Identity, "gb", "M0", scale=65536.0)
-    act(T.RB[:, 0:128], T.Bo[:], F.Identity, "Bo", "RB0", scale=16.0)
-    act(T.RB[:, 128:256], T.Bo[:], F.Identity, "Bo", "RB1", scale=-16.0)
-    act(T.nI[:], T.I[:], F.Identity, "I", "nI", scale=-1.0)
-    act(T.M1[:], T.Dg[:], F.Identity, "Dg", "M1", scale=-1048576.0, bias=1048576.0)
-    act(T.M2[:], T.Dg[:], F.Identity, "Dg", "M2", scale=16777216.0, bias=-16777216.0)
-    for name, src, c in (("Bo8", "Bo", 8.0), ("nBo8", "Bo", -8.0), ("I32", "I", 1.0), ("IX", "I", -128.0)):
-        act(T[name][:], T[src][:], F.Identity, src, name, scale=c)
-    act(T.R1[:, 0:128], T.I[:], F.Identity, "I", "R1a", scale=16.0)
-    act(T.nR1[:, 0:128], T.I[:], F.Identity, "I", "nR1a", scale=-16.0)
-    ts(T.cl[:, 8:16], T.l16[:], -1.0 / 2048, 127.0 / 128, A.mult, A.add, "l16", "cl")
-    ts(T.cl[:, 8 + CV:16], T.l16[:, CV:8], -1.0 / 4096, 127.0 / 256, A.mult, A.add, "l16", "cl")
-    ts(T.cnt[:, CV:8], T.l16[:, CV:8], -0.125, 254.0, A.mult, A.add, "l16", "cntc")
-    ts(T.cap[:, 1:16:2], T.l16[:], 1.0 / 16384, 1.0, A.mult, A.add, "l16", "cap")
-    cp(T.VX[:, 0, 0:8], T.Z[:, 0, 0:8], "v0", "vu0")
-    ts(T.uwx[:, 0:1], T.uwi[:, 0:1], 2047, None, A.bitwise_and, r="uwi", w="uwx0")
-    ts(T.R0[:], T.jr[:], pg, 16.0, A.is_equal, A.mult, "jr pf0", "R0")
-    cp(T.uwf[:, 0:1], T.uwx[:, 0:1], "uwx0", "uwf0")
-    ts(T.Wu[:], T.Bo[:], T.uwf[:, 0:1], None, A.mult, r="Bo uwf0", w="Wu")
-    ts(T.tC[:], T.ok[:], T.uwf[:, 0:1], None, A.mult, r="ok uwf0", w="tC")
-    act(T.one[:], T.mh[:], F.Identity, "mh", "one", scale=-2.0)
+            return ea, [e for e in ec if e not in ea]
+        return ea, ec
 
     sent = [0]
+
+    def send(kind, t, src, dst, r):
+        j = 0 if kind in "PM" else 1
+        hop = (HN, HZ)[j][t]
+        es = masks(rank, t)[j]
+        rid, pid = topo.addr(T.cores[(rank + hop) % N], core)
+        sem = "a%s%d" % (kind, t)
+        lands("l%s%d" % (kind, t), sem, len(masks(rank - hop, t)[j]))
+        op("G", lambda q: q.remote_dma(dst, src, T.sem[sem], T.sem.sent, pid, rid, sum(1 << e for e in es)), r, sem=False)
+        sent[0] += len(es)
+
+    ms(T.bti[:], 0, "bti")
+    dma("Y", T.uwi[:, 0:1], T.uw[:], "", "uwi", "du")
+    dma("S", T.zb[:, 0, :], T.z0[:], "", "z0", "dz")
+    dma("Y", T.Z[:], T.v0[:], "", "v0", "dv")
+    dma("Y", T.bti[0:128:16, :], T.bt[:], "", "bti", "db")
+    dma("Y", T.Bi[:], T.bag[:], "", "Bi", "dB")
+    dma("Y", T.X[:], T.xt[:], "", "X", "dX")
+
     PK = T.PK
+    uL, nL, ub = T.p7[:, 144:160], T.p1[:, 0:16], T.p7[:, 256:384]
+    kb = T.CS[:, 0:128]
+    pg, pk, pp = T.pf[:, 0:1], T.pf[:, 1:2], T.pf[:, 2:3]
 
     def blk(a, b):
         return PK[:, a, :] if b == a + 1 else PK[:, a:b, :]
 
-    def u_list(zz, kk):
-        o = T.p1[:, 256:384]
-        mm(o, T.I[:], T.M2[:], True, False, "I M2", "ub", "1")
-        mm(o, zz, T.Wu[:], False, True, kk + " Wu", "ub", "1")
-        act(T.uM[:], o, F.Relu, "ub", "uM", "1")
-        mm(T.p7[:, 144:152], T.uM[:], T.sel32[:], True, True, "uM sel32", "uL", "7")
+    def scaled(src, *outs):
+        for name, out, c in outs:
+            act(out, T[src][:], F.Identity, src, name, scale=c)
 
-    def key_start(t):
-        mm(blk(1, 4), T.I[:], T.CS[:], True, False, "I kb CS1 CS2", "K", "3")
-        for s in range(1, 4):
-            mm(blk(s, s + 1), T.I[:], T.M0[:], False, False, "M0", "K", "3")
-        mm(blk(2, 4), T.btB[:, t, :], T.RB[:], False, False, "btB%d RB0 RB1" % t, "K", "3")
-        if t:
-            mm(blk(2, 4), T.sA[:, t - 1, 0:128], T.RB[:], False, False, "sA%d" % (t - 1), "K", "3")
+    iota(T.pi[:, 0:1], [[0, 1]], 1, "pi", True)
+    iota(T.gb[:], [[1, 8], [0, 16]], 0, "gb")
+    iota(kb, [[0, 8], [1, 16]], 0, "kb")
+    iota(T.jb[:], [[1, 128]], 0, "jb")
+    iota(T.j24[:], [[0, 3], [1, 8]], 0, "j24")
+    iota(T.ci[:], [[16, 8]], 0, "ci")
+    ms(T.mh[:], -0.5, "mh")
+    ms(T.top[:], 1048576.0, "top")
+    ms(T.SB[:, 15:960:80], 0.0, " ".join("s%d%d" % (j, h) for j in range(6) for h in range(2)))
+    ms(T.nc[:, 0:16], 0.0, "nc")
+    ts(T.pc[:, 0:1], T.pi[:, 0:1], 4, None, A.arith_shift_right, r="pi", w="pc0")
+    ts(T.pc[:, 1:2], T.pi[:, 0:1], 15, None, A.bitwise_and, r="pi", w="pc1")
+    cp(T.pf[:, 2:3], T.pi[:, 0:1], "pi", "pf2")
+    ms(T.cap[:], -1.0, "cap")
+    ms(T.top[:, 0:64:16], 0.0, "top")
+    ms(T.R1[:, 128:160], 0.0, "R1b")
+    cp(T.pf[:, 0:2], T.pc[:, 0:2], "pc0 pc1", "pf0")
+    ms(T.nR1[:, 128:160], 0.0, "nR1b")
+    ms(T.cl[:, 0, 0:8], 7.0, "cl0")
+    ms(T.cl[:, 1, 0:8], 6.0, "cl1")
+    ts(T.ok[:], kb, 2.0, 1.0, A.mult, A.add, "kb", "ok")
+    ts(T.Bo[:], T.gb[:], pg, None, A.is_equal, r="gb pf0", w="Bo")
+    ts(T.Dg[:], kb, pk, None, A.is_equal, r="kb pf0", w="Dg")
+    ts(T.pf[:, 3:4], pk, -8.0, 128.0, A.mult, A.add, "pf0", "pf3")
+    ts(T.pf[:, 4:5], pk, 1.0, None, A.add, r="pf0", w="pf4")
+    tt(T.ok[:], T.ok[:], T.Bo[:], A.mult, "Bo", "ok")
+    ts(T.uwf[:, 0:1], T.uwi[:, 0:1], -2048.0, None, A.add, r="uwi", w="uwf0")
+    ts(T.I[:], T.jb[:], pp, None, A.is_equal, r="jb pf2", w="I")
+    ts(T.pf[:, 5:6], pk, 0.0, 4194304.0, A.is_equal, A.mult, "pf0", "pf5")
+    ts(T.pf[:, 6:7], pk, 1.0, 0.5, A.is_equal, A.mult, "pf0", "pf6")
+    ts(T.Wu[:], T.Bo[:], T.uwf[:, 0:1], None, A.mult, r="Bo uwf0", w="Wu")
+    ts(T.tC[:], T.ok[:], T.uwf[:, 0:1], 66560.0, A.mult, A.add, r="ok uwf0", w="tC")
+    ts(T.sel[:], T.j24[:], pg, None, A.is_equal, r="j24 pf0", w="sel")
+    cp(T.VX[:, 0, 8:16], T.Z[:], "v0", "vu0")
+    cp(T.btf[:], T.bti[:], "bti", "btf")
+    ts(T.tA[:], T.tC[:], 2047, None, A.bitwise_and, r="tC", w="tA")
+    ts(T.l16[:], T.ci[:], pk, 16.0, A.add, A.mult, "ci pf0", "l16")
+    ts(T.oc[:], T.ci[:], 0.0625, None, A.mult, r="ci", w="oc")
+    ts(T.v2[:], T.Z[:], 2.0, None, A.mult, r="v0", w="v2")
+    ts(T.W2[:], T.tA[:], -1024.0, None, A.add, r="tA", w="W2")
+
+    scaled("mh", ("one", T.one[:], -2.0), ("CQ3", T.CQ[:, 384:512], -31.0), ("m256", T.m256[:], 512.0),
+           ("CS1", T.CS[:, 128:256], -32.0))
+    scaled("Bo", ("RB0", T.RB[:, 0:128], 16.0), ("RB1", T.RB[:, 128:256], -16.0))
+    act(T.M2[:], T.Dg[:], F.Identity, "Dg", "M2", scale=16777216.0, bias=-8388608.0)
+    for s, c in enumerate((15.5, -0.5, 15.5)):
+        act(T.CQ[:, 128 * s:128 * s + 128], T.Dg[:], F.Identity, "Dg", "CQ%d" % s, scale=c - 1048576.0, bias=1048576.0)
+    scaled("I", ("nI", T.nI[:], -1.0))
+    act(T.hc[:], T.one[:], F.Identity, "one pf5 pf6", "hc", scale=T.pf[:, 5:6], bias=T.pf[:, 6:7])
+    act(T.sel32[:], T.sel[:, 0:16], F.Identity, "sel", "sel32")
+
+    def u_list(less):
+        if less:
+            mm(uL, T.I[:], T.cu[:], True, False, "cu0 cu1", "uL", "7")
+        mm(uL, T.uM[:], T.sel32[:], not less, True, "uM sel32", "uL", "7")
+
+    def bands(t):
+        act(T.btB[:, t, :], T.one[:], F.Identity, "one btf", "btB%d" % t, scale=T.btf[:, t:t + 1])
+
+    mm(ub, T.I[:], T.M2[:], True, False, "I M2", "ub", "7")
+    mm(ub, T.zb[:, 0, :], T.Wu[:], False, True, "z0 Wu", "ub", "7")
+    act(T.uM[:], ub, F.Relu, "ub", "uM", "7")
+    u_list(False)
+    send("Z", 0, T.zb[:, 0, :], T.lZ[:, 0, :], "z0")
+    bands(0)
+    scaled("sel", ("R16", T.R16[:], 16.0), ("R32", T.R32[:], -32.0))
+    scaled("Bo", ("Bo8", T.Bo8[:], 8.0), ("nBo8", T.nBo8[:], -8.0), ("nBo", T.nBo[:], -1.0))
+    for t in range(1, RO):
+        bands(t)
+    iota(T.rs[:], [[0, KD[8]]], 0, "rs")
+    for c in range(8):
+        op("G", lambda q: q.iota(T.rs[:, KD[c]:KD[c] + 1], [[0, 1]], 4096, 0, allow_small_or_imprecise_dtypes=True),
+           "rs", "rs%d" % c)
+    cp(T.Pu[:], T.Bi[:].indirect(T.VX[:, 0, 8:16]), "Bi vu0", "Pa Pb")
+    cp(T.ui[:, 0:8], uL[:, 0:8], "uL", "ui", "7")
+    ts(T.ke[:, 0:1], T.pf[:, 3:4], T.pf[:, 4:5], -1.0, A.mult, A.add, "pf3 pf4", "ke")
+    for j in range(2):
+        ts(T.cl[:, j, 8:16], T.l16[:], -1.0 / 4096, 7.25, A.mult, A.add, "l16", "cm%d" % j)
+    ts(T.u15[:], T.ui[:, 0:8], 15, None, A.bitwise_and, r="ui", w="u15")
+    ms(T.cu[:, 0:8], 0.0, "cu0")
+    ms(T.cu[:, 8:16], 1023.0, "cu1")
+    cp(T.B[:, B0 + 1024:B0 + 1025], T.Bi[:, 0:1], "Bi", "Bz")
+    tt(T.O[:, 0, 1:16:2], T.u15[:], T.l16[:], A.add, "u15 l16", "xi0")
+    act(T.cap[:, 1:16:2], T.l16[:], F.Identity, "l16", "cap", scale=1.0 / 16, bias=1025.0)
+
+    def late_constants():
+        scaled("I", ("IX", T.IX[:], -128.0), ("IQ", T.IQ[:], -2048.0), ("R1a", T.R1[:, 0:128], 16.0),
+               ("nR1a", T.nR1[:, 0:128], -16.0))
+        scaled("Bo", ("BoK", T.BoK[:], 256.0))
+        act(T.R1[:, 129:160:2], T.sel[:, 0:16], F.Identity, "sel", "R1b", scale=0.5)
+        act(T.nR1[:, 129:160:2], T.sel[:, 0:16], F.Identity, "sel", "nR1b", scale=-0.5)
+
+    def bag_copy(j):
+        cp(T.B[:, B0 + BP[j]:B0 + BP[j + 1]], T.Bi[:, BP[j]:BP[j + 1]], "Bi", "B%d" % j)
+
+    rsk = " ".join("rs%d" % c for c in range(8))
+
+    dq, xr, zs = T.p7[:, 0:128], T.p7[:, 128:256], T.p7[:, 384:512]
+    xq, Hr = T.p2[:, 0:128], T.p2[:, 128:256]
+    E1, E2 = T.p2[:, 256:384], T.p2[:, 384:512]
 
     def query_start(t):
-        mm(blk(4, 7), T.I[:], T.CQ[:], True, False, "CQ0 CQ1 CQ2", "KQ", "4")
-        for s in range(4, 7):
-            mm(blk(s, s + 1), T.I[:], T.M1[:], False, False, "M1", "KQ", "4")
-        mm(blk(7, 8), T.I[:], T.CQ[:, 0:128], False, False, "", "KQ Kv", "4")
-        mm(blk(7, 8), T.I[:], T.M0[:], False, False, "M0", "KQ", "4")
+        mm(blk(4, 8), T.I[:], T.CQ[:], True, False, "CQ0 CQ1 CQ2 CQ3", "KQ", "4")
         mm(blk(4, 6), T.btB[:, t, :], T.RB[:], False, False, "btB%d RB0 RB1" % t, "KQ", "4")
         if t:
             mm(blk(4, 6), T.sA[:, t - 1, 0:128], T.RB[:], False, False, "sA%d" % (t - 1), "KQ", "4")
 
-    tt(T.M1[:], T.M1[:], T.M0[:], A.add, "M1 M0", "M1")
-    u_list(T.zb[:, 0, :], "z0")
-    ts(T.tA[:], T.tC[:], 2047, None, A.bitwise_and, r="tC", w="tA")
-    tt(T.W2[:], T.tA[:], T.Bo[:], A.mult, "tA Bo", "W2")
-    cp(T.ui[:], T.p7[:, 144:152], "uL", "ui", "7")
-    ts(T.u15[:], T.ui[:], 15, None, A.bitwise_and, r="ui", w="u15")
-    tt(T.Z[:, 0, 8:16], T.u15[:], T.l16[:], A.add, "u15 l16", "x0i")
-    cp(T.Pu[:, 0, :], T.Bi[:].indirect(T.VX[:, 0, 0:8]), "Bi vu0", "P0a P0b")
-    cp(T.VX[:, 0, 8:16], T.Z[:, 0, 8:16], "x0i", "xu0")
-    cp(T.btf[:], T.bti[:], "bti", "btf")
-    cp(T.B[:, 0:1024], T.Bi[:], "Bi", "B")
-    for t in range(RO):
-        act(T.btB[:, t, :], T.one[:], F.Identity, "one btf", "btB%d" % t, scale=T.btf[:, t:t + 1])
+    def step_start(t):
+        mm(blk(1, 2), T.I[:], kb, True, False, "I kb", "K Kb", "3")
+        mm(blk(2, 4), T.btB[:, t, :], T.RB[:], False, False, "btB%d RB0 RB1" % t, "K", "3")
+        mm(blk(2, 3), T.I[:], T.CS[:, 128:256], False, False, "CS1", "K", "3")
+        if t:
+            mm(blk(2, 4), T.sA[:, t - 1, 0:128], T.RB[:], False, False, "sA%d" % (t - 1), "K", "3")
+        z, zk = T.zb[:, t, :], "z%d" % t
+        mm(Hr, T.Bo[:], T.hc[:], True, False, "hc", "E1 E2 Hr", "2")
+        mm(zs, T.I[:], T.mh[:], True, False, "mh", "al", "7")
+        mm(Hr, T.W2[:], z, False, False, "W2 " + zk, "Hr", "2")
+        for o, k, b in ((xq, "Hr", "2"), (dq, "al", "7"), (zs, "al", "7"), (xr, "al", "7")):
+            mm(o, T.I[:], z, False, False, zk, k, b)
+
+    def own_items(t):
+        act(T.xo[:], T.X[:].indirect(T.VX[:, t, 0:8]), F.Copy, "X xu%d" % t, "xo")
+
+    def own_sums():
+        mm(xq, T.I[:], T.xo[:], False, False, "xo", "Hr", "2")
+        mm(xr, T.I[:], T.xo[:], False, False, "xo", "al", "7")
+
+    def wraps():
+        act(T.xs[:], xq, F.Sign, "Hr", "xs", "2", bias=-255.5)
+        act(T.hy[:], Hr, F.Identity, "Hr", "hy", "2", bias=8388607.5, scale=1.0 / 2048)
+
     query_start(0)
+    step_start(0)
+    W = T.B[:, B0 + 1:]
 
     for t in range(RO):
         last = t == RO - 1
-        z, zk, Pk = T.zb[:, t, :], "z%d" % t, "P%da P%db" % (t, t)
-        xu, xuk = T.VX[:, t, 8:16], "xu%d" % t
-        _, da, dc = peers(rank, t)
-        ida, idc = topo.addr(da, core), topo.addr(dc, core)
-        sa, sc = peers(rank - HN[t], t), peers(rank - HZ[t], t)
-        lands("lP%d" % t, "aP%d" % t, len(early(*sa)[0]))
-        lands("lZ%d" % t, "aZ%d" % t, len(early(*sc)[1]))
-        lands("lM%d" % t, "aM%d" % t, len(masks(*sa)[0]))
-        lands("lA%d" % t, "aA%d" % t, len(masks(*sc)[1]))
-        ea, ec = early(core, da, dc)
-        trs = [RemoteDMATransfer(dst_ids=[DstId(rid=ida[0], pnc=ida[1])], dma_engine_mask=bits(ea), remote_sem=T.sem["aP%d" % t],
-                                 src=T.Pu[:, t, :], dst=T.lP[:, t, :]),
-               RemoteDMATransfer(dst_ids=[DstId(rid=idc[0], pnc=idc[1])], dma_engine_mask=bits(ec), remote_sem=T.sem["aZ%d" % t],
-                                 src=z, dst=T.lZ[:, t, :])]
-        if masks(core, da, dc)[2]:
-            op("G", lambda q: q.remote_dma_fused(trs, local_sem=T.sem.sent), Pk + " " + zk, sem=False)
-        else:
-            op("G", lambda q: q.remote_dma_fused(trs[1:], local_sem=T.sem.sent), zk, sem=False)
-            op("G", lambda q: q.remote_dma_fused(trs[:1], local_sem=T.sem.sent), Pk, sem=False)
-        sent[0] += len(ea) + len(ec)
+        z, zk = T.zb[:, t, :], "z%d" % t
+        xu, xuk = T.VX[:, t, 0:8], "xu%d" % t
+        O, PP, Pk = T.O[:, t, :], T.PP[:, t, :], "PP%d" % t
+        xik, ck = "xi%d" % t, "c%d" % t
 
-
+        x0 = ((T.p5[:, 0:64], "5"), (T.p0[:, 64:128], "0"))
+        pds = ((T.p1, "1"), (T.p6, "6"))
         for h, GV in enumerate(GVS):
             c = 64 * h
-            cp(T.xg[:, 16 * c:16 * (c + GV)], T.X[:].indirect(T.Pu[:, t, c:c + GV]), "X " + Pk.split()[h], "xg%da" % h)
-            act(T.xg[:, 16 * (c + GV):16 * c + 1024], T.X[:].indirect(T.Pu[:, t, c + GV:c + 64]), F.Copy, "X " + Pk.split()[h],
+            cp(T.xg[:, 16 * c:16 * (c + GV)], T.X[:].indirect(T.Pu[:, c:c + GV]), "X P" + "ab"[h], "xg%da" % h)
+            act(T.xg[:, 16 * (c + GV):16 * c + 1024], T.X[:].indirect(T.Pu[:, c + GV:c + 64]), F.Copy, "X P" + "ab"[h],
                 "xg%db" % h)
             xk = "xg%da xg%db" % (h, h)
-            pd, bd = (T.p1, "1") if h == 0 else (T.p2, "2")
+            if h and not t:
+                own_items(0)
+            mm(x0[h][0], T.I[:], T.xg[:, 16 * c:16 * c + 1024:16], True, True, xk, "x0%d" % h, x0[h][1])
+            pd, bd = pds[h]
+            for j in range(NS if h == 0 else NB):
+                k, o = 2 * j + 2, pd[:, 64 * j:64 * j + 64]
+                mm(o, T.I[:], T.xg[:, 16 * c + k:16 * c + 1024:16], True, False, xk, "pd%d" % h, bd)
+                mm(o, T.nI[:], T.xg[:, 16 * c:16 * c + 1024:16], False, True, "nI", "pd%d" % h, bd)
             if h == 0:
-                key_start(t)
-                o = T.p6[:, 256:384]
-                mm(T.p7[:, 0:128], T.I[:], z, True, False, zk, "dq", "7")
-                mm(o, T.nI[:], T.mh[:], True, False, "nI mh", "Hr", "6")
-                mm(o, T.nBo8[:], T.m256[:], False, False, "nBo8 m256", "Hr", "6")
-                mm(o, T.W2[:], z, False, False, "W2 " + zk, "Hr", "6")
-            mm(T.p0[:, c:c + 64], T.I[:], T.xg[:, 16 * c:16 * c + 1024:16], True, True, xk, "x0", "0")
-            for j in range(NS):
-                k, pk_ = 2 * j + 2, "pd%d" % h
-                if h == 1 and j == NB:
-                    for kk in range(1, NA + 1):
-                        tt(T.mn[:, kk - 1, 0:64], T.xg[:, 2 * kk - 1:1024:16], T.p5[:, 0:64], A.min, "xg0a xg0b xa0",
-                           "ma%d" % kk, "5")
-                if h == 1 and j >= NB:
-                    pd, bd, pk_ = T.p5, "5", "pd2"
-                mm(pd[:, 64 * j:64 * j + 64], T.I[:], T.xg[:, 16 * c + k:16 * c + 1024:16], True, False, xk, pk_, bd)
-                mm(pd[:, 64 * j:64 * j + 64], T.nI[:], T.xg[:, 16 * c:16 * c + 1024:16], False, True, "nI", pk_, bd)
-            if h == 0:
-                mm(T.p5[:, 0:64], T.I[:], T.xg[:, 0:1024:16], True, True, xk, "xa0", "5")
-                mm(T.p7[:, 0:64], T.nI[:], T.xg[:, 0:1024:16], False, False, xk, "dq", "7")
+                cp(PP, T.Pu[:], "Pa Pb", Pk)
+                send("P", t, PP, T.lP[:, t, :], Pk)
+                if t:
+                    mm(Hr, T.I[:], PP, False, True, Pk, "Hr", "2")
+                else:
+                    cp(T.VX[:, 0, 0:8], T.O[:, 0, 1:16:2], "xi0", "xu0")
         xk = "xg0a xg0b xg1a xg1b"
-        cp(T.PP[:, 0:128], T.Pu[:, t, :], Pk, "PP0")
-        act(T.ad[:, :, 0:64], T.p1[:, 0:64 * NS], F.Abs, "pd0", "ad0", "1")
-        act(T.ad[:, 0:NB, 64:128], T.p2[:, 0:64 * NB], F.Abs, "pd1", "ad1", "2")
-        act(T.ad[:, NB:NS, 64:128], T.p5[:, 64 * NB:64 * NS], F.Abs, "pd2", "ad2", "5")
-        for k in range(1, NV + 1):
-            c = 64 if k <= NA else 0
-            tt(T.mn[:, k - 1, c:128], T.xg[:, 16 * c + 2 * k - 1:2048:16], T.p0[:, c:128], A.min, xk + " x0", "mn%d" % k, "0")
-        if t:
-            cp(T.Z[:, t, :], T.vs[:, 1:32:2], "vs", "v%d x%di" % (t, t))
-        mm(PK[:, 1:4, 1:128:2], T.xg[:, 0:2048:16], T.R0[:], False, False, xk + " R0", "K", "3")
+        for h in range(2):
+            c, hk = 64 * h, "xg%da xg%db x0%d" % (h, h, h)
+            if h:
+                for j in range(NB, NS):
+                    tt(T.dd[:, j - NB, :], T.xg[:, 1024 + 2 * j + 2:2048:16], x0[1][0], A.subtract, hk, "dd%d" % j, x0[1][1])
+            n = NB if h else NS
+            act(T.ad[:, 0:n, c:c + 64], pds[h][0][:, 0:64 * n], F.Abs, "pd%d" % h, "ad%d" % h, pds[h][1])
+            if h:
+                act(T.ad[:, NB:NS, 64:128], T.dd[:], F.Abs, " ".join("dd%d" % j for j in range(NB, NS)), "ad2")
+            for k in range(1, NV + 1):
+                tt(T.mn[:, k - 1, c:c + 64], T.xg[:, 16 * c + 2 * k - 1:16 * c + 1024:16], x0[h][0], A.min,
+                   hk, "mn%d%d" % (h, k), x0[h][1])
+            if h == 0 and t:
+                wraps()
+        for s in range(1, 4):
+            mm(PK[:, s, 1:128:2], T.xg[:, 0:2048:16], T.RB[:, 0:128:2], False, False, xk, "K", "3")
         for k in range(1, NV + 1):
             mm(PK[:, 1:4, 2 * k - 1:128:16], T.xg[:, 2 * k - 1:2048:16], T.R16[:], False, False, "R16", "K", "3")
+        if not t:
+            own_sums()
+            mm(Hr, T.I[:], PP, False, True, Pk, "Hr", "2")
+            wraps()
+            late_constants()
         for k in range(1, NV + 1):
-            mm(PK[:, 1:4, 2 * k - 1:128:16], T.mn[:, k - 1, :], T.R32[:], False, False, "mn%d ma%d R32" % (k, k), "K", "3")
-            if k == NV - 2:
-                for j in range(NB):
-                    mm(PK[:, 1:4, 2 * j + 2:128:16], T.ad[:, j, :], T.R16[:], False, False, "ad0 ad1", "K", "3")
-        for j in range(NB, NS):
-            mm(PK[:, 1:4, 2 * j + 2:128:16], T.ad[:, j, :], T.R16[:], False, j == NS - 1, "ad0 ad2", "K", "3")
-        ts(T.v2[:], T.Z[:, t, 0:8], 2.0, None, A.mult, r="v%d" % t, w="v2")
-        cp(T.dv[:, 17:32:2], T.Z[:, t, 8:16], "x%di" % t, "dv2")
+            mm(PK[:, 1:4, 2 * k - 1:128:16], T.mn[:, k - 1, :], T.R32[:], False, k == NV, "mn0%d mn1%d R32" % (k, k), "K", "3")
+            if k in (4, NV - 1):
+                for j in (range(NB) if k == 4 else range(NB, NS)):
+                    mm(PK[:, 1:4, 2 * j + 2:128:16], T.ad[:, j, :], T.R16[:], False, False,
+                       "ad0 ad1" if k == 4 else "ad2", "K", "3")
+        ts(T.h2[:, 0:8], T.v2[:], 1023, None, A.bitwise_and, r="v2", w="h2a")
+        if t:
+            ts(T.nn[:], T.hy[:], -8390656.0, None, A.add, r="hy", w="nn")
+        tt(T.hM[:], T.h2[:, 0:8].indirect(T.oc[:]), T.Dg[:], A.mult, "h2a oc Dg", "hM")
 
-        def item_sum():
-            act(T.xo[:], T.X[:].indirect(xu), F.Copy, "X " + xuk, "xo")
-            mm(T.p1[:, 0:128], T.I[:], z, True, False, zk, "xq", "1")
-            mm(T.p1[:, 0:128], T.I[:], T.xo[:], False, True, "xo", "xq", "1")
-
-        def item_wrap():
-            act(T.xs[:], T.p1[:, 0:128], F.Sign, "xq", "xs", "1", bias=-255.5)
-            mm(T.p1[:, 0:128], T.I[:], z, True, False, zk, "xq", "1")
-            mm(T.p1[:, 0:128], T.I[:], T.xo[:], False, False, "xo", "xq", "1")
-            mm(T.p1[:, 0:128], T.IX[:], T.xs[:], False, True, "IX xs", "xq", "1")
-
-        mm(T.p7[:, 64:128], T.nI[:], T.xg[:, 1024:2048:16], False, True, xk, "dq", "7")
-        mm(T.p6[:, 256:384], T.I16[:], T.PP[:, 0:128], False, True, "I16 PP0", "Hr", "6")
-        item_sum()
-        act(T.aq[:], T.p7[:, 0:128], F.Abs, "dq", "aq", "7")
+        mm(dq, T.nI[:], T.xg[:, 0:2048:16], False, False, xk, "al", "7")
+        mm(xr, T.IX[:], T.xs[:], False, False, "IX xs", "al", "7")
+        mm(zs, T.I[:], T.lZ[:, t, :], False, True, "lZ%d" % t, "al", "7")
+        act(T.aq[:], dq, F.Abs, "al", "aq", "7")
+        act(T.av1[:], zs, F.Identity, "al", "av1", "7", bias=MAGIC, scale=0.5)
+        act(T.xn[:], xr, F.Identity, "al", "xn", "7", bias=-128.0)
+        mm(E1, T.W2[:], z, True, False, "", "Hr E1", "2")
+        mm(E2, T.W2[:], z, False, False, "", "E2", "2")
+        mm(E2, T.I[:], PP, False, False, "", "E2", "2")
         for s in range(4, 8):
             mm(blk(s, s + 1), T.aq[:], T.RB[:, 0:128], False, s == 7, "aq", "KQ", "4")
-        act(T.hy[:], T.p6[:, 256:384], F.Identity, "Hr", "hy", "6", bias=8388607.5, scale=1.0 / 2048)
-        item_wrap()
-        mm(T.p0[:, 384:512], T.I[:], z, True, False, zk, "zs", "0")
-        mm(T.p0[:, 384:512], T.I[:], T.mh[:], False, False, "mh", "zs", "0")
-        mm(T.p0[:, 384:512], T.I[:], T.lZ[:, t, :], False, True, "lZ%d" % t, "zs", "0")
-        E1, E2 = T.p2[:, 128:256], T.p2[:, 256:384]
-        mm(E1, T.W2[:], z, True, False, "", "E1", "2")
-        mm(E2, T.W2[:], z, False, False, "", "E2", "2")
-        mm(E2, T.I16[:], T.PP[:, 0:128], False, False, "", "E2", "2")
 
         for j in range(6):
             for h in range(2):
                 c = 160 * j + 80 * h + 16
-                d1 = T.m256[:, 0:64] if j == 0 else T.SB[:, c - 161:c - 97]
-                op("V", lambda q: q.tensor_tensor_scan(T.SB[:, c:c + 64], PK[:, 1, 64 * h:64 * h + 64], d1, 0.0, A.max,
-                                                       A.min if j else A.max),
-                   "K " + ("m256" if j == 0 else "s%d%d" % (j - 1, h)), "s%d%d" % (j, h), "3")
-            if j < 2:
-                ts(T.h2[:, 8 * j:8 * j + 8], T.v2[:], 1023, None, A.bitwise_and, r="v2", w="h2" + "ab"[j])
+                d1 = T.top[:] if j == 0 else T.SB[:, c - 161:c - 97]
+                scan(T.SB[:, c:c + 64], PK[:, 1, 64 * h:64 * h + 64], d1, 0.0, A.max, A.min,
+                     "K " + ("top" if j == 0 else "s%d%d" % (j - 1, h)), "s%d%d" % (j, h), "3")
+            if j == 0:
+                ts(T.h2[:, 8:16], T.v2[:], 1023, None, A.bitwise_and, r="v2", w="h2b")
+            if j == 1 and not t:
+                ts(T.nn[:], T.hy[:], -8390656.0, None, A.add, r="hy", w="nn")
+        mm(E1, T.IQ[:], T.nn[:], False, False, "IQ nn", "E1", "2")
+        mm(E2, T.IQ[:], T.nn[:], False, False, "", "E2", "2")
 
         def before_e(gs):
             for gi in gs:
@@ -389,13 +412,14 @@ def rank_program(g, core, T, topo):
                 act(T.nc[:, 16 + 16 * gi:32 + 16 * gi], T.SB[:, c:c + 16], F.Sign, "s0%d nc" % (gi // 4), "nc%d" % gi,
                     scale=-1.0, bias=T.SB[:, c + 15:c + 16])
 
-        act(T.nn[:], T.hy[:], F.Identity, "hy", "nn", bias=2048.0 * 8388624, scale=-2048.0)
-        before_e(range(3))
-        act(T.xn[:], T.p1[:, 0:128], F.Identity, "xq", "xn", "1", bias=-128.0)
-        act(T.av1[:], T.p0[:, 384:512], F.Identity, "zs", "av1", "0", bias=MAGIC, scale=0.5)
-        before_e(range(3, 8 - NE))
-        mm(E1, T.I32[:], T.nn[:], False, False, "I32 nn", "E1", "2")
-        mm(E2, T.I32[:], T.nn[:], False, False, "", "E2", "2")
+        nk = " ".join("nc%d" % gi for gi in range(8))
+        mid, amb, Xs, sT, Kb = T.p5[:, 0:128], T.p6[:, 0:160], T.p0[:, 128:256], T.p1[:, 384:512], PK[:, 0, :]
+        act(T.av[:], T.av1[:], F.Identity, "av1", "av", bias=-MAGIC)
+        before_e(range(8))
+        mm(T.p7[:, 256:384], T.I[:], T.M2[:], True, False, "", "al ub", "7")
+        mm(T.p7[:, 256:384], T.av[:], T.Wu[:], False, True, "av", "ub", "7")
+        mm(sT, T.nc[:, 16:144], T.I[:], True, False, nk, "sT", "1")
+        mm(sT, T.nc[:, 15:143], T.nI[:], False, True, "", "sT", "1")
         for gi in range(8):
             c = 816 + 16 * gi + 16 * (gi // 4) + 15
             ts(T.FL[:, :, 16 * gi:16 * gi + 16], PK[:, 2:4, 16 * gi:16 * gi + 16], T.SB[:, c:c + 1], None, A.is_le,
@@ -404,97 +428,85 @@ def rank_program(g, core, T, topo):
                 scale=-1.0, bias=T.SB[:, c:c + 1])
         fl = " ".join("F%d" % gi for gi in range(8))
         fq = " ".join("G%d" % gi for gi in range(8))
-        nk = " ".join("nc%d" % gi for gi in range(8))
-        mm(T.p5[:, 0:128], T.FL[:, 1, :], T.I[:], True, False, fl, "mid", "5")
-        mm(T.p5[:, 0:128], T.FL[:, 0, :], T.nI[:], False, True, "", "mid", "5")
-        mm(T.p7[:, 128:144], T.I[:], T.cl[:], True, False, "cl", "nL", "7")
-        mm(T.p7[:, 128:144], T.FQ[:, 2, :], T.R1[:, 129:160:2], False, True, fq + " R1b", "nL", "7")
-        mm(T.p6[:, 0:160], T.FQ[:, 1, :], T.R1[:], True, False, "R1a R1b", "amb", "6")
-        mm(T.p6[:, 0:160], T.FQ[:, 0, :], T.nR1[:], False, True, "nR1a nR1b", "amb", "6")
-        act(T.av[:], T.av1[:], F.Identity, "av1", "av", bias=-MAGIC)
-        before_e(range(8 - NE, 8))
-        mm(T.p0[:, 128:256], T.FL[:, 0, :], T.I[:], True, False, "", "Xs", "0")
-        mm(T.p0[:, 128:256], T.FL[:, 1, :], T.I[:], False, False, "", "Xs", "0")
-        mm(T.p0[:, 128:256], T.FQ[:, 3, :], T.I[:], False, True, "", "Xs", "0")
-        mm(T.p1[:, 256:384], T.I[:], T.M2[:], True, False, "", "ub", "1")
-        mm(T.p1[:, 256:384], T.av[:], T.Wu[:], False, True, "av", "ub", "1")
-        mm(T.p1[:, 384:512], T.nc[:, 16:144], T.I[:], True, False, nk, "sT", "1")
-        mm(T.p1[:, 384:512], T.nc[:, 15:143], T.nI[:], False, True, "", "sT", "1")
+        act(T.uM[:], T.p7[:, 256:384], F.Relu, "ub", "uM", "7")
+        mm(mid, T.FL[:, 1, :], T.I[:], True, False, fl, "mid", "5")
+        mm(mid, T.FL[:, 0, :], T.nI[:], False, True, "", "mid", "5")
+        act(T.sg[:], sT, F.Copy, "sT", "sg", "1")
+        mm(Xs, T.FL[:, 0, :], T.I[:], True, False, "", "Xs", "0")
+        mm(Xs, T.FL[:, 1, :], T.I[:], False, False, "", "Xs", "0")
+        mm(Xs, T.FQ[:, 3, :], T.I[:], False, True, fq, "Xs", "0")
+        mm(amb, T.FQ[:, 1, :], T.R1[:], True, False, "R1a R1b", "amb", "6")
+        mm(amb, T.FQ[:, 0, :], T.nR1[:], False, True, "nR1a nR1b", "amb", "6")
+        mm(nL, T.I[:], T.cl[:, int(last), :], True, False, "cl0 cl1 cm0 cm1", "nL", "1")
+        mm(nL, T.FQ[:, 2, :], T.R1[:, 129:160:2], False, True, "", "nL", "1")
+        mm(Kb, T.I[:], T.jb[:], True, False, "jb", "Kb", "3")
+        mm(Kb, T.FQ[:, 3, :], T.IX[:], False, False, "", "Kb", "3")
+        mm(Kb, T.BoK[:], T.hM[:], False, True, "BoK hM", "Kb", "3")
+        mm(E2, T.nI[:], T.lP[:, t, :], False, True, "lP%d" % t, "E1 E2", "2")
+        u_list(not last)
         cp(T.X[:].indirect(xu), T.xn[:], xuk + " xn", "X")
-        act(T.sM[:, t, :], T.p5[:, 0:128], F.Copy, "mid", "sM%d" % t, "5")
-        act(T.sA[:, t, :], T.p6[:, 0:160], F.Copy, "amb", "sA%d" % t, "6")
-        ea, ec, _ = masks(core, da, dc)
-        op("G", lambda q: q.remote_dma(T.lM[:, t, :], T.sM[:, t, :], T.sem["aM%d" % t], T.sem.sent, ida[1], ida[0], bits(ea)),
-           "sM%d" % t, sem=False)
-        op("G", lambda q: q.remote_dma(T.lA[:, t, :], T.sA[:, t, :], T.sem["aA%d" % t], T.sem.sent, idc[1], idc[0], bits(ec)),
-           "sA%d" % t, sem=False)
-        sent[0] += len(ea) + len(ec)
+        if not t:
+            bag_copy(0)
+        act(T.sM[:, t, :], mid, F.Copy, "mid", "sM%d" % t, "5")
+        act(T.xa[:], Xs, F.Abs, "Xs", "xa", "0", bias=-1.0)
+        act(T.sA[:, t, :], amb, F.Copy, "amb", "sA%d" % t, "6")
+        send("M", t, T.sM[:, t, :], T.lM[:, t, :], "sM%d" % t)
+        send("A", t, T.sA[:, t, :], T.lA[:, t, :], "sA%d" % t)
 
-        tt(T.w1[:], T.h2[:], T.p7[:, 128:144], A.subtract, "h2a h2b nL", "w1", "7")
-        cp(T.PP[:, 128:256], T.lP[:, t, :], "lP%d" % t, "PP1")
-        tt(T.wM[:], T.w1[:, 0:8].indirect(T.oc[:]), T.Dg[:], A.mult, "w1 oc Dg", "wM")
-        ts(T.wi[:], T.w1[:, 0:8], -6.0, None, A.add, r="w1", w="wi")
-        ts(T.bc[:], T.w1[:], -128.0, -127.5, A.mult, A.add, "w1", "bc")
-        mm(E2, T.nI16[:], T.PP[:, 128:256], False, True, "nI16 PP1", "E2 E2c", "2")
-        mm(blk(7, 8), T.I[:], T.jb[:], True, False, "jb", "Kv KQ", "4")
-        mm(T.p6[:, 384:512], T.I[:], T.jb[:], True, False, "jb", "Kb", "6")
-        mm(T.p6[:, 384:512], T.BoK[:], T.wM[:], False, True, "BoK wM", "Kb", "6")
-        mm(blk(7, 8), T.BoK[:], T.wM[:], False, True, "BoK wM", "Kv", "4")
-        act(T.xa[:], T.p0[:, 128:256], F.Abs, "Xs", "xa", "0", bias=-1.0)
+        tt(O[:, 17:48:2], T.h2[:], nL, A.subtract, "h2a h2b nL", ck + " bc", "1")
+        if not t:
+            bag_copy(1)
         act(T.ns[:], T.xa[:], F.Sign, "xa", "ns", scale=-1.0, bias=2.0)
-        act(T.uM[:], T.p1[:, 256:384], F.Relu, "ub", "uM", "1")
-        act(T.sg[:], T.p1[:, 384:512], F.Copy, "sT", "sg", "1")
-        mm(T.p7[:, 144:152], T.uM[:], T.sel32[:], True, True, "uM sel32", "uL", "7")
-
-        def counts(cs):
-            for c in cs:
-                for j in range(2):
-                    n = 8 * j + c
-                    act(T.junk[:, n, 16 * c:128], T.p6[:, 384 + 16 * c:512], F.Sign, "Kb bc", "cnt%d" % n, "6",
-                        bias=T.bc[:, n:n + 1], accum_out=T.cnt[:, n:n + 1])
-
-        counts(range(CV))
-        ts(T.Z[:, t, 0:8], T.wi[:], 1023, None, A.bitwise_and, r="wi", w="v%d" % t)
-        tt(E1, E1, T.ns[:], A.mult, "E1 E2c ns", "E1", "2")
+        for c in range(8):
+            act(T.kd[:, KD[c]:KD[c + 1]], Kb[:, 16 * c:128], F.Abs, "Kb bc", "kd%d" % c, "3",
+                scale=-1.0 / 256, bias=O[:, 33 + 2 * c:34 + 2 * c])
+        base, sd, S = T.p1[:, 128:256], T.p0[:, 256:384], T.p5[:, 0:128]
+        mm(base, T.I[:], PP, True, False, "", "base", "1")
+        cp(T.ui[:], uL, "uL", "ui", "7")
+        tt(T.be[:], E1, T.ns[:], A.mult, "E1 ns", "be", "2")
         tt(E2, E2, T.ns[:], A.mult, "E2 ns", "E2", "2")
-        ts(T.dw[:, 1:16:2], T.Z[:, t, 0:8], 1.0 / 1024, None, A.mult, r="v%d" % t, w="dw1")
-        cp(T.dv[:, 1:16:2], T.Z[:, t, 0:8], "v%d" % t, "dv1")
-        for c in range(CV, 8):
-            ts(T.kd[:, c - CV, 16 * c:128], PK[:, 7, 16 * c:128], T.bc[:, 8 + c:9 + c], 4.0, A.add, A.mult,
-               "Kv bc", "kd%d" % c, "4")
-        tt(E1, E1, T.PP[:, 0:128], A.add, "E1 PP0", "E1", "2")
-        cp(T.ui[:], T.p7[:, 144:152], "uL", "ui", "7")
-        for c in range(CV, 8):
-            op("V", lambda q: q.tensor_reduce(T.cnt[:, 8 + c:9 + c], T.kd[:, c - CV, 16 * c:128], X1, A.min,
-                                              apply_absolute_value=True), "kd%d" % c, "cnt%d" % (8 + c))
-        tt(T.sbf[:], E1, T.sg[:], A.mult, "E1 sg", "sbf", "2")
-        ts(T.u15[:], T.ui[:], 15, None, A.bitwise_and, r="ui", w="u15")
-        tt(T.dw[:, 2 * CV:16:2], T.cnt[:, CV:8], T.cnt[:, 8 + CV:16], A.subtract,
-           "cntc " + " ".join("cnt%d" % n for n in range(8 + CV, 16)), "dw2")
-        ck = " ".join("cnt%d" % n for n in range(CV)) + " " + " ".join("cnt%d" % n for n in range(8, 8 + CV))
-        tt(T.dw[:, 0:2 * CV:2], T.cnt[:, 8:8 + CV], T.cnt[:, 0:CV], A.subtract, ck, "dw0")
-        ts(T.un[:, 0:8], T.ui[:], 1023, None, A.bitwise_and, r="ui", w="un0")
-        tt(T.un[:, 8:16], T.u15[:], T.l16[:], A.add, "u15 l16", "un1")
-        tt(T.p0[:, 256:384], E2, T.sg[:], A.mult, "E2 sg", "sd", "20")
-        op("V", lambda q: q.tensor_tensor_scan(T.ds[:], T.cap[:], T.dw[:], 0.0, A.min, A.max), "cap dw0 dw1 dw2", "ds")
+        mm(base, T.I[:], T.be[:], False, True, "be", "base", "1")
+        mm(T.p7[:, 256:384], T.I[:], z, True, False, zk, "zq", "7")
+        mm(T.p7[:, 384:512], T.I[:], T.av[:], False, False, "av", "zq", "7")
+        mm(T.p7[:, 384:512], T.I[:], T.m256[:], False, False, "m256", "zq", "7")
+
+        def least(a, b):
+            scan(T.km[:, KD[a]:KD[b]], T.rs[:, KD[a]:KD[b]], T.kd[:, KD[a]:KD[b]], 0.0, A.max, A.min,
+                 rsk + " " + " ".join("kd%d" % c for c in range(a, b)), "km%d" % a)
+
+        least(0, 4)
+        tt(sd, E2, T.sg[:], A.mult, "E2 sg", "sd", "20")
+        least(4, 8)
+        tt(T.sbf[:], base, T.sg[:], A.mult, "base sg", "sbf", "1")
+        ts(O[:, 16:48:2], T.km[:].indirect(T.ke[:, 0:1]), -1048576.0, 260096.0, A.mult, A.add, "km0 km4 ke", "lose")
+        ts(T.u15[:], T.ui[:, 0:8], 15, None, A.bitwise_and, r="ui", w="u15")
+        ts(T.un[:, 8:16], T.ui[:, 8:16], 1023, None, A.bitwise_and, r="ui", w="un0")
         if last:
             lands("allsent", "sent", sent[0])
             dma("Y", T.yx[:], T.X[:], "X allsent", "", "o1")
         else:
             query_start(t + 1)
-        mm(T.p5[:, 0:128], T.nBo16[:], T.sbf[:], True, False, "nBo16 sbf", "S", "5")
-        mm(T.p7[:, 256:384], T.I[:], z, True, False, zk, "zq", "7")
-        mm(T.p7[:, 384:512], T.I[:], T.av[:], False, False, "av", "zq", "7")
-        mm(T.p7[:, 384:512], T.I[:], T.m256[:], False, False, "m256", "zq", "7")
+        mm(S, T.nBo[:], T.sbf[:], True, False, "nBo sbf", "S", "5")
+        scan(T.ds[:], T.cap[:], O[:, 16:32], 0.0, A.min, A.max, "cap lose " + ck, "ds")
+        tt(T.un[:, 0:8], T.u15[:], T.l16[:], A.add, "u15 l16", "un1")
+        if not t:
+            bag_copy(2)
+        if last:
+            ts(T.wl[:], O[:, 17:32:2], 1023.5, None, A.is_lt, r=ck, w="wl")
 
         lm, la = "lM%d" % t, "lA%d" % t
-        tt(T.tp[:], T.lM[:, t, :], T.p0[:, 256:384], A.mult, lm + " sd", "tp", "0")
-        mm(T.p5[:, 0:128], T.Bo16[:], T.tp[:], False, True, "Bo16 tp", "S", "5")
+        tt(T.tp[:], T.lM[:, t, :], sd, A.mult, lm + " sd", "tp", "0")
+        mm(S, T.Bo[:], T.tp[:], False, True, "tp", "S", "5")
         tt(T.y1[:], T.lM[:, t, :], E2, A.mult, lm + " E2", "y1", "2")
-        tt(T.dv[:, 0:32:2], T.un[:], T.Z[:, t, :], A.subtract, "un0 un1 v%d x%di" % (t, t), "dv")
-        ts(T.wu[:], T.ds[:, 1:16:2], 1024.0, None, A.mult, r="ds", w="wu")
-        tt(T.y2[:], E1, T.y1[:], A.subtract, "y1 E1", "y2", "2")
-        tt(T.rr[:], T.p5[:, 0:128], T.sg[:], A.mult, "S sg", "rr", "5")
+        ts(T.wu[:], T.ds[:, 1:16:2], -1.0 if last else 0.0, None, A.add, r="ds", w="wu")
+        if last:
+            tt(O[:, 17:32:2], O[:, 17:32:2], T.wl[:], A.mult, "wl", ck)
+        else:
+            tt(O[:, 0:32:2], T.un[:], O[:, 1:32:2], A.subtract, "un0 un1 %s %s" % (xik, ck), "lose")
+        tt(T.y2[:], base, T.y1[:], A.subtract, "y1 base", "y2", "1")
+        tt(T.rr[:], S, T.sg[:], A.mult, "S sg", "rr", "5")
+        if last:
+            tt(O[:, 0:32:2], T.un[:], O[:, 1:32:2], A.subtract, "un0 un1 %s %s" % (xik, ck), "lose")
         mm(T.p7[:, 256:384], T.nBo8[:], T.lA[:, t, 0:128], False, False, "nBo8 " + la, "zq", "7")
         mm(T.p7[:, 384:512], T.Bo8[:], T.lA[:, t, 0:128], False, True, "Bo8", "zq", "7")
         act(T.zr[:], T.p7[:, 256:512], F.Relu, "zq", "zr", "7")
@@ -504,27 +516,33 @@ def rank_program(g, core, T, topo):
             act(T.zb[:, t + 1, :], T.p6[:, 0:128], F.Copy, "zn", "z%d" % (t + 1), "6")
 
         def pick():
-            op("V", lambda q: q.tensor_tensor_scan(T.vs[:], T.lA[:, t, 128:160], T.dv[:], 0.0, A.mult, A.add),
-               la + " dv dv1 dv2", "vs")
+            scan(T.O[:, t + 1, 0:32], T.lA[:, t, 128:160], O[:, 0:32], 0.0, A.mult, A.add,
+                 "%s lose %s %s" % (la, xik, ck), "xi%d c%d" % (t + 1, t + 1))
 
         if not last:
             pick()
-        tt(T.B[:].indirect(T.wu[:]), T.y2[:], T.rr[:], A.add, "wu y2 rr", "B")
+        tt(W.indirect(T.wu[:]), T.y2[:], T.rr[:], A.add, "wu y2 rr", "B Bz B0 B1 B2")
         if not last:
-            cp(T.VX[:, t + 1, :], T.vs[:, 1:32:2], "vs", "vu%d xu%d" % (t + 1, t + 1))
+            send("Z", t + 1, T.zb[:, t + 1, :], T.lZ[:, t + 1, :], "z%d" % (t + 1))
+            cp(T.VX[:, t + 1, :], T.O[:, t + 1, 1:32:2], "c%d" % (t + 1), "vu%d xu%d" % (t + 1, t + 1))
+            step_start(t + 1)
+            own_items(t + 1)
+            own_sums()
+            ts(T.v2[:], T.O[:, t + 1, 17:32:2], 2.0, 2.0, A.mult, A.add, "c%d" % (t + 1), "v2")
             for h in range(2):
-                cp(T.Pu[:, t + 1, 64 * h:64 * h + 64], T.B[:, 0:1024].indirect(T.VX[:, t + 1, 4 * h:4 * h + 4]),
-                   "B vu%d" % (t + 1), "P%d%s" % (t + 1, "ab"[h]))
+                cp(T.Pu[:, 64 * h:64 * h + 64], W[:, 0:1024].indirect(T.VX[:, t + 1, 8 + 4 * h:12 + 4 * h]),
+                   "B vu%d" % (t + 1), "P" + "ab"[h])
     pick()
-    cp(T.vf[:], T.vs[:, 1:16:2], "vs", "vf")
+    cp(T.zb[:, RO, :], T.p6[:, 0:128], "zn", "z%d" % RO, "6")
+    cp(T.vf[:], T.O[:, RO, 17:32:2], "c%d" % RO, "vf")
+    cp(T.B[:, B0:B0 + 1], T.B[:, B0 + 1024:B0 + 1025], "B", "Bz")
+    dma("Y", T.yz[:], T.zb[:, RO, :], "z%d" % RO, "", "o2")
     dma("Y", T.yv[:], T.vf[:], "vf", "", "o5")
-    for h, (pb, bk) in enumerate(((T.p1, "1"), (T.p2, "2"), (T.p5, "5"), (T.p0, "0"))):
+    for h, (pb, bk) in zip((3, 2, 1, 0), ((T.p1, "1"), (T.p2, "2"), (T.p5, "5"), (T.p0, "0"))):
         c = 128 * h
-        act(pb[:, 0:128], T.B[:, 512 + c:640 + c], F.Identity, "B", "hi%d" % h, bk, scale=2048.0)
-        tt(T.yo[:, c:c + 128], T.B[:, c:c + 128], pb[:, 0:128], A.add, "B hi%d" % h, "yo%d" % h, bk)
-    dma("Y", T.yb[:, 0:256], T.yo[:, 0:256], "yo0 yo1", "", "o3")
-    act(T.zb[:, RO, :], T.p6[:, 0:128], F.Copy, "zn", "z%d" % RO, "6")
-    dma("S", T.yz[:], T.zb[:, RO, :], "z%d" % RO, "", "o2")
+        act(pb[:, 0:128], T.B[:, B0 + 512 + c:B0 + 640 + c], F.Identity, "B", "hi%d" % h, bk, scale=2048.0)
+        tt(T.yo[:, c:c + 128], T.B[:, B0 + c:B0 + c + 128], pb[:, 0:128], A.add, "B Bz hi%d" % h, "yo%d" % h, bk)
     dma("Y", T.yb[:, 256:512], T.yo[:, 256:512], "yo2 yo3", "", "o4")
+    dma("S", T.yb[:, 0:256], T.yo[:, 0:256], "yo0 yo1", "", "o3")
     for s, v in count.items():
         wait("G", (s, v))

@@ -1,14 +1,14 @@
-from concourse.bass import DstId, RemoteDMATransfer
 from concourse.mybir import AluOpType as A, ActivationFunctionType as F
 
 RO, HN, HZ = 4, [1, 2, 3, 1], [3, 1, 2, 2]
 NV = 8
 NS = 15 - NV
-NB = 4
-NE = 4
+NB = 2
+ND = 2
+KA = (0, 2, 6)
 GVS = (32, 32)
-BP = (0, 448, 864, 1024)
-MAGIC = 12582912.0
+BP = (0, 256, 512, 704)
+YP = (512, 448, 384, 256, 128, 0)
 B0 = 7
 KD = [128 * c - 8 * c * (c - 1) for c in range(9)]
 f32, bf, f16, i32, u16 = "float32", "bfloat16", "float16", "int32", "uint16"
@@ -20,30 +20,27 @@ def _sb(n, d):
 
 SCRATCH = {
     "X": _sb(2048, bf), "Bi": _sb(1024, i32), "B": _sb(1168, f32), "xg": _sb(2048, bf),
-    "Z": _sb(8, i32), "VX": _sb([4, 16], u16), "vf": _sb(8, f32), "O": _sb([5, 48], f32),
+    "Z": _sb(8, i32), "VX": _sb([4, 16], u16), "vf": _sb(8, f32), "O": _sb([5, 80], f32),
     "uwi": _sb(4, i32), "bti": _sb(4, i32), "zb": _sb([5, 128], bf),
-    "Pu": _sb(128, u16), "PP": _sb([4, 128], f16), "lP": _sb([4, 128], f16), "lZ": _sb([4, 128], bf), "lM": _sb([4, 128], bf),
-    "lA": _sb([4, 160], bf), "sM": _sb([4, 128], bf), "sA": _sb([4, 160], bf), "one": _sb(128, bf),
-    "v2": _sb(8, i32), "h2": _sb(16, i32), "hM": _sb(128, f16),
+    "Pu": _sb(128, u16), "PP": _sb([4, 128], f16), "lP": _sb([4, 128], f16), "lZ": _sb([4, 128], bf),
+    "lM": _sb([4, 128], bf), "sM": _sb([4, 128], bf), "lA": _sb([4, 160], bf), "sA": _sb([4, 160], bf), "sB": _sb(128, f16),
+    "v2": _sb(8, i32), "h2": _sb(24, i32), "hM": _sb(128, f16),
     "mn": _sb([NV, 128], bf), "ad": _sb([NS, 128], bf), "dd": _sb([NS - NB, 64], bf), "aq": _sb(128, bf), "SB": _sb(960, f32),
     "FL": _sb([2, 128], bf), "FQ": _sb([4, 128], bf), "hy": _sb(128, f32), "nn": _sb(128, f16),
     "kd": _sb(576, bf), "km": _sb(576, bf), "rs": _sb(576, bf), "ds": _sb(16, f32), "wu": _sb(8, u16), "wl": _sb(8, f32),
-    "nc": _sb(144, bf), "xa": _sb(128, bf), "ns": _sb(128, f32), "be": _sb(128, f16),
-    "sg": _sb(128, f32), "av1": _sb(128, f32), "av": _sb(128, bf), "uM": _sb(128, f32), "ui": _sb(16, i32),
-    "u15": _sb(8, i32), "un": _sb(16, i32),
-    "xo": _sb(128, bf), "xs": _sb(128, bf), "xn": _sb(128, bf), "sbf": _sb(128, f16),
+    "nc": _sb(144, bf), "xa": _sb(128, bf), "ns": _sb(128, bf),
+    "sg": _sb(128, f32), "av1": _sb(128, f16), "av": _sb(128, bf), "uM": _sb(128, f32), "ui": _sb(16, i32),
+    "u15": _sb(8, i32), "un": _sb(16, i32), "xs": _sb(128, i32), "xn": _sb(128, i32), "sbf": _sb(128, f16),
     "tp": _sb(128, f16), "y1": _sb(128, f32), "y2": _sb(128, f32), "rr": _sb(128, f32), "zr": _sb(256, bf),
     "yo": _sb(512, f32),
     "pi": _sb(4, i32), "pc": _sb(4, i32), "pf": _sb(8, f32), "jb": _sb(128, bf), "gb": _sb(128, bf), "j24": _sb(24, bf),
-    "ci": _sb(8, f32), "tA": _sb(128, i32), "tC": _sb(128, i32), "ok": _sb(128, bf),
-    "I": _sb(128, bf), "nI": _sb(128, bf), "IQ": _sb(128, bf),
-    "IX": _sb(128, bf), "Bo": _sb(128, bf), "RB": _sb(256, bf), "Bo8": _sb(128, bf), "nBo8": _sb(128, bf),
-    "BoK": _sb(128, bf), "nBo": _sb(128, bf), "Dg": _sb(128, bf), "top": _sb(64, f32),
-    "hc": _sb(128, bf), "M2": _sb(128, bf), "CS": _sb(256, bf), "CQ": _sb(512, bf), "sel": _sb(24, bf),
-    "R16": _sb(24, bf), "R32": _sb(24, bf), "R1": _sb(160, bf), "nR1": _sb(160, bf), "sel32": _sb(16, f32),
-    "m256": _sb(128, bf), "mh": _sb(128, bf), "btf": _sb(4, f32), "btB": _sb([4, 128], bf),
-    "W2": _sb(128, f16), "Wu": _sb(128, f16), "uwf": _sb(4, f32),
-    "oc": _sb(8, u16), "ke": _sb(2, u16), "l16": _sb(8, f32), "cl": _sb([2, 16], f16), "cu": _sb(16, f16), "cap": _sb(16, f32),
+    "ci": _sb(8, f32), "tA": _sb(128, i32), "tC": _sb(128, i32), "ok": _sb(128, bf), "kb": _sb(128, bf), "one": _sb(128, bf),
+    "I": _sb(128, bf), "nI": _sb(128, bf), "IQ": _sb(128, bf), "IX": _sb(128, bf), "Bo": _sb(128, bf), "RB": _sb(256, bf),
+    "Bo8": _sb(128, bf), "nBo8": _sb(128, bf), "BoK": _sb(128, bf), "nBo": _sb(128, bf), "Dg": _sb(128, bf),
+    "top": _sb(64, f32), "to3": _sb(64, f32), "cut": _sb([2, 64], f32), "hc": _sb(128, bf), "M2": _sb(128, bf), "CQ": _sb(512, bf), "sel": _sb(24, bf),
+    "R16": _sb(24, bf), "R32": _sb(24, bf), "Rh": _sb(24, bf), "R1": _sb(160, bf), "nR1": _sb(160, bf), "sel32": _sb(16, f32),
+    "bth": _sb(4, f32), "W2": _sb(128, f16), "Wu": _sb(128, f16), "uwf": _sb(4, f32),
+    "oc": _sb(8, u16), "ke": _sb(2, u16), "l16": _sb(8, f32), "cl": _sb([2, 24], f16), "cu": _sb(16, f16), "cap": _sb(16, f32),
     "p0": ("psum", [128, 512], f32), "p1": ("psum", [128, 512], f32), "p2": ("psum", [128, 512], f32),
     "PK": ("psum", [128, 8, 128], f32), "p5": ("psum", [128, 512], f32), "p6": ("psum", [128, 512], f32),
     "p7": ("psum", [128, 512], f32),
@@ -134,11 +131,8 @@ def rank_program(g, core, T, topo):
     def dma(e, out, x, r, w, sem):
         op(e, lambda q: q.dma_start(out, x), r, w, "", sem, 16)
 
-    def iota(out, pat, cm, w, whole=False):
-        if whole:
-            op("G", lambda q: q.iota(out, pat, 0, cm), "", w)
-        else:
-            op("G", lambda q: q.iota(out, pat, 0, cm, allow_small_or_imprecise_dtypes=True), "", w)
+    def iota(out, pat, base, cm, r, w):
+        op("G", lambda q: q.iota(out, pat, base, cm, allow_small_or_imprecise_dtypes=True), r, w)
 
     def masks(r, t):
         src, da, dc = T.cores[r % N], T.cores[(r + HN[t]) % N], T.cores[(r + HZ[t]) % N]
@@ -170,8 +164,7 @@ def rank_program(g, core, T, topo):
     dma("Y", T.X[:], T.xt[:], "", "X", "dX")
 
     PK = T.PK
-    uL, nL, ub = T.p7[:, 144:160], T.p1[:, 0:16], T.p7[:, 256:384]
-    kb = T.CS[:, 0:128]
+    uL, nL, ub = T.p7[:, 144:160], T.p1[:, 0:24], T.p7[:, 256:384]
     pg, pk, pp = T.pf[:, 0:1], T.pf[:, 1:2], T.pf[:, 2:3]
 
     def blk(a, b):
@@ -181,29 +174,34 @@ def rank_program(g, core, T, topo):
         for name, out, c in outs:
             act(out, T[src][:], F.Identity, src, name, scale=c)
 
-    iota(T.pi[:, 0:1], [[0, 1]], 1, "pi", True)
-    iota(T.gb[:], [[1, 8], [0, 16]], 0, "gb")
-    iota(kb, [[0, 8], [1, 16]], 0, "kb")
-    iota(T.jb[:], [[1, 128]], 0, "jb")
-    iota(T.j24[:], [[0, 3], [1, 8]], 0, "j24")
-    iota(T.ci[:], [[16, 8]], 0, "ci")
-    ms(T.mh[:], -0.5, "mh")
+    op("G", lambda q: q.iota(T.pi[:, 0:1], [[0, 1]], 0, 1), "", "pi")
+    iota(T.gb[:], [[1, 8], [0, 16]], 0, 0, "", "gb")
+    iota(T.kb[:], [[0, 8], [1, 16]], 0, 0, "", "kb")
+    iota(T.jb[:], [[1, 128]], 0, 0, "", "jb")
+    iota(T.j24[:], [[0, 3], [1, 8]], 0, 0, "", "j24")
+    iota(T.ci[:], [[16, 8]], 0, 0, "", "ci")
+    ms(T.one[:], 1.0, "one")
     ms(T.top[:], 1048576.0, "top")
-    ms(T.SB[:, 15:960:80], 0.0, " ".join("s%d%d" % (j, h) for j in range(6) for h in range(2)))
+    sk = " ".join("s%d%d" % (j, h) for j in range(6) for h in range(2))
+    ms(T.SB[:, 15:480:80], 0.0, sk)
+    ms(T.to3[:], 1048576.0, "to3")
     ms(T.nc[:, 0:16], 0.0, "nc")
     ts(T.pc[:, 0:1], T.pi[:, 0:1], 4, None, A.arith_shift_right, r="pi", w="pc0")
     ts(T.pc[:, 1:2], T.pi[:, 0:1], 15, None, A.bitwise_and, r="pi", w="pc1")
     cp(T.pf[:, 2:3], T.pi[:, 0:1], "pi", "pf2")
     ms(T.cap[:], -1.0, "cap")
     ms(T.top[:, 0:64:16], 0.0, "top")
+    ms(T.SB[:, 560:960:80], 0.0, sk)
+    ms(T.to3[:, 2:64:16], 0.0, "to3")
     ms(T.R1[:, 128:160], 0.0, "R1b")
     cp(T.pf[:, 0:2], T.pc[:, 0:2], "pc0 pc1", "pf0")
     ms(T.nR1[:, 128:160], 0.0, "nR1b")
+    ms(T.cl[:, :, 16:24], 7.0, "cl2")
     ms(T.cl[:, 0, 0:8], 7.0, "cl0")
     ms(T.cl[:, 1, 0:8], 6.0, "cl1")
-    ts(T.ok[:], kb, 2.0, 1.0, A.mult, A.add, "kb", "ok")
+    ts(T.ok[:], T.kb[:], 2.0, 1.0, A.mult, A.add, "kb", "ok")
     ts(T.Bo[:], T.gb[:], pg, None, A.is_equal, r="gb pf0", w="Bo")
-    ts(T.Dg[:], kb, pk, None, A.is_equal, r="kb pf0", w="Dg")
+    ts(T.Dg[:], T.kb[:], pk, None, A.is_equal, r="kb pf0", w="Dg")
     ts(T.pf[:, 3:4], pk, -8.0, 128.0, A.mult, A.add, "pf0", "pf3")
     ts(T.pf[:, 4:5], pk, 1.0, None, A.add, r="pf0", w="pf4")
     tt(T.ok[:], T.ok[:], T.Bo[:], A.mult, "Bo", "ok")
@@ -215,46 +213,44 @@ def rank_program(g, core, T, topo):
     ts(T.tC[:], T.ok[:], T.uwf[:, 0:1], 66560.0, A.mult, A.add, r="ok uwf0", w="tC")
     ts(T.sel[:], T.j24[:], pg, None, A.is_equal, r="j24 pf0", w="sel")
     cp(T.VX[:, 0, 8:16], T.Z[:], "v0", "vu0")
-    cp(T.btf[:], T.bti[:], "bti", "btf")
+    ts(T.pf[:, 7:8], pk, 0.0, 0.5, A.is_equal, A.mult, "pf0", "pf7")
     ts(T.tA[:], T.tC[:], 2047, None, A.bitwise_and, r="tC", w="tA")
     ts(T.l16[:], T.ci[:], pk, 16.0, A.add, A.mult, "ci pf0", "l16")
     ts(T.oc[:], T.ci[:], 0.0625, None, A.mult, r="ci", w="oc")
-    ts(T.v2[:], T.Z[:], 2.0, None, A.mult, r="v0", w="v2")
+    ts(T.bth[:], T.bti[:], T.pf[:, 7:8], None, A.add, r="bti pf7", w="bth")
     ts(T.W2[:], T.tA[:], -1024.0, None, A.add, r="tA", w="W2")
+    ts(T.v2[:], T.Z[:], 2.0, None, A.mult, r="v0", w="v2")
 
-    scaled("mh", ("one", T.one[:], -2.0), ("CQ3", T.CQ[:, 384:512], -31.0), ("m256", T.m256[:], 512.0),
-           ("CS1", T.CS[:, 128:256], -32.0))
-    scaled("Bo", ("RB0", T.RB[:, 0:128], 16.0), ("RB1", T.RB[:, 128:256], -16.0))
+    scaled("one", ("CQ3", T.CQ[:, 384:512], 15.5))
+    scaled("Bo", ("RB0", T.RB[:, 0:128], 16.0), ("RB1", T.RB[:, 128:256], -16.0), ("Bo8", T.Bo8[:], 8.0))
     act(T.M2[:], T.Dg[:], F.Identity, "Dg", "M2", scale=16777216.0, bias=-8388608.0)
-    for s, c in enumerate((15.5, -0.5, 15.5)):
+    for s, c in enumerate((7.5, 7.5, 15.5)):
         act(T.CQ[:, 128 * s:128 * s + 128], T.Dg[:], F.Identity, "Dg", "CQ%d" % s, scale=c - 1048576.0, bias=1048576.0)
     scaled("I", ("nI", T.nI[:], -1.0))
     act(T.hc[:], T.one[:], F.Identity, "one pf5 pf6", "hc", scale=T.pf[:, 5:6], bias=T.pf[:, 6:7])
     act(T.sel32[:], T.sel[:, 0:16], F.Identity, "sel", "sel32")
-
-    def u_list(less):
-        if less:
-            mm(uL, T.I[:], T.cu[:], True, False, "cu0 cu1", "uL", "7")
-        mm(uL, T.uM[:], T.sel32[:], not less, True, "uM sel32", "uL", "7")
-
-    def bands(t):
-        act(T.btB[:, t, :], T.one[:], F.Identity, "one btf", "btB%d" % t, scale=T.btf[:, t:t + 1])
-
     mm(ub, T.I[:], T.M2[:], True, False, "I M2", "ub", "7")
     mm(ub, T.zb[:, 0, :], T.Wu[:], False, True, "z0 Wu", "ub", "7")
     act(T.uM[:], ub, F.Relu, "ub", "uM", "7")
-    u_list(False)
+    mm(uL, T.uM[:], T.sel32[:], True, True, "uM sel32", "uL", "7")
     send("Z", 0, T.zb[:, 0, :], T.lZ[:, 0, :], "z0")
-    bands(0)
-    scaled("sel", ("R16", T.R16[:], 16.0), ("R32", T.R32[:], -32.0))
-    scaled("Bo", ("Bo8", T.Bo8[:], 8.0), ("nBo8", T.nBo8[:], -8.0), ("nBo", T.nBo[:], -1.0))
-    for t in range(1, RO):
-        bands(t)
-    iota(T.rs[:], [[0, KD[8]]], 0, "rs")
+    act(T.sB[:], T.one[:], F.Identity, "one bth", "sB", scale=T.bth[:, 0:1])
+    scaled("sel", ("R16", T.R16[:], 16.0), ("R32", T.R32[:], -32.0), ("Rh", T.Rh[:], 0.5))
+    scaled("Bo", ("nBo8", T.nBo8[:], -8.0), ("nBo", T.nBo[:], -1.0), ("BoK", T.BoK[:], 256.0))
+
+    def late_constants():
+        scaled("I", ("IQ", T.IQ[:], -2048.0), ("IX", T.IX[:], -128.0), ("R1a", T.R1[:, 0:128], 16.0),
+               ("nR1a", T.nR1[:, 0:128], -16.0))
+
+    act(T.R1[:, 129:160:2], T.sel[:, 0:16], F.Identity, "sel", "R1b", scale=0.5)
+    act(T.nR1[:, 129:160:2], T.sel[:, 0:16], F.Identity, "sel", "nR1b", scale=-0.5)
+    act(T.cap[:, 1:16:2], T.l16[:], F.Identity, "l16", "cap", scale=1.0 / 16, bias=1025.0)
+    iota(T.rs[:], [[0, KD[8]]], 0, 0, "", "rs")
     for c in range(8):
-        op("G", lambda q: q.iota(T.rs[:, KD[c]:KD[c] + 1], [[0, 1]], 4096, 0, allow_small_or_imprecise_dtypes=True),
-           "rs", "rs%d" % c)
+        iota(T.rs[:, KD[c]:KD[c] + 1], [[0, 1]], 4096, 0, "rs", "rs%d" % c)
+    rsk = " ".join("rs%d" % c for c in range(8))
     cp(T.Pu[:], T.Bi[:].indirect(T.VX[:, 0, 8:16]), "Bi vu0", "Pa Pb")
+    cp(T.B[:, B0 + BP[3]:B0 + 1024], T.Bi[:, BP[3]:1024], "Bi", "B3")
     cp(T.ui[:, 0:8], uL[:, 0:8], "uL", "ui", "7")
     ts(T.ke[:, 0:1], T.pf[:, 3:4], T.pf[:, 4:5], -1.0, A.mult, A.add, "pf3 pf4", "ke")
     for j in range(2):
@@ -264,56 +260,31 @@ def rank_program(g, core, T, topo):
     ms(T.cu[:, 8:16], 1023.0, "cu1")
     cp(T.B[:, B0 + 1024:B0 + 1025], T.Bi[:, 0:1], "Bi", "Bz")
     tt(T.O[:, 0, 1:16:2], T.u15[:], T.l16[:], A.add, "u15 l16", "xi0")
-    act(T.cap[:, 1:16:2], T.l16[:], F.Identity, "l16", "cap", scale=1.0 / 16, bias=1025.0)
-
-    def late_constants():
-        scaled("I", ("IX", T.IX[:], -128.0), ("IQ", T.IQ[:], -2048.0), ("R1a", T.R1[:, 0:128], 16.0),
-               ("nR1a", T.nR1[:, 0:128], -16.0))
-        scaled("Bo", ("BoK", T.BoK[:], 256.0))
-        act(T.R1[:, 129:160:2], T.sel[:, 0:16], F.Identity, "sel", "R1b", scale=0.5)
-        act(T.nR1[:, 129:160:2], T.sel[:, 0:16], F.Identity, "sel", "nR1b", scale=-0.5)
 
     def bag_copy(j):
         cp(T.B[:, B0 + BP[j]:B0 + BP[j + 1]], T.Bi[:, BP[j]:BP[j + 1]], "Bi", "B%d" % j)
 
-    rsk = " ".join("rs%d" % c for c in range(8))
+    dq, zs = T.p7[:, 0:128], T.p7[:, 384:512]
+    Hr, E1, E2 = T.p2[:, 128:256], T.p2[:, 256:384], T.p2[:, 384:512]
 
-    dq, xr, zs = T.p7[:, 0:128], T.p7[:, 128:256], T.p7[:, 384:512]
-    xq, Hr = T.p2[:, 0:128], T.p2[:, 128:256]
-    E1, E2 = T.p2[:, 256:384], T.p2[:, 384:512]
-
-    def query_start(t):
+    def thresholds():
+        mm(blk(1, 2), T.I[:], T.kb[:], True, False, "I kb", "K mid1", "3")
         mm(blk(4, 8), T.I[:], T.CQ[:], True, False, "CQ0 CQ1 CQ2 CQ3", "KQ", "4")
-        mm(blk(4, 6), T.btB[:, t, :], T.RB[:], False, False, "btB%d RB0 RB1" % t, "KQ", "4")
-        if t:
-            mm(blk(4, 6), T.sA[:, t - 1, 0:128], T.RB[:], False, False, "sA%d" % (t - 1), "KQ", "4")
 
-    def step_start(t):
-        mm(blk(1, 2), T.I[:], kb, True, False, "I kb", "K Kb", "3")
-        mm(blk(2, 4), T.btB[:, t, :], T.RB[:], False, False, "btB%d RB0 RB1" % t, "K", "3")
-        mm(blk(2, 3), T.I[:], T.CS[:, 128:256], False, False, "CS1", "K", "3")
-        if t:
-            mm(blk(2, 4), T.sA[:, t - 1, 0:128], T.RB[:], False, False, "sA%d" % (t - 1), "K", "3")
+    def bands():
+        mm(blk(2, 4), T.sB[:], T.RB[:], False, False, "sB RB0 RB1", "K", "3")
+        mm(blk(4, 6), T.sB[:], T.RB[:], False, False, "", "KQ", "4")
+
+    def query_sums(t):
         z, zk = T.zb[:, t, :], "z%d" % t
         mm(Hr, T.Bo[:], T.hc[:], True, False, "hc", "E1 E2 Hr", "2")
-        mm(zs, T.I[:], T.mh[:], True, False, "mh", "al", "7")
         mm(Hr, T.W2[:], z, False, False, "W2 " + zk, "Hr", "2")
-        for o, k, b in ((xq, "Hr", "2"), (dq, "al", "7"), (zs, "al", "7"), (xr, "al", "7")):
-            mm(o, T.I[:], z, False, False, zk, k, b)
+        mm(dq, T.I[:], z, True, False, zk, "al", "7")
+        mm(zs, T.I[:], z, False, False, zk, "al", "7")
 
-    def own_items(t):
-        act(T.xo[:], T.X[:].indirect(T.VX[:, t, 0:8]), F.Copy, "X xu%d" % t, "xo")
-
-    def own_sums():
-        mm(xq, T.I[:], T.xo[:], False, False, "xo", "Hr", "2")
-        mm(xr, T.I[:], T.xo[:], False, False, "xo", "al", "7")
-
-    def wraps():
-        act(T.xs[:], xq, F.Sign, "Hr", "xs", "2", bias=-255.5)
-        act(T.hy[:], Hr, F.Identity, "Hr", "hy", "2", bias=8388607.5, scale=1.0 / 2048)
-
-    query_start(0)
-    step_start(0)
+    thresholds()
+    bands()
+    query_sums(0)
     W = T.B[:, B0 + 1:]
 
     for t in range(RO):
@@ -324,87 +295,95 @@ def rank_program(g, core, T, topo):
         xik, ck = "xi%d" % t, "c%d" % t
 
         x0 = ((T.p5[:, 0:64], "5"), (T.p0[:, 64:128], "0"))
-        pds = ((T.p1, "1"), (T.p6, "6"))
         for h, GV in enumerate(GVS):
             c = 64 * h
             cp(T.xg[:, 16 * c:16 * (c + GV)], T.X[:].indirect(T.Pu[:, c:c + GV]), "X P" + "ab"[h], "xg%da" % h)
             act(T.xg[:, 16 * (c + GV):16 * c + 1024], T.X[:].indirect(T.Pu[:, c + GV:c + 64]), F.Copy, "X P" + "ab"[h],
                 "xg%db" % h)
             xk = "xg%da xg%db" % (h, h)
-            if h and not t:
-                own_items(0)
+            if h == 0:
+                if not t:
+                    cp(T.VX[:, 0, 0:8], T.O[:, 0, 1:16:2], "xi0", "xu0")
             mm(x0[h][0], T.I[:], T.xg[:, 16 * c:16 * c + 1024:16], True, True, xk, "x0%d" % h, x0[h][1])
-            pd, bd = pds[h]
+            pd, bd = ((T.p1, "1"), (T.p6, "6"))[h]
             for j in range(NS if h == 0 else NB):
                 k, o = 2 * j + 2, pd[:, 64 * j:64 * j + 64]
-                mm(o, T.I[:], T.xg[:, 16 * c + k:16 * c + 1024:16], True, False, xk, "pd%d" % h, bd)
-                mm(o, T.nI[:], T.xg[:, 16 * c:16 * c + 1024:16], False, True, "nI", "pd%d" % h, bd)
-            if h == 0:
-                cp(PP, T.Pu[:], "Pa Pb", Pk)
-                send("P", t, PP, T.lP[:, t, :], Pk)
-                if t:
-                    mm(Hr, T.I[:], PP, False, True, Pk, "Hr", "2")
-                else:
-                    cp(T.VX[:, 0, 0:8], T.O[:, 0, 1:16:2], "xi0", "xu0")
+                mm(o, T.I[:], T.xg[:, 16 * c + k:16 * c + 1024:16], True, False, xk, "pd" + bd, bd)
+                mm(o, T.nI[:], T.xg[:, 16 * c:16 * c + 1024:16], False, True, "nI", "pd" + bd, bd)
+        act(T.ad[:, :, 0:64], T.p1[:, 0:64 * NS], F.Abs, "pd1", "ad0", "1")
         xk = "xg0a xg0b xg1a xg1b"
+        pieces = ((0, NB), (NB, NB + ND), (NB + ND, NS))
         for h in range(2):
             c, hk = 64 * h, "xg%da xg%db x0%d" % (h, h, h)
             if h:
                 for j in range(NB, NS):
                     tt(T.dd[:, j - NB, :], T.xg[:, 1024 + 2 * j + 2:2048:16], x0[1][0], A.subtract, hk, "dd%d" % j, x0[1][1])
-            n = NB if h else NS
-            act(T.ad[:, 0:n, c:c + 64], pds[h][0][:, 0:64 * n], F.Abs, "pd%d" % h, "ad%d" % h, pds[h][1])
-            if h:
-                act(T.ad[:, NB:NS, 64:128], T.dd[:], F.Abs, " ".join("dd%d" % j for j in range(NB, NS)), "ad2")
+                act(T.ad[:, 0:NB, 64:128], T.p6[:, 0:64 * NB], F.Abs, "pd6", "ae0", "6")
+                for n in (1, 2):
+                    a, b = pieces[n]
+                    act(T.ad[:, a:b, 64:128], T.dd[:, a - NB:b - NB, :], F.Abs, " ".join("dd%d" % j for j in range(a, b)),
+                        "ae%d" % n)
             for k in range(1, NV + 1):
                 tt(T.mn[:, k - 1, c:c + 64], T.xg[:, 16 * c + 2 * k - 1:16 * c + 1024:16], x0[h][0], A.min,
                    hk, "mn%d%d" % (h, k), x0[h][1])
-            if h == 0 and t:
-                wraps()
+            if h == 0:
+                cp(PP, T.Pu[:], "Pa Pb", Pk)
+                send("P", t, PP, T.lP[:, t, :], Pk)
         for s in range(1, 4):
             mm(PK[:, s, 1:128:2], T.xg[:, 0:2048:16], T.RB[:, 0:128:2], False, False, xk, "K", "3")
         for k in range(1, NV + 1):
             mm(PK[:, 1:4, 2 * k - 1:128:16], T.xg[:, 2 * k - 1:2048:16], T.R16[:], False, False, "R16", "K", "3")
-        if not t:
-            own_sums()
-            mm(Hr, T.I[:], PP, False, True, Pk, "Hr", "2")
-            wraps()
-            late_constants()
-        for k in range(1, NV + 1):
-            mm(PK[:, 1:4, 2 * k - 1:128:16], T.mn[:, k - 1, :], T.R32[:], False, k == NV, "mn0%d mn1%d R32" % (k, k), "K", "3")
-            if k in (4, NV - 1):
-                for j in (range(NB) if k == 4 else range(NB, NS)):
-                    mm(PK[:, 1:4, 2 * j + 2:128:16], T.ad[:, j, :], T.R16[:], False, False,
-                       "ad0 ad1" if k == 4 else "ad2", "K", "3")
-        ts(T.h2[:, 0:8], T.v2[:], 1023, None, A.bitwise_and, r="v2", w="h2a")
-        if t:
-            ts(T.nn[:], T.hy[:], -8390656.0, None, A.add, r="hy", w="nn")
-        tt(T.hM[:], T.h2[:, 0:8].indirect(T.oc[:]), T.Dg[:], A.mult, "h2a oc Dg", "hM")
+        mm(Hr, T.I[:], PP, False, True, Pk, "Hr", "2")
+        todo = []
+        for k in range(NV + 1):
+            if k:
+                todo.append((2 * k - 1, T.mn[:, k - 1, :], T.R32, "mn0%d mn1%d R32" % (k, k)))
+            for n in range(3):
+                if KA[n] == k:
+                    todo += [(2 * j + 2, T.ad[:, j, :], T.R16, "ad0 ae%d" % n) for j in range(*pieces[n])]
+        for i, (k, l, rh, rk) in enumerate(todo):
+            mm(PK[:, 1:4, k:128:16], l, rh[:], False, i == len(todo) - 1, rk, "K", "3")
+        ts(T.h2[:, 0:8], T.v2[:], 1023, None, A.bitwise_and, r="v2", w="h20")
+        tt(T.xs[:], T.X[:].indirect(xu), z, A.add, "X %s %s" % (xuk, zk), "xs")
+        tt(T.hM[:], T.h2[:, 0:8].indirect(T.oc[:]), T.Dg[:], A.mult, "h20 oc Dg", "hM")
 
+        act(T.hy[:], Hr, F.Identity, "Hr", "hy", "2", bias=8388607.5, scale=1.0 / 2048)
+        if not t:
+            late_constants()
+        act(T.nn[:], T.hy[:], F.Identity, "hy", "nn", bias=-8390656.0)
         mm(dq, T.nI[:], T.xg[:, 0:2048:16], False, False, xk, "al", "7")
-        mm(xr, T.IX[:], T.xs[:], False, False, "IX xs", "al", "7")
         mm(zs, T.I[:], T.lZ[:, t, :], False, True, "lZ%d" % t, "al", "7")
         act(T.aq[:], dq, F.Abs, "al", "aq", "7")
-        act(T.av1[:], zs, F.Identity, "al", "av1", "7", bias=MAGIC, scale=0.5)
-        act(T.xn[:], xr, F.Identity, "al", "xn", "7", bias=-128.0)
+        act(T.av1[:], zs, F.Identity, "al", "av1", "7", bias=1279.75, scale=0.5)
         mm(E1, T.W2[:], z, True, False, "", "Hr E1", "2")
         mm(E2, T.W2[:], z, False, False, "", "E2", "2")
         mm(E2, T.I[:], PP, False, False, "", "E2", "2")
         for s in range(4, 8):
             mm(blk(s, s + 1), T.aq[:], T.RB[:, 0:128], False, s == 7, "aq", "KQ", "4")
 
-        for j in range(6):
+        def back(x, c):
+            return x[:, c + 63:c - 1:-1] if c else x[:, 63::-1]
+
+        for j in range(3):
             for h in range(2):
                 c = 160 * j + 80 * h + 16
-                d1 = T.top[:] if j == 0 else T.SB[:, c - 161:c - 97]
-                scan(T.SB[:, c:c + 64], PK[:, 1, 64 * h:64 * h + 64], d1, 0.0, A.max, A.min,
-                     "K " + ("top" if j == 0 else "s%d%d" % (j - 1, h)), "s%d%d" % (j, h), "3")
-            if j == 0:
-                ts(T.h2[:, 8:16], T.v2[:], 1023, None, A.bitwise_and, r="v2", w="h2b")
-            if j == 1 and not t:
-                ts(T.nn[:], T.hy[:], -8390656.0, None, A.add, r="hy", w="nn")
-        mm(E1, T.IQ[:], T.nn[:], False, False, "IQ nn", "E1", "2")
-        mm(E2, T.IQ[:], T.nn[:], False, False, "", "E2", "2")
+                scan(T.SB[:, c:c + 64], PK[:, 1, 64 * h:64 * h + 64], T.SB[:, c - 161:c - 97] if j else T.top[:], 0.0,
+                     A.max, A.min, "K " + ("s%d%d" % (j - 1, h) if j else "top"), "s%d%d" % (j, h), "3")
+                scan(back(T.SB, c + 480) if j < 2 else back(T.p6, 64 * h), back(PK[:, 1, :], 64 * h),
+                     back(T.SB, c + 321) if j else back(T.top, 0), 0.0, A.max, A.min,
+                     "K " + ("s%d%d" % (j + 2, h) if j else "top"), "s%d%d" % (j + 3, h), "3" if j < 2 else "36")
+        ts(T.h2[:, 8:16], T.v2[:], 1023, None, A.bitwise_and, r="v2", w="h21")
+        for h in range(2):
+            c = 336 + 80 * h
+            tt(T.cut[:, h, :], T.SB[:, c - 1:c + 63], T.p6[:, 64 * h:64 * h + 64], A.min, "s2%d s5%d" % (h, h), "cut%d" % h, "6")
+            if h == 0:
+                ts(T.h2[:, 16:24], T.v2[:], 1023, None, A.bitwise_and, r="v2", w="h22")
+        ts(T.xn[:, 0:64], T.xs[:, 0:64], 255, None, A.bitwise_and, r="xs", w="xn0")
+        for h in range(2):
+            c = 816 + 80 * h
+            scan(T.SB[:, c:c + 64], T.cut[:, h, :], T.to3[:], 0.0, A.max, A.min, "cut%d to3" % h, "m%d" % h)
+            if h == 0:
+                ts(T.xn[:, 64:128], T.xs[:, 64:128], 255, None, A.bitwise_and, r="xs", w="xn1")
 
         def before_e(gs):
             for gi in gs:
@@ -413,136 +392,144 @@ def rank_program(g, core, T, topo):
                     scale=-1.0, bias=T.SB[:, c + 15:c + 16])
 
         nk = " ".join("nc%d" % gi for gi in range(8))
-        mid, amb, Xs, sT, Kb = T.p5[:, 0:128], T.p6[:, 0:160], T.p0[:, 128:256], T.p1[:, 384:512], PK[:, 0, :]
-        act(T.av[:], T.av1[:], F.Identity, "av1", "av", bias=-MAGIC)
-        before_e(range(8))
-        mm(T.p7[:, 256:384], T.I[:], T.M2[:], True, False, "", "al ub", "7")
-        mm(T.p7[:, 256:384], T.av[:], T.Wu[:], False, True, "av", "ub", "7")
+        mid = ((T.p6[:, 256:320], "6"), (PK[:, 1, 0:64], "3"))
+        amb, Xs, sT, Kb = T.p6[:, 0:160], T.p5[:, 128:256], T.p1[:, 384:512], T.p0[:, 128:256]
+        before_e(range(4))
+        act(T.av[:], T.av1[:], F.Identity, "av1", "av", bias=-1280.0)
+        before_e(range(4, 8))
+        mm(E1, T.IQ[:], T.nn[:], False, False, "IQ nn", "E1", "2")
+        mm(E2, T.IQ[:], T.nn[:], False, False, "", "E2", "2")
+        mm(Kb, T.I[:], T.jb[:], True, False, "jb", "Kb", "0")
+        mm(Kb, T.BoK[:], T.hM[:], False, False, "BoK hM", "Kb", "0")
+        mm(ub, T.I[:], T.M2[:], True, False, "M2", "al ub", "7")
+        mm(ub, T.av[:], T.Wu[:], False, True, "av", "ub", "7")
         mm(sT, T.nc[:, 16:144], T.I[:], True, False, nk, "sT", "1")
         mm(sT, T.nc[:, 15:143], T.nI[:], False, True, "", "sT", "1")
         for gi in range(8):
-            c = 816 + 16 * gi + 16 * (gi // 4) + 15
-            ts(T.FL[:, :, 16 * gi:16 * gi + 16], PK[:, 2:4, 16 * gi:16 * gi + 16], T.SB[:, c:c + 1], None, A.is_le,
-               r="K s5%d" % (gi // 4), w="F%d" % gi, b="3")
-            act(T.FQ[:, :, 16 * gi:16 * gi + 16], PK[:, 4:8, 16 * gi:16 * gi + 16], F.Sign, "KQ s5%d" % (gi // 4), "G%d" % gi, "4",
+            c = 816 + 16 * gi + 16 * (gi // 4) + 13
+            ts(T.FL[:, :, 16 * gi:16 * gi + 16], PK[:, 2:4, 16 * gi:16 * gi + 16], 8.0, T.SB[:, c:c + 1], A.add, A.is_le,
+               "K m%d" % (gi // 4), "F%d" % gi, "3")
+            act(T.FQ[:, :, 16 * gi:16 * gi + 16], PK[:, 4:8, 16 * gi:16 * gi + 16], F.Sign, "KQ m%d" % (gi // 4), "G%d" % gi, "4",
                 scale=-1.0, bias=T.SB[:, c:c + 1])
         fl = " ".join("F%d" % gi for gi in range(8))
         fq = " ".join("G%d" % gi for gi in range(8))
-        act(T.uM[:], T.p7[:, 256:384], F.Relu, "ub", "uM", "7")
-        mm(mid, T.FL[:, 1, :], T.I[:], True, False, fl, "mid", "5")
-        mm(mid, T.FL[:, 0, :], T.nI[:], False, True, "", "mid", "5")
+        cp(T.X[:].indirect(xu), T.xn[:], xuk + " xn0 xn1", "X")
         act(T.sg[:], sT, F.Copy, "sT", "sg", "1")
-        mm(Xs, T.FL[:, 0, :], T.I[:], True, False, "", "Xs", "0")
-        mm(Xs, T.FL[:, 1, :], T.I[:], False, False, "", "Xs", "0")
-        mm(Xs, T.FQ[:, 3, :], T.I[:], False, True, fq, "Xs", "0")
+        act(T.uM[:], ub, F.Relu, "ub", "uM", "7")
+        for h, (o, b) in enumerate(mid):
+            mm(o, T.FL[:, 1, :], T.I[:, 64 * h:64 * h + 64], True, False, fl, "mid%d" % h, b)
+            mm(o, T.FL[:, 0, :], T.nI[:, 64 * h:64 * h + 64], False, True, "", "mid%d" % h, b)
+            cp(T.sM[:, t, 64 * h:64 * h + 64], o, "mid%d" % h, "sM%d" % h, b)
+        send("M", t, T.sM[:, t, :], T.lM[:, t, :], "sM0 sM1")
+        mm(Xs, T.FL[:, 0, :], T.I[:], True, False, "", "Xs", "5")
+        mm(Xs, T.FL[:, 1, :], T.I[:], False, False, "", "Xs", "5")
+        mm(Xs, T.FQ[:, 3, :], T.I[:], False, True, fq, "Xs", "5")
+        mm(nL, T.I[:], T.cl[:, int(last), :], True, False, "cl0 cl1 cl2 cm0 cm1", "nL", "1")
+        mm(nL, T.FQ[:, 2, :], T.Rh[:], False, True, "Rh", "nL", "1")
+        mm(Kb, T.FQ[:, 3, :], T.IX[:], False, True, "IX", "Kb", "0")
         mm(amb, T.FQ[:, 1, :], T.R1[:], True, False, "R1a R1b", "amb", "6")
         mm(amb, T.FQ[:, 0, :], T.nR1[:], False, True, "nR1a nR1b", "amb", "6")
-        mm(nL, T.I[:], T.cl[:, int(last), :], True, False, "cl0 cl1 cm0 cm1", "nL", "1")
-        mm(nL, T.FQ[:, 2, :], T.R1[:, 129:160:2], False, True, "", "nL", "1")
-        mm(Kb, T.I[:], T.jb[:], True, False, "jb", "Kb", "3")
-        mm(Kb, T.FQ[:, 3, :], T.IX[:], False, False, "", "Kb", "3")
-        mm(Kb, T.BoK[:], T.hM[:], False, True, "BoK hM", "Kb", "3")
         mm(E2, T.nI[:], T.lP[:, t, :], False, True, "lP%d" % t, "E1 E2", "2")
-        u_list(not last)
-        cp(T.X[:].indirect(xu), T.xn[:], xuk + " xn", "X")
+        if not last:
+            mm(uL, T.I[:], T.cu[:], True, False, "cu0 cu1", "uL", "7")
+        mm(uL, T.uM[:], T.sel32[:], last, True, "uM", "uL", "7")
         if not t:
             bag_copy(0)
-        act(T.sM[:, t, :], mid, F.Copy, "mid", "sM%d" % t, "5")
-        act(T.xa[:], Xs, F.Abs, "Xs", "xa", "0", bias=-1.0)
-        act(T.sA[:, t, :], amb, F.Copy, "amb", "sA%d" % t, "6")
-        send("M", t, T.sM[:, t, :], T.lM[:, t, :], "sM%d" % t)
-        send("A", t, T.sA[:, t, :], T.lA[:, t, :], "sA%d" % t)
-
-        tt(O[:, 17:48:2], T.h2[:], nL, A.subtract, "h2a h2b nL", ck + " bc", "1")
+        act(T.xa[:], Xs, F.Abs, "Xs", "xa", "5", bias=-1.0)
+        tt(O[:, 17:64:2], T.h2[:], nL, A.subtract, "h20 h21 h22 nL", ck + " bc", "1")
         if not t:
             bag_copy(1)
-        act(T.ns[:], T.xa[:], F.Sign, "xa", "ns", scale=-1.0, bias=2.0)
+        ts(T.ns[:], T.xa[:], 1.5, None, A.is_le, r="xa", w="ns")
+        cp(T.sA[:, t, :], amb, "amb", "sA%d" % t, "6")
+        send("A", t, T.sA[:, t, :], T.lA[:, t, :], "sA%d" % t)
+
         for c in range(8):
-            act(T.kd[:, KD[c]:KD[c + 1]], Kb[:, 16 * c:128], F.Abs, "Kb bc", "kd%d" % c, "3",
+            act(T.kd[:, KD[c]:KD[c + 1]], Kb[:, 16 * c:128], F.Abs, "Kb bc", "kd%d" % c, "0",
                 scale=-1.0 / 256, bias=O[:, 33 + 2 * c:34 + 2 * c])
-        base, sd, S = T.p1[:, 128:256], T.p0[:, 256:384], T.p5[:, 0:128]
-        mm(base, T.I[:], PP, True, False, "", "base", "1")
-        cp(T.ui[:], uL, "uL", "ui", "7")
-        tt(T.be[:], E1, T.ns[:], A.mult, "E1 ns", "be", "2")
-        tt(E2, E2, T.ns[:], A.mult, "E2 ns", "E2", "2")
-        mm(base, T.I[:], T.be[:], False, True, "be", "base", "1")
-        mm(T.p7[:, 256:384], T.I[:], z, True, False, zk, "zq", "7")
-        mm(T.p7[:, 384:512], T.I[:], T.av[:], False, False, "av", "zq", "7")
-        mm(T.p7[:, 384:512], T.I[:], T.m256[:], False, False, "m256", "zq", "7")
+        if last:
+            ts(T.wl[:], O[:, 17:32:2], 1023.5, None, A.is_lt, r=ck, w="wl")
+        else:
+            act(T.sB[:], amb[:, 0:128], F.Identity, "amb", "sB", "6", bias=T.bth[:, t + 1:t + 2])
+            thresholds()
 
         def least(a, b):
             scan(T.km[:, KD[a]:KD[b]], T.rs[:, KD[a]:KD[b]], T.kd[:, KD[a]:KD[b]], 0.0, A.max, A.min,
                  rsk + " " + " ".join("kd%d" % c for c in range(a, b)), "km%d" % a)
 
+        S, sd = ((T.p5[:, 0:64], "5"), (T.p0[:, 0:64], "0")), T.p1[:, 128:256]
+        tt(E1, E1, T.ns[:], A.mult, "ns", "E1", "2")
+        tt(E2, E2, T.ns[:], A.mult, "ns", "E2", "2")
+        cp(T.ui[:], uL, "uL", "ui", "7")
+        mm(T.p7[:, 256:384], T.I[:], z, True, False, zk, "zq", "7")
+        mm(T.p7[:, 384:512], T.I[:], T.av[:], False, False, "av", "zq", "7")
+        tt(E1, E1, PP, A.add, Pk, "E1", "2")
+        tt(sd, E2, T.sg[:], A.mult, "E2 sg", "sd", "21")
         least(0, 4)
-        tt(sd, E2, T.sg[:], A.mult, "E2 sg", "sd", "20")
+        tt(T.sbf[:], E1, T.sg[:], A.mult, "E1 sg", "sbf", "2")
         least(4, 8)
-        tt(T.sbf[:], base, T.sg[:], A.mult, "base sg", "sbf", "1")
-        ts(O[:, 16:48:2], T.km[:].indirect(T.ke[:, 0:1]), -1048576.0, 260096.0, A.mult, A.add, "km0 km4 ke", "lose")
         ts(T.u15[:], T.ui[:, 0:8], 15, None, A.bitwise_and, r="ui", w="u15")
         ts(T.un[:, 8:16], T.ui[:, 8:16], 1023, None, A.bitwise_and, r="ui", w="un0")
         if last:
+            tt(O[:, 17:32:2], O[:, 17:32:2], T.wl[:], A.mult, "wl", ck)
+        for h, (o, b) in enumerate(S):
+            mm(o, T.nBo[:], T.sbf[:, 64 * h:64 * h + 64], True, False, "nBo sbf", "S%d" % h, b)
+        if last:
             lands("allsent", "sent", sent[0])
             dma("Y", T.yx[:], T.X[:], "X allsent", "", "o1")
-        else:
-            query_start(t + 1)
-        mm(S, T.nBo[:], T.sbf[:], True, False, "nBo sbf", "S", "5")
-        scan(T.ds[:], T.cap[:], O[:, 16:32], 0.0, A.min, A.max, "cap lose " + ck, "ds")
-        tt(T.un[:, 0:8], T.u15[:], T.l16[:], A.add, "u15 l16", "un1")
         if not t:
             bag_copy(2)
-        if last:
-            ts(T.wl[:], O[:, 17:32:2], 1023.5, None, A.is_lt, r=ck, w="wl")
+        ts(O[:, 48:80:2], T.km[:].indirect(T.ke[:, 0:1]), -1048576.0, 260096.0, A.mult, A.add, "km0 km4 ke", "lose")
+        tt(T.un[:, 0:8], T.u15[:], T.l16[:], A.add, "u15 l16", "un1")
 
         lm, la = "lM%d" % t, "lA%d" % t
-        tt(T.tp[:], T.lM[:, t, :], sd, A.mult, lm + " sd", "tp", "0")
-        mm(S, T.Bo[:], T.tp[:], False, True, "tp", "S", "5")
+        for h, (o, b) in enumerate(S):
+            c = 64 * h
+            tt(T.tp[:, c:c + 64], T.lM[:, t, c:c + 64], sd[:, c:c + 64], A.mult, lm + " sd", "tp%d" % h, "1")
+            mm(o, T.Bo[:], T.tp[:, c:c + 64], False, True, "tp%d" % h, "S%d" % h, b)
         tt(T.y1[:], T.lM[:, t, :], E2, A.mult, lm + " E2", "y1", "2")
-        ts(T.wu[:], T.ds[:, 1:16:2], -1.0 if last else 0.0, None, A.add, r="ds", w="wu")
-        if last:
-            tt(O[:, 17:32:2], O[:, 17:32:2], T.wl[:], A.mult, "wl", ck)
-        else:
-            tt(O[:, 0:32:2], T.un[:], O[:, 1:32:2], A.subtract, "un0 un1 %s %s" % (xik, ck), "lose")
-        tt(T.y2[:], base, T.y1[:], A.subtract, "y1 base", "y2", "1")
-        tt(T.rr[:], S, T.sg[:], A.mult, "S sg", "rr", "5")
-        if last:
-            tt(O[:, 0:32:2], T.un[:], O[:, 1:32:2], A.subtract, "un0 un1 %s %s" % (xik, ck), "lose")
-        mm(T.p7[:, 256:384], T.nBo8[:], T.lA[:, t, 0:128], False, False, "nBo8 " + la, "zq", "7")
-        mm(T.p7[:, 384:512], T.Bo8[:], T.lA[:, t, 0:128], False, True, "Bo8", "zq", "7")
-        act(T.zr[:], T.p7[:, 256:512], F.Relu, "zq", "zr", "7")
-        mm(T.p6[:, 0:128], T.I[:], T.zr[:, 0:128], True, False, "zr", "zn", "6")
-        mm(T.p6[:, 0:128], T.I[:], T.zr[:, 128:256], False, True, "zr", "zn", "6")
-        if not last:
-            act(T.zb[:, t + 1, :], T.p6[:, 0:128], F.Copy, "zn", "z%d" % (t + 1), "6")
+        scan(T.ds[:], T.cap[:], O[:, 48:64], 0.0, A.min, A.max, "cap lose bc", "ds")
+        tt(O[:, 0:32:2], T.un[:], O[:, 1:32:2], A.subtract, "un0 un1 %s %s" % (xik, ck), "diff")
 
         def pick():
             scan(T.O[:, t + 1, 0:32], T.lA[:, t, 128:160], O[:, 0:32], 0.0, A.mult, A.add,
-                 "%s lose %s %s" % (la, xik, ck), "xi%d c%d" % (t + 1, t + 1))
+                 "%s diff %s %s" % (la, xik, ck), "xi%d c%d" % (t + 1, t + 1))
 
+        tt(T.y2[:], E1, T.y1[:], A.subtract, "y1 E1", "y2", "2")
+        cp(T.wu[:], T.ds[:, 1:16:2], "ds", "wu")
+        for h, (o, b) in enumerate(S):
+            tt(T.rr[:, 64 * h:64 * h + 64], o, T.sg[:, 64 * h:64 * h + 64], A.mult, "S%d sg" % h, "rr%d" % h, b)
         if not last:
             pick()
-        tt(W.indirect(T.wu[:]), T.y2[:], T.rr[:], A.add, "wu y2 rr", "B Bz B0 B1 B2")
+        mm(T.p7[:, 256:384], T.nBo8[:], T.lA[:, t, 0:128], False, False, "nBo8 " + la, "zq", "7")
+        mm(T.p7[:, 384:512], T.Bo8[:], T.lA[:, t, 0:128], False, True, "Bo8", "zq", "7")
+        if not last:
+            bands()
+        act(T.zr[:, 0:128], T.p7[:, 256:384], F.Relu, "zq", "zr0", "7")
+        act(T.zr[:, 128:256], T.p7[:, 384:512], F.Relu, "zq", "zr1", "7", bias=-256.0)
+        mm(T.p6[:, 0:128], T.I[:], T.zr[:, 0:128], True, False, "zr0", "amb zn", "6")
+        mm(T.p6[:, 0:128], T.I[:], T.zr[:, 128:256], False, True, "zr1", "zn", "6")
+        if not last:
+            act(T.zb[:, t + 1, :], T.p6[:, 0:128], F.Copy, "zn", "z%d" % (t + 1), "6")
+        tt(W.indirect(T.wu[:]), T.y2[:], T.rr[:], A.add, "wu y2 rr0 rr1", "B Bz B0 B1 B2 B3")
         if not last:
             send("Z", t + 1, T.zb[:, t + 1, :], T.lZ[:, t + 1, :], "z%d" % (t + 1))
+            query_sums(t + 1)
             cp(T.VX[:, t + 1, :], T.O[:, t + 1, 1:32:2], "c%d" % (t + 1), "vu%d xu%d" % (t + 1, t + 1))
-            step_start(t + 1)
-            own_items(t + 1)
-            own_sums()
             ts(T.v2[:], T.O[:, t + 1, 17:32:2], 2.0, 2.0, A.mult, A.add, "c%d" % (t + 1), "v2")
             for h in range(2):
                 cp(T.Pu[:, 64 * h:64 * h + 64], W[:, 0:1024].indirect(T.VX[:, t + 1, 8 + 4 * h:12 + 4 * h]),
                    "B vu%d" % (t + 1), "P" + "ab"[h])
     pick()
-    cp(T.zb[:, RO, :], T.p6[:, 0:128], "zn", "z%d" % RO, "6")
-    cp(T.vf[:], T.O[:, RO, 17:32:2], "c%d" % RO, "vf")
     cp(T.B[:, B0:B0 + 1], T.B[:, B0 + 1024:B0 + 1025], "B", "Bz")
-    dma("Y", T.yz[:], T.zb[:, RO, :], "z%d" % RO, "", "o2")
+    cp(T.vf[:], T.O[:, RO, 17:32:2], "c%d" % RO, "vf")
+    cp(T.zb[:, RO, :], T.p6[:, 0:128], "zn", "z%d" % RO, "6")
     dma("Y", T.yv[:], T.vf[:], "vf", "", "o5")
-    for h, (pb, bk) in zip((3, 2, 1, 0), ((T.p1, "1"), (T.p2, "2"), (T.p5, "5"), (T.p0, "0"))):
-        c = 128 * h
-        act(pb[:, 0:128], T.B[:, B0 + 512 + c:B0 + 640 + c], F.Identity, "B", "hi%d" % h, bk, scale=2048.0)
-        tt(T.yo[:, c:c + 128], T.B[:, B0 + c:B0 + c + 128], pb[:, 0:128], A.add, "B Bz hi%d" % h, "yo%d" % h, bk)
-    dma("Y", T.yb[:, 256:512], T.yo[:, 256:512], "yo2 yo3", "", "o4")
-    dma("S", T.yb[:, 0:256], T.yo[:, 0:256], "yo0 yo1", "", "o3")
+    dma("Y", T.yz[:], T.zb[:, RO, :], "z%d" % RO, "", "o2")
+    for h, (pb, bk) in enumerate(((T.p1, "1"), (T.p2, "2"), (T.p5, "5"), (T.p0, "0"), (T.p7, "7"))):
+        a, b = YP[h + 1], YP[h]
+        act(pb[:, 0:b - a], T.B[:, B0 + 512 + a:B0 + 512 + b], F.Identity, "B", "hi%d" % h, bk, scale=2048.0)
+        tt(T.yo[:, a:b], T.B[:, B0 + a:B0 + b], pb[:, 0:b - a], A.add, "B hi%d" % h + ("" if a else " Bz"), "yo%d" % h, bk)
+    dma("Y", T.yb[:, 256:512], T.yo[:, 256:512], "yo0 yo1 yo2", "", "o4")
+    dma("S", T.yb[:, 0:256], T.yo[:, 0:256], "yo3 yo4", "", "o3")
     for s, v in count.items():
         wait("G", (s, v))

from concourse.mybir import AluOpType as A, ActivationFunctionType as F

RO, HN, HZ = 4, [1, 2, 3, 1], [3, 1, 2, 2]
NV = 8
NS = 15 - NV
NB = 2
ND = 2
KA = (0, 2, 6)
GVS = (32, 32)
BP = (0, 256, 512, 704)
YP = (512, 448, 384, 256, 128, 0)
B0 = 7
KD = [128 * c - 8 * c * (c - 1) for c in range(9)]
f32, bf, f16, i32, u16 = "float32", "bfloat16", "float16", "int32", "uint16"


def _sb(n, d):
    return ("sbuf", [128] + (n if isinstance(n, list) else [n]), d)


SCRATCH = {
    "X": _sb(2048, bf), "Bi": _sb(1024, i32), "B": _sb(1168, f32), "xg": _sb(2048, bf),
    "Z": _sb(8, i32), "VX": _sb([4, 16], u16), "vf": _sb(8, f32), "O": _sb([5, 80], f32),
    "uwi": _sb(4, i32), "bti": _sb(4, i32), "zb": _sb([5, 128], bf),
    "Pu": _sb(128, u16), "PP": _sb([4, 128], f16), "lP": _sb([4, 128], f16), "lZ": _sb([4, 128], bf),
    "lM": _sb([4, 128], bf), "sM": _sb([4, 128], bf), "lA": _sb([4, 160], bf), "sA": _sb([4, 160], bf), "sB": _sb(128, f16),
    "v2": _sb(8, i32), "h2": _sb(24, i32), "hM": _sb(128, f16),
    "mn": _sb([NV, 128], bf), "ad": _sb([NS, 128], bf), "dd": _sb([NS - NB, 64], bf), "aq": _sb(128, bf), "SB": _sb(960, f32),
    "FL": _sb([2, 128], bf), "FQ": _sb([4, 128], bf), "hy": _sb(128, f32), "nn": _sb(128, f16),
    "kd": _sb(576, bf), "km": _sb(576, bf), "rs": _sb(576, bf), "ds": _sb(16, f32), "wu": _sb(8, u16), "wl": _sb(8, f32),
    "nc": _sb(144, bf), "xa": _sb(128, bf), "ns": _sb(128, bf),
    "sg": _sb(128, f32), "av1": _sb(128, f16), "av": _sb(128, bf), "uM": _sb(128, f32), "ui": _sb(16, i32),
    "u15": _sb(8, i32), "un": _sb(16, i32), "xs": _sb(128, i32), "xn": _sb(128, i32), "sbf": _sb(128, f16),
    "tp": _sb(128, f16), "y1": _sb(128, f32), "y2": _sb(128, f32), "rr": _sb(128, f32), "zr": _sb(256, bf),
    "yo": _sb(512, f32),
    "pi": _sb(4, i32), "pc": _sb(4, i32), "pf": _sb(8, f32), "jb": _sb(128, bf), "gb": _sb(128, bf), "j24": _sb(24, bf),
    "ci": _sb(8, f32), "tA": _sb(128, i32), "tC": _sb(128, i32), "ok": _sb(128, bf), "kb": _sb(128, bf), "one": _sb(128, bf),
    "I": _sb(128, bf), "nI": _sb(128, bf), "IQ": _sb(128, bf), "IX": _sb(128, bf), "Bo": _sb(128, bf), "RB": _sb(256, bf),
    "Bo8": _sb(128, bf), "nBo8": _sb(128, bf), "BoK": _sb(128, bf), "nBo": _sb(128, bf), "Dg": _sb(128, bf),
    "top": _sb(64, f32), "to3": _sb(64, f32), "cut": _sb([2, 64], f32), "hc": _sb(128, bf), "M2": _sb(128, bf), "CQ": _sb(512, bf), "sel": _sb(24, bf),
    "R16": _sb(24, bf), "R32": _sb(24, bf), "Rh": _sb(24, bf), "R1": _sb(160, bf), "nR1": _sb(160, bf), "sel32": _sb(16, f32),
    "bth": _sb(4, f32), "W2": _sb(128, f16), "Wu": _sb(128, f16), "uwf": _sb(4, f32),
    "oc": _sb(8, u16), "ke": _sb(2, u16), "l16": _sb(8, f32), "cl": _sb([2, 24], f16), "cu": _sb(16, f16), "cap": _sb(16, f32),
    "p0": ("psum", [128, 512], f32), "p1": ("psum", [128, 512], f32), "p2": ("psum", [128, 512], f32),
    "PK": ("psum", [128, 8, 128], f32), "p5": ("psum", [128, 512], f32), "p6": ("psum", [128, 512], f32),
    "p7": ("psum", [128, 512], f32),
}
SEMAPHORES = (["cV", "cS", "cP", "cG", "sent", "dv", "du", "db", "dz", "dB", "dX", "o1", "o2", "o3", "o4", "o5"]
              + ["a%s%d" % (k, t) for k in "PZMA" for t in range(RO)])


def rank_program(g, core, T, topo):
    rank = T.rank_of(core)
    if rank is None:
        return
    N = len(T.cores)
    Q = {"V": g.vector, "S": g.scalar, "P": g.tensor, "G": g, "Y": g.sync}
    count = {}
    know = {e: {} for e in Q}
    after = {}
    lastw, readers, bank = {}, {}, {}

    def wait(e, tok):
        s, v = tok
        if know[e].get(s, 0) >= v:
            return
        Q[e].wait_ge(T.sem[s], v)
        for s2, v2 in after[tok].items():
            if know[e].get(s2, 0) < v2:
                know[e][s2] = v2

    def op(e, fn, r="", w="", b="", sem=None, inc=1):
        r, w = r.split(), w.split()
        deps = [lastw[k] for k in r + w if k in lastw]
        for k in w:
            deps += readers.get(k, [])
        deps += [bank[k][1] for k in b if k in bank and bank[k][0] != e]
        if e == "P":
            deps = [d for d in deps if d[0] != "cP"]
        best = {}
        for s, v in deps:
            best[s] = max(best.get(s, 0), v)
        for s, v in sorted(best.items(), key=lambda x: -len(after[x])):
            wait(e, (s, v))
        ins = fn(Q[e])
        if sem is False:
            return
        s = sem or "c" + e
        count[s] = count.get(s, 0) + inc
        tok = (s, count[s])
        ins.then_inc(T.sem[s], inc)
        after[tok] = dict(know[e])
        after[tok][s] = count[s]
        for k in r:
            readers.setdefault(k, []).append(tok)
        for k in w:
            lastw[k] = tok
            readers[k] = []
        for k in b:
            bank[k] = (e, tok)

    def lands(key, s, n):
        count[s] = n
        after[(s, n)] = {s: n}
        lastw[key] = (s, n)

    def ts(out, in0, s1, s2, o0, o1=None, r="", w="", b=""):
        if o1 is None:
            op("V", lambda q: q.tensor_scalar(out, in0, s1, None, o0), r, w, b)
        else:
            op("V", lambda q: q.tensor_scalar(out, in0, s1, s2, o0, o1), r, w, b)

    def tt(out, x, y, o, r="", w="", b=""):
        op("V", lambda q: q.tensor_tensor(out, x, y, o), r, w, b)

    def cp(out, x, r="", w="", b=""):
        op("V", lambda q: q.tensor_copy(out, x), r, w, b)

    def scan(out, x, y, init, o0, o1, r="", w="", b=""):
        op("V", lambda q: q.tensor_tensor_scan(out, x, y, init, o0, o1), r, w, b)

    def act(out, x, fn, r="", w="", b="", **kw):
        op("S", lambda q: q.activation(out, x, fn, **kw), r, w, b)

    def mm(out, l, rh, st, sp, r="", w="", b=""):
        op("P", lambda q: q.matmul(out, l, rh, st, sp), r, w, b)

    def ms(ap, val, w):
        op("V", lambda q: q.memset(ap, val), "", w)

    def dma(e, out, x, r, w, sem):
        op(e, lambda q: q.dma_start(out, x), r, w, "", sem, 16)

    def iota(out, pat, base, cm, r, w):
        op("G", lambda q: q.iota(out, pat, base, cm, allow_small_or_imprecise_dtypes=True), r, w)

    def masks(r, t):
        src, da, dc = T.cores[r % N], T.cores[(r + HN[t]) % N], T.cores[(r + HZ[t]) % N]
        ea, ec = topo.engines(src, da), topo.engines(src, dc)
        if len(ea) > len(ec):
            return [e for e in ea if e not in ec], ec
        if len(ec) > len(ea):
            return ea, [e for e in ec if e not in ea]
        return ea, ec

    sent = [0]

    def send(kind, t, src, dst, r):
        j = 0 if kind in "PM" else 1
        hop = (HN, HZ)[j][t]
        es = masks(rank, t)[j]
        rid, pid = topo.addr(T.cores[(rank + hop) % N], core)
        sem = "a%s%d" % (kind, t)
        lands("l%s%d" % (kind, t), sem, len(masks(rank - hop, t)[j]))
        op("G", lambda q: q.remote_dma(dst, src, T.sem[sem], T.sem.sent, pid, rid, sum(1 << e for e in es)), r, sem=False)
        sent[0] += len(es)

    ms(T.bti[:], 0, "bti")
    dma("Y", T.uwi[:, 0:1], T.uw[:], "", "uwi", "du")
    dma("S", T.zb[:, 0, :], T.z0[:], "", "z0", "dz")
    dma("Y", T.Z[:], T.v0[:], "", "v0", "dv")
    dma("Y", T.bti[0:128:16, :], T.bt[:], "", "bti", "db")
    dma("Y", T.Bi[:], T.bag[:], "", "Bi", "dB")
    dma("Y", T.X[:], T.xt[:], "", "X", "dX")

    PK = T.PK
    uL, nL, ub = T.p7[:, 144:160], T.p1[:, 0:24], T.p7[:, 256:384]
    pg, pk, pp = T.pf[:, 0:1], T.pf[:, 1:2], T.pf[:, 2:3]

    def blk(a, b):
        return PK[:, a, :] if b == a + 1 else PK[:, a:b, :]

    def scaled(src, *outs):
        for name, out, c in outs:
            act(out, T[src][:], F.Identity, src, name, scale=c)

    op("G", lambda q: q.iota(T.pi[:, 0:1], [[0, 1]], 0, 1), "", "pi")
    iota(T.gb[:], [[1, 8], [0, 16]], 0, 0, "", "gb")
    iota(T.kb[:], [[0, 8], [1, 16]], 0, 0, "", "kb")
    iota(T.jb[:], [[1, 128]], 0, 0, "", "jb")
    iota(T.j24[:], [[0, 3], [1, 8]], 0, 0, "", "j24")
    iota(T.ci[:], [[16, 8]], 0, 0, "", "ci")
    ms(T.one[:], 1.0, "one")
    ms(T.top[:], 1048576.0, "top")
    sk = " ".join("s%d%d" % (j, h) for j in range(6) for h in range(2))
    ms(T.SB[:, 15:480:80], 0.0, sk)
    ms(T.to3[:], 1048576.0, "to3")
    ms(T.nc[:, 0:16], 0.0, "nc")
    ts(T.pc[:, 0:1], T.pi[:, 0:1], 4, None, A.arith_shift_right, r="pi", w="pc0")
    ts(T.pc[:, 1:2], T.pi[:, 0:1], 15, None, A.bitwise_and, r="pi", w="pc1")
    cp(T.pf[:, 2:3], T.pi[:, 0:1], "pi", "pf2")
    ms(T.cap[:], -1.0, "cap")
    ms(T.top[:, 0:64:16], 0.0, "top")
    ms(T.SB[:, 560:960:80], 0.0, sk)
    ms(T.to3[:, 2:64:16], 0.0, "to3")
    ms(T.R1[:, 128:160], 0.0, "R1b")
    cp(T.pf[:, 0:2], T.pc[:, 0:2], "pc0 pc1", "pf0")
    ms(T.nR1[:, 128:160], 0.0, "nR1b")
    ms(T.cl[:, :, 16:24], 7.0, "cl2")
    ms(T.cl[:, 0, 0:8], 7.0, "cl0")
    ms(T.cl[:, 1, 0:8], 6.0, "cl1")
    ts(T.ok[:], T.kb[:], 2.0, 1.0, A.mult, A.add, "kb", "ok")
    ts(T.Bo[:], T.gb[:], pg, None, A.is_equal, r="gb pf0", w="Bo")
    ts(T.Dg[:], T.kb[:], pk, None, A.is_equal, r="kb pf0", w="Dg")
    ts(T.pf[:, 3:4], pk, -8.0, 128.0, A.mult, A.add, "pf0", "pf3")
    ts(T.pf[:, 4:5], pk, 1.0, None, A.add, r="pf0", w="pf4")
    tt(T.ok[:], T.ok[:], T.Bo[:], A.mult, "Bo", "ok")
    ts(T.uwf[:, 0:1], T.uwi[:, 0:1], -2048.0, None, A.add, r="uwi", w="uwf0")
    ts(T.I[:], T.jb[:], pp, None, A.is_equal, r="jb pf2", w="I")
    ts(T.pf[:, 5:6], pk, 0.0, 4194304.0, A.is_equal, A.mult, "pf0", "pf5")
    ts(T.pf[:, 6:7], pk, 1.0, 0.5, A.is_equal, A.mult, "pf0", "pf6")
    ts(T.Wu[:], T.Bo[:], T.uwf[:, 0:1], None, A.mult, r="Bo uwf0", w="Wu")
    ts(T.tC[:], T.ok[:], T.uwf[:, 0:1], 66560.0, A.mult, A.add, r="ok uwf0", w="tC")
    ts(T.sel[:], T.j24[:], pg, None, A.is_equal, r="j24 pf0", w="sel")
    cp(T.VX[:, 0, 8:16], T.Z[:], "v0", "vu0")
    ts(T.pf[:, 7:8], pk, 0.0, 0.5, A.is_equal, A.mult, "pf0", "pf7")
    ts(T.tA[:], T.tC[:], 2047, None, A.bitwise_and, r="tC", w="tA")
    ts(T.l16[:], T.ci[:], pk, 16.0, A.add, A.mult, "ci pf0", "l16")
    ts(T.oc[:], T.ci[:], 0.0625, None, A.mult, r="ci", w="oc")
    ts(T.bth[:], T.bti[:], T.pf[:, 7:8], None, A.add, r="bti pf7", w="bth")
    ts(T.W2[:], T.tA[:], -1024.0, None, A.add, r="tA", w="W2")
    ts(T.v2[:], T.Z[:], 2.0, None, A.mult, r="v0", w="v2")

    scaled("one", ("CQ3", T.CQ[:, 384:512], 15.5))
    scaled("Bo", ("RB0", T.RB[:, 0:128], 16.0), ("RB1", T.RB[:, 128:256], -16.0), ("Bo8", T.Bo8[:], 8.0))
    act(T.M2[:], T.Dg[:], F.Identity, "Dg", "M2", scale=16777216.0, bias=-8388608.0)
    for s, c in enumerate((7.5, 7.5, 15.5)):
        act(T.CQ[:, 128 * s:128 * s + 128], T.Dg[:], F.Identity, "Dg", "CQ%d" % s, scale=c - 1048576.0, bias=1048576.0)
    scaled("I", ("nI", T.nI[:], -1.0))
    act(T.hc[:], T.one[:], F.Identity, "one pf5 pf6", "hc", scale=T.pf[:, 5:6], bias=T.pf[:, 6:7])
    act(T.sel32[:], T.sel[:, 0:16], F.Identity, "sel", "sel32")
    mm(ub, T.I[:], T.M2[:], True, False, "I M2", "ub", "7")
    mm(ub, T.zb[:, 0, :], T.Wu[:], False, True, "z0 Wu", "ub", "7")
    act(T.uM[:], ub, F.Relu, "ub", "uM", "7")
    mm(uL, T.uM[:], T.sel32[:], True, True, "uM sel32", "uL", "7")
    send("Z", 0, T.zb[:, 0, :], T.lZ[:, 0, :], "z0")
    act(T.sB[:], T.one[:], F.Identity, "one bth", "sB", scale=T.bth[:, 0:1])
    scaled("sel", ("R16", T.R16[:], 16.0), ("R32", T.R32[:], -32.0), ("Rh", T.Rh[:], 0.5))
    scaled("Bo", ("nBo8", T.nBo8[:], -8.0), ("nBo", T.nBo[:], -1.0), ("BoK", T.BoK[:], 256.0))

    def late_constants():
        scaled("I", ("IQ", T.IQ[:], -2048.0), ("IX", T.IX[:], -128.0), ("R1a", T.R1[:, 0:128], 16.0),
               ("nR1a", T.nR1[:, 0:128], -16.0))

    act(T.R1[:, 129:160:2], T.sel[:, 0:16], F.Identity, "sel", "R1b", scale=0.5)
    act(T.nR1[:, 129:160:2], T.sel[:, 0:16], F.Identity, "sel", "nR1b", scale=-0.5)
    act(T.cap[:, 1:16:2], T.l16[:], F.Identity, "l16", "cap", scale=1.0 / 16, bias=1025.0)
    iota(T.rs[:], [[0, KD[8]]], 0, 0, "", "rs")
    for c in range(8):
        iota(T.rs[:, KD[c]:KD[c] + 1], [[0, 1]], 4096, 0, "rs", "rs%d" % c)
    rsk = " ".join("rs%d" % c for c in range(8))
    cp(T.Pu[:], T.Bi[:].indirect(T.VX[:, 0, 8:16]), "Bi vu0", "Pa Pb")
    cp(T.B[:, B0 + BP[3]:B0 + 1024], T.Bi[:, BP[3]:1024], "Bi", "B3")
    cp(T.ui[:, 0:8], uL[:, 0:8], "uL", "ui", "7")
    ts(T.ke[:, 0:1], T.pf[:, 3:4], T.pf[:, 4:5], -1.0, A.mult, A.add, "pf3 pf4", "ke")
    for j in range(2):
        ts(T.cl[:, j, 8:16], T.l16[:], -1.0 / 4096, 7.25, A.mult, A.add, "l16", "cm%d" % j)
    ts(T.u15[:], T.ui[:, 0:8], 15, None, A.bitwise_and, r="ui", w="u15")
    ms(T.cu[:, 0:8], 0.0, "cu0")
    ms(T.cu[:, 8:16], 1023.0, "cu1")
    cp(T.B[:, B0 + 1024:B0 + 1025], T.Bi[:, 0:1], "Bi", "Bz")
    tt(T.O[:, 0, 1:16:2], T.u15[:], T.l16[:], A.add, "u15 l16", "xi0")

    def bag_copy(j):
        cp(T.B[:, B0 + BP[j]:B0 + BP[j + 1]], T.Bi[:, BP[j]:BP[j + 1]], "Bi", "B%d" % j)

    dq, zs = T.p7[:, 0:128], T.p7[:, 384:512]
    Hr, E1, E2 = T.p2[:, 128:256], T.p2[:, 256:384], T.p2[:, 384:512]

    def thresholds():
        mm(blk(1, 2), T.I[:], T.kb[:], True, False, "I kb", "K mid1", "3")
        mm(blk(4, 8), T.I[:], T.CQ[:], True, False, "CQ0 CQ1 CQ2 CQ3", "KQ", "4")

    def bands():
        mm(blk(2, 4), T.sB[:], T.RB[:], False, False, "sB RB0 RB1", "K", "3")
        mm(blk(4, 6), T.sB[:], T.RB[:], False, False, "", "KQ", "4")

    def query_sums(t):
        z, zk = T.zb[:, t, :], "z%d" % t
        mm(Hr, T.Bo[:], T.hc[:], True, False, "hc", "E1 E2 Hr", "2")
        mm(Hr, T.W2[:], z, False, False, "W2 " + zk, "Hr", "2")
        mm(dq, T.I[:], z, True, False, zk, "al", "7")
        mm(zs, T.I[:], z, False, False, zk, "al", "7")

    thresholds()
    bands()
    query_sums(0)
    W = T.B[:, B0 + 1:]

    for t in range(RO):
        last = t == RO - 1
        z, zk = T.zb[:, t, :], "z%d" % t
        xu, xuk = T.VX[:, t, 0:8], "xu%d" % t
        O, PP, Pk = T.O[:, t, :], T.PP[:, t, :], "PP%d" % t
        xik, ck = "xi%d" % t, "c%d" % t

        x0 = ((T.p5[:, 0:64], "5"), (T.p0[:, 64:128], "0"))
        for h, GV in enumerate(GVS):
            c = 64 * h
            cp(T.xg[:, 16 * c:16 * (c + GV)], T.X[:].indirect(T.Pu[:, c:c + GV]), "X P" + "ab"[h], "xg%da" % h)
            act(T.xg[:, 16 * (c + GV):16 * c + 1024], T.X[:].indirect(T.Pu[:, c + GV:c + 64]), F.Copy, "X P" + "ab"[h],
                "xg%db" % h)
            xk = "xg%da xg%db" % (h, h)
            if h == 0:
                if not t:
                    cp(T.VX[:, 0, 0:8], T.O[:, 0, 1:16:2], "xi0", "xu0")
            mm(x0[h][0], T.I[:], T.xg[:, 16 * c:16 * c + 1024:16], True, True, xk, "x0%d" % h, x0[h][1])
            pd, bd = ((T.p1, "1"), (T.p6, "6"))[h]
            for j in range(NS if h == 0 else NB):
                k, o = 2 * j + 2, pd[:, 64 * j:64 * j + 64]
                mm(o, T.I[:], T.xg[:, 16 * c + k:16 * c + 1024:16], True, False, xk, "pd" + bd, bd)
                mm(o, T.nI[:], T.xg[:, 16 * c:16 * c + 1024:16], False, True, "nI", "pd" + bd, bd)
        act(T.ad[:, :, 0:64], T.p1[:, 0:64 * NS], F.Abs, "pd1", "ad0", "1")
        xk = "xg0a xg0b xg1a xg1b"
        pieces = ((0, NB), (NB, NB + ND), (NB + ND, NS))
        for h in range(2):
            c, hk = 64 * h, "xg%da xg%db x0%d" % (h, h, h)
            if h:
                for j in range(NB, NS):
                    tt(T.dd[:, j - NB, :], T.xg[:, 1024 + 2 * j + 2:2048:16], x0[1][0], A.subtract, hk, "dd%d" % j, x0[1][1])
                act(T.ad[:, 0:NB, 64:128], T.p6[:, 0:64 * NB], F.Abs, "pd6", "ae0", "6")
                for n in (1, 2):
                    a, b = pieces[n]
                    act(T.ad[:, a:b, 64:128], T.dd[:, a - NB:b - NB, :], F.Abs, " ".join("dd%d" % j for j in range(a, b)),
                        "ae%d" % n)
            for k in range(1, NV + 1):
                tt(T.mn[:, k - 1, c:c + 64], T.xg[:, 16 * c + 2 * k - 1:16 * c + 1024:16], x0[h][0], A.min,
                   hk, "mn%d%d" % (h, k), x0[h][1])
            if h == 0:
                cp(PP, T.Pu[:], "Pa Pb", Pk)
                send("P", t, PP, T.lP[:, t, :], Pk)
        for s in range(1, 4):
            mm(PK[:, s, 1:128:2], T.xg[:, 0:2048:16], T.RB[:, 0:128:2], False, False, xk, "K", "3")
        for k in range(1, NV + 1):
            mm(PK[:, 1:4, 2 * k - 1:128:16], T.xg[:, 2 * k - 1:2048:16], T.R16[:], False, False, "R16", "K", "3")
        mm(Hr, T.I[:], PP, False, True, Pk, "Hr", "2")
        todo = []
        for k in range(NV + 1):
            if k:
                todo.append((2 * k - 1, T.mn[:, k - 1, :], T.R32, "mn0%d mn1%d R32" % (k, k)))
            for n in range(3):
                if KA[n] == k:
                    todo += [(2 * j + 2, T.ad[:, j, :], T.R16, "ad0 ae%d" % n) for j in range(*pieces[n])]
        for i, (k, l, rh, rk) in enumerate(todo):
            mm(PK[:, 1:4, k:128:16], l, rh[:], False, i == len(todo) - 1, rk, "K", "3")
        ts(T.h2[:, 0:8], T.v2[:], 1023, None, A.bitwise_and, r="v2", w="h20")
        tt(T.xs[:], T.X[:].indirect(xu), z, A.add, "X %s %s" % (xuk, zk), "xs")
        tt(T.hM[:], T.h2[:, 0:8].indirect(T.oc[:]), T.Dg[:], A.mult, "h20 oc Dg", "hM")

        act(T.hy[:], Hr, F.Identity, "Hr", "hy", "2", bias=8388607.5, scale=1.0 / 2048)
        if not t:
            late_constants()
        act(T.nn[:], T.hy[:], F.Identity, "hy", "nn", bias=-8390656.0)
        mm(dq, T.nI[:], T.xg[:, 0:2048:16], False, False, xk, "al", "7")
        mm(zs, T.I[:], T.lZ[:, t, :], False, True, "lZ%d" % t, "al", "7")
        act(T.aq[:], dq, F.Abs, "al", "aq", "7")
        act(T.av1[:], zs, F.Identity, "al", "av1", "7", bias=1279.75, scale=0.5)
        mm(E1, T.W2[:], z, True, False, "", "Hr E1", "2")
        mm(E2, T.W2[:], z, False, False, "", "E2", "2")
        mm(E2, T.I[:], PP, False, False, "", "E2", "2")
        for s in range(4, 8):
            mm(blk(s, s + 1), T.aq[:], T.RB[:, 0:128], False, s == 7, "aq", "KQ", "4")

        def back(x, c):
            return x[:, c + 63:c - 1:-1] if c else x[:, 63::-1]

        for j in range(3):
            for h in range(2):
                c = 160 * j + 80 * h + 16
                scan(T.SB[:, c:c + 64], PK[:, 1, 64 * h:64 * h + 64], T.SB[:, c - 161:c - 97] if j else T.top[:], 0.0,
                     A.max, A.min, "K " + ("s%d%d" % (j - 1, h) if j else "top"), "s%d%d" % (j, h), "3")
                scan(back(T.SB, c + 480) if j < 2 else back(T.p6, 64 * h), back(PK[:, 1, :], 64 * h),
                     back(T.SB, c + 321) if j else back(T.top, 0), 0.0, A.max, A.min,
                     "K " + ("s%d%d" % (j + 2, h) if j else "top"), "s%d%d" % (j + 3, h), "3" if j < 2 else "36")
        ts(T.h2[:, 8:16], T.v2[:], 1023, None, A.bitwise_and, r="v2", w="h21")
        for h in range(2):
            c = 336 + 80 * h
            tt(T.cut[:, h, :], T.SB[:, c - 1:c + 63], T.p6[:, 64 * h:64 * h + 64], A.min, "s2%d s5%d" % (h, h), "cut%d" % h, "6")
            if h == 0:
                ts(T.h2[:, 16:24], T.v2[:], 1023, None, A.bitwise_and, r="v2", w="h22")
        ts(T.xn[:, 0:64], T.xs[:, 0:64], 255, None, A.bitwise_and, r="xs", w="xn0")
        for h in range(2):
            c = 816 + 80 * h
            scan(T.SB[:, c:c + 64], T.cut[:, h, :], T.to3[:], 0.0, A.max, A.min, "cut%d to3" % h, "m%d" % h)
            if h == 0:
                ts(T.xn[:, 64:128], T.xs[:, 64:128], 255, None, A.bitwise_and, r="xs", w="xn1")

        def before_e(gs):
            for gi in gs:
                c = 16 + 16 * gi + 16 * (gi // 4)
                act(T.nc[:, 16 + 16 * gi:32 + 16 * gi], T.SB[:, c:c + 16], F.Sign, "s0%d nc" % (gi // 4), "nc%d" % gi,
                    scale=-1.0, bias=T.SB[:, c + 15:c + 16])

        nk = " ".join("nc%d" % gi for gi in range(8))
        mid = ((T.p6[:, 256:320], "6"), (PK[:, 1, 0:64], "3"))
        amb, Xs, sT, Kb = T.p6[:, 0:160], T.p5[:, 128:256], T.p1[:, 384:512], T.p0[:, 128:256]
        before_e(range(4))
        act(T.av[:], T.av1[:], F.Identity, "av1", "av", bias=-1280.0)
        before_e(range(4, 8))
        mm(E1, T.IQ[:], T.nn[:], False, False, "IQ nn", "E1", "2")
        mm(E2, T.IQ[:], T.nn[:], False, False, "", "E2", "2")
        mm(Kb, T.I[:], T.jb[:], True, False, "jb", "Kb", "0")
        mm(Kb, T.BoK[:], T.hM[:], False, False, "BoK hM", "Kb", "0")
        mm(ub, T.I[:], T.M2[:], True, False, "M2", "al ub", "7")
        mm(ub, T.av[:], T.Wu[:], False, True, "av", "ub", "7")
        mm(sT, T.nc[:, 16:144], T.I[:], True, False, nk, "sT", "1")
        mm(sT, T.nc[:, 15:143], T.nI[:], False, True, "", "sT", "1")
        for gi in range(8):
            c = 816 + 16 * gi + 16 * (gi // 4) + 13
            ts(T.FL[:, :, 16 * gi:16 * gi + 16], PK[:, 2:4, 16 * gi:16 * gi + 16], 8.0, T.SB[:, c:c + 1], A.add, A.is_le,
               "K m%d" % (gi // 4), "F%d" % gi, "3")
            act(T.FQ[:, :, 16 * gi:16 * gi + 16], PK[:, 4:8, 16 * gi:16 * gi + 16], F.Sign, "KQ m%d" % (gi // 4), "G%d" % gi, "4",
                scale=-1.0, bias=T.SB[:, c:c + 1])
        fl = " ".join("F%d" % gi for gi in range(8))
        fq = " ".join("G%d" % gi for gi in range(8))
        cp(T.X[:].indirect(xu), T.xn[:], xuk + " xn0 xn1", "X")
        act(T.sg[:], sT, F.Copy, "sT", "sg", "1")
        act(T.uM[:], ub, F.Relu, "ub", "uM", "7")
        for h, (o, b) in enumerate(mid):
            mm(o, T.FL[:, 1, :], T.I[:, 64 * h:64 * h + 64], True, False, fl, "mid%d" % h, b)
            mm(o, T.FL[:, 0, :], T.nI[:, 64 * h:64 * h + 64], False, True, "", "mid%d" % h, b)
            cp(T.sM[:, t, 64 * h:64 * h + 64], o, "mid%d" % h, "sM%d" % h, b)
        send("M", t, T.sM[:, t, :], T.lM[:, t, :], "sM0 sM1")
        mm(Xs, T.FL[:, 0, :], T.I[:], True, False, "", "Xs", "5")
        mm(Xs, T.FL[:, 1, :], T.I[:], False, False, "", "Xs", "5")
        mm(Xs, T.FQ[:, 3, :], T.I[:], False, True, fq, "Xs", "5")
        mm(nL, T.I[:], T.cl[:, int(last), :], True, False, "cl0 cl1 cl2 cm0 cm1", "nL", "1")
        mm(nL, T.FQ[:, 2, :], T.Rh[:], False, True, "Rh", "nL", "1")
        mm(Kb, T.FQ[:, 3, :], T.IX[:], False, True, "IX", "Kb", "0")
        mm(amb, T.FQ[:, 1, :], T.R1[:], True, False, "R1a R1b", "amb", "6")
        mm(amb, T.FQ[:, 0, :], T.nR1[:], False, True, "nR1a nR1b", "amb", "6")
        mm(E2, T.nI[:], T.lP[:, t, :], False, True, "lP%d" % t, "E1 E2", "2")
        if not last:
            mm(uL, T.I[:], T.cu[:], True, False, "cu0 cu1", "uL", "7")
        mm(uL, T.uM[:], T.sel32[:], last, True, "uM", "uL", "7")
        if not t:
            bag_copy(0)
        act(T.xa[:], Xs, F.Abs, "Xs", "xa", "5", bias=-1.0)
        tt(O[:, 17:64:2], T.h2[:], nL, A.subtract, "h20 h21 h22 nL", ck + " bc", "1")
        if not t:
            bag_copy(1)
        ts(T.ns[:], T.xa[:], 1.5, None, A.is_le, r="xa", w="ns")
        cp(T.sA[:, t, :], amb, "amb", "sA%d" % t, "6")
        send("A", t, T.sA[:, t, :], T.lA[:, t, :], "sA%d" % t)

        for c in range(8):
            act(T.kd[:, KD[c]:KD[c + 1]], Kb[:, 16 * c:128], F.Abs, "Kb bc", "kd%d" % c, "0",
                scale=-1.0 / 256, bias=O[:, 33 + 2 * c:34 + 2 * c])
        if last:
            ts(T.wl[:], O[:, 17:32:2], 1023.5, None, A.is_lt, r=ck, w="wl")
        else:
            act(T.sB[:], amb[:, 0:128], F.Identity, "amb", "sB", "6", bias=T.bth[:, t + 1:t + 2])
            thresholds()

        def least(a, b):
            scan(T.km[:, KD[a]:KD[b]], T.rs[:, KD[a]:KD[b]], T.kd[:, KD[a]:KD[b]], 0.0, A.max, A.min,
                 rsk + " " + " ".join("kd%d" % c for c in range(a, b)), "km%d" % a)

        S, sd = ((T.p5[:, 0:64], "5"), (T.p0[:, 0:64], "0")), T.p1[:, 128:256]
        tt(E1, E1, T.ns[:], A.mult, "ns", "E1", "2")
        tt(E2, E2, T.ns[:], A.mult, "ns", "E2", "2")
        cp(T.ui[:], uL, "uL", "ui", "7")
        mm(T.p7[:, 256:384], T.I[:], z, True, False, zk, "zq", "7")
        mm(T.p7[:, 384:512], T.I[:], T.av[:], False, False, "av", "zq", "7")
        tt(E1, E1, PP, A.add, Pk, "E1", "2")
        tt(sd, E2, T.sg[:], A.mult, "E2 sg", "sd", "21")
        least(0, 4)
        tt(T.sbf[:], E1, T.sg[:], A.mult, "E1 sg", "sbf", "2")
        least(4, 8)
        ts(T.u15[:], T.ui[:, 0:8], 15, None, A.bitwise_and, r="ui", w="u15")
        ts(T.un[:, 8:16], T.ui[:, 8:16], 1023, None, A.bitwise_and, r="ui", w="un0")
        if last:
            tt(O[:, 17:32:2], O[:, 17:32:2], T.wl[:], A.mult, "wl", ck)
        for h, (o, b) in enumerate(S):
            mm(o, T.nBo[:], T.sbf[:, 64 * h:64 * h + 64], True, False, "nBo sbf", "S%d" % h, b)
        if last:
            lands("allsent", "sent", sent[0])
            dma("Y", T.yx[:], T.X[:], "X allsent", "", "o1")
        if not t:
            bag_copy(2)
        ts(O[:, 48:80:2], T.km[:].indirect(T.ke[:, 0:1]), -1048576.0, 260096.0, A.mult, A.add, "km0 km4 ke", "lose")
        tt(T.un[:, 0:8], T.u15[:], T.l16[:], A.add, "u15 l16", "un1")

        lm, la = "lM%d" % t, "lA%d" % t
        for h, (o, b) in enumerate(S):
            c = 64 * h
            tt(T.tp[:, c:c + 64], T.lM[:, t, c:c + 64], sd[:, c:c + 64], A.mult, lm + " sd", "tp%d" % h, "1")
            mm(o, T.Bo[:], T.tp[:, c:c + 64], False, True, "tp%d" % h, "S%d" % h, b)
        tt(T.y1[:], T.lM[:, t, :], E2, A.mult, lm + " E2", "y1", "2")
        scan(T.ds[:], T.cap[:], O[:, 48:64], 0.0, A.min, A.max, "cap lose bc", "ds")
        tt(O[:, 0:32:2], T.un[:], O[:, 1:32:2], A.subtract, "un0 un1 %s %s" % (xik, ck), "diff")

        def pick():
            scan(T.O[:, t + 1, 0:32], T.lA[:, t, 128:160], O[:, 0:32], 0.0, A.mult, A.add,
                 "%s diff %s %s" % (la, xik, ck), "xi%d c%d" % (t + 1, t + 1))

        tt(T.y2[:], E1, T.y1[:], A.subtract, "y1 E1", "y2", "2")
        cp(T.wu[:], T.ds[:, 1:16:2], "ds", "wu")
        for h, (o, b) in enumerate(S):
            tt(T.rr[:, 64 * h:64 * h + 64], o, T.sg[:, 64 * h:64 * h + 64], A.mult, "S%d sg" % h, "rr%d" % h, b)
        if not last:
            pick()
        mm(T.p7[:, 256:384], T.nBo8[:], T.lA[:, t, 0:128], False, False, "nBo8 " + la, "zq", "7")
        mm(T.p7[:, 384:512], T.Bo8[:], T.lA[:, t, 0:128], False, True, "Bo8", "zq", "7")
        if not last:
            bands()
        act(T.zr[:, 0:128], T.p7[:, 256:384], F.Relu, "zq", "zr0", "7")
        act(T.zr[:, 128:256], T.p7[:, 384:512], F.Relu, "zq", "zr1", "7", bias=-256.0)
        mm(T.p6[:, 0:128], T.I[:], T.zr[:, 0:128], True, False, "zr0", "amb zn", "6")
        mm(T.p6[:, 0:128], T.I[:], T.zr[:, 128:256], False, True, "zr1", "zn", "6")
        if not last:
            act(T.zb[:, t + 1, :], T.p6[:, 0:128], F.Copy, "zn", "z%d" % (t + 1), "6")
        tt(W.indirect(T.wu[:]), T.y2[:], T.rr[:], A.add, "wu y2 rr0 rr1", "B Bz B0 B1 B2 B3")
        if not last:
            send("Z", t + 1, T.zb[:, t + 1, :], T.lZ[:, t + 1, :], "z%d" % (t + 1))
            query_sums(t + 1)
            cp(T.VX[:, t + 1, :], T.O[:, t + 1, 1:32:2], "c%d" % (t + 1), "vu%d xu%d" % (t + 1, t + 1))
            ts(T.v2[:], T.O[:, t + 1, 17:32:2], 2.0, 2.0, A.mult, A.add, "c%d" % (t + 1), "v2")
            for h in range(2):
                cp(T.Pu[:, 64 * h:64 * h + 64], W[:, 0:1024].indirect(T.VX[:, t + 1, 8 + 4 * h:12 + 4 * h]),
                   "B vu%d" % (t + 1), "P" + "ab"[h])
    pick()
    cp(T.B[:, B0:B0 + 1], T.B[:, B0 + 1024:B0 + 1025], "B", "Bz")
    cp(T.vf[:], T.O[:, RO, 17:32:2], "c%d" % RO, "vf")
    cp(T.zb[:, RO, :], T.p6[:, 0:128], "zn", "z%d" % RO, "6")
    dma("Y", T.yv[:], T.vf[:], "vf", "", "o5")
    dma("Y", T.yz[:], T.zb[:, RO, :], "z%d" % RO, "", "o2")
    for h, (pb, bk) in enumerate(((T.p1, "1"), (T.p2, "2"), (T.p5, "5"), (T.p0, "0"), (T.p7, "7"))):
        a, b = YP[h + 1], YP[h]
        act(pb[:, 0:b - a], T.B[:, B0 + 512 + a:B0 + 512 + b], F.Identity, "B", "hi%d" % h, bk, scale=2048.0)
        tt(T.yo[:, a:b], T.B[:, B0 + a:B0 + b], pb[:, 0:b - a], A.add, "B hi%d" % h + ("" if a else " Bz"), "yo%d" % h, bk)
    dma("Y", T.yb[:, 256:512], T.yo[:, 256:512], "yo0 yo1 yo2", "", "o4")
    dma("S", T.yb[:, 0:256], T.yo[:, 0:256], "yo3 yo4", "", "o3")
    for s, v in count.items():
        wait("G", (s, v))
